import numpy as np
import ml_dtypes


def mxq(x, axis, fmt="e4m3"):
    dtype, down = {"e4m3": (ml_dtypes.float8_e4m3fn, 7), "e5m2": (ml_dtypes.float8_e5m2, 14)}[fmt]
    v = np.moveaxis(np.asarray(x, np.float32).astype(ml_dtypes.bfloat16).astype(np.float64), axis, -1)
    blocks = v.reshape(v.shape[:-1] + (-1, 32))
    amax = np.abs(blocks).max(-1, keepdims=True)
    byte = np.maximum(np.where(amax > 0, np.frexp(amax)[1] - 1 + 127, 0) - down, 1)
    scale = np.exp2(byte - 127.0)
    codes = (blocks / scale).astype(np.float32).astype(dtype).astype(np.float64)
    return np.moveaxis((codes * scale).reshape(v.shape), -1, axis)


WIDE = False


def mx_kscale(k):
    if not WIDE:
        return np.ones(k)
    levels = np.array([10, -10, 5, -5, 0])
    if k % 512:
        return np.exp2(np.random.permutation(np.resize(levels, k // 32))).repeat(32)
    a = np.empty((k // 512, 16))
    for p in range(k // 512):
        a[p, :8] = np.random.permutation(np.resize(levels, 8))
        for g in range(8):
            far = levels[np.abs(levels - a[p, g]) >= 10]
            a[p, g + 8] = far[np.random.randint(len(far))]
    return np.exp2(a.ravel()).repeat(32)


def f64(x):
    return np.asarray(x).astype(np.float64)


def striped(idx):
    return np.tile(idx.reshape(-1, 16).T, (8, 1)).astype(np.uint16)


def unstriped(offs):
    return offs[:16].T.reshape(-1).astype(np.int64)


E2M1 = np.array([0.0, 0.5, 1.0, 1.5, 2.0, 3.0, 4.0, 6.0, -0.0, -0.5, -1.0, -1.5, -2.0, -3.0, -4.0, -6.0])


def pack_weight(w, fmt):
    k, n = w.shape
    w = f64(np.asarray(w, np.float32).astype(ml_dtypes.bfloat16)).reshape(k // 32, 32, n)
    amax = np.abs(w).max(1)
    if fmt == "e4m3":
        byte = np.frexp(amax)[1] - 1 + 127 - 7
    else:
        mant, ex = np.frexp(amax / 6.0)
        byte = np.where(mant > 0.5, ex, ex - 1) + 127
    byte = np.clip(np.where(amax > 0, byte, 1), 1, 254)
    scaled = (w * np.exp2(127.0 - byte)[:, None, :]).reshape(k, n).astype(np.float32)
    by_word = np.ascontiguousarray(scaled.reshape(k // 512, 128, 4, n).transpose(0, 1, 3, 2))
    if fmt == "e4m3":
        words = by_word.astype(ml_dtypes.float8_e4m3fn).view(np.uint8)
    else:
        c = by_word.astype(ml_dtypes.float4_e2m1fn).view(np.uint8) & 0xF
        words = (c[..., 0::2] | (c[..., 1::2] << 4)).reshape(k // 512, 128, 2 * n)
    return np.ascontiguousarray(words), np.ascontiguousarray(byte.astype(np.uint8).reshape(k // 512, 16, n))


def unpack_weight(words, scales, fmt):
    g, _, n = scales.shape
    words = np.ascontiguousarray(words).reshape(g, 128, n, -1)
    if fmt == "e4m3":
        vals = words.view(ml_dtypes.float8_e4m3fn).astype(np.float64)
    else:
        nib = np.empty((g, 128, n, 4), np.uint8)
        nib[..., 0::2] = words & 0xF
        nib[..., 1::2] = words >> 4
        vals = E2M1[nib]
    vals = vals * np.repeat(np.exp2(scales.astype(np.float64) - 127.0), 8, axis=1)[..., None]
    return vals.transpose(0, 1, 3, 2).reshape(g * 512, n)


def gelu(v):
    return 0.5 * v * (1.0 + np.tanh(np.sqrt(2.0 / np.pi) * (v + 0.044715 * v**3)))


def bf(x):
    return np.asarray(x, np.float32).astype(ml_dtypes.bfloat16)

def planes(Y):
    n, m = Y.shape
    b = f64(bf(Y)).reshape(n // 32, 32, m)
    amax = np.abs(b).max(1)
    byte = np.clip(np.where(amax > 0, np.frexp(amax)[1] - 1 + 127 - 7, 1), 1, 254)
    codes = (b * np.exp2(127.0 - byte)[:, None, :]).reshape(n, m).astype(np.float32).astype(ml_dtypes.float8_e4m3fn).view(np.uint8)
    words = codes.reshape(n // 512, 128, 4, m).transpose(0, 1, 3, 2)
    return np.ascontiguousarray(words), np.ascontiguousarray(byte.astype(np.uint8).reshape(n // 512, 16, m))


K, T, S, H, T2, S2 = 1024, 4096, 1024, 512, 2048, 1024

def setup_inputs():
    n = np.random.standard_normal
    s = mx_kscale(K)[:, None]
    u = mx_kscale(H)[:, None]
    offs = striped(np.random.permutation(T)[:S])
    idx2 = np.random.permutation(T2)[:S2]
    offs2 = striped(idx2)
    amp = np.exp(0.8 * n(T2))
    tab_words, tab_scales = pack_weight(n((K, T)) * s, "e4m3")
    tab2_words, tab2_scales = pack_weight((n((H, T2)) + 0.125) * amp[None, :] / np.sqrt(H) / u, "e4m3")
    w4_words, w4_scales = pack_weight(0.85 * n((K, H)) / np.sqrt(K) / s, "e2m1")
    w1 = 0.55 * n((K, H)) / np.sqrt(K) / s
    g = np.exp(0.3 * n(H)) * u[:, 0]
    base = 0.8 * np.exp(0.2 * n(S2)) * amp[idx2]
    return {"tab_words": tab_words, "tab_scales": tab_scales, "offs": offs,
            "tab2_words": tab2_words, "tab2_scales": tab2_scales, "offs2": offs2,
            "w4_words": w4_words, "w4_scales": w4_scales,
            "w1": w1.astype(np.float32), "g": g.astype(np.float32), "base": base.astype(np.float32)}

def reference(tab_words, tab_scales, offs, tab2_words, tab2_scales, offs2, w4_words, w4_scales, w1, g, base):
    v = unpack_weight(tab_words, tab_scales, "e4m3")[:, unstriped(offs)]
    v2 = unpack_weight(tab2_words, tab2_scales, "e4m3")[:, unstriped(offs2)]
    w4 = unpack_weight(w4_words, w4_scales, "e2m1")
    w1q = mxq(f64(w1), 0, "e4m3")
    p = w4.T @ v + w1q.T @ v
    q = p * p
    h = f64(g)[:, None] * (q / (1.0 + q))
    hq = mxq(h, 0, "e4m3")
    y = np.maximum(v2.T @ hq, f64(base)[:, None])
    words, scales = planes(y)
    return y, words, scales

@@ -1,0 +1,218 @@
+import math
+from contextlib import ExitStack
+
+import concourse.mybir as mybir
+
+F32 = mybir.dt.float32
+BF16 = mybir.dt.bfloat16
+I32 = mybir.dt.int32
+U32 = mybir.dt.uint32
+U16 = mybir.dt.uint16
+U8 = mybir.dt.uint8
+FP8X4 = mybir.dt.float8_e4m3fn_x4
+FP4X4 = mybir.dt.float4_e2m1fn_x4
+ACT = mybir.ActivationFunctionType
+ALU = mybir.AluOpType
+
+K, T, S, H, T2, S2 = 1024, 4096, 1024, 512, 2048, 1024
+P = 128
+CH = 256
+NCH = S // CH
+SHIFT = 1.375
+FLOPS = 2 * (2 * K * H * S + H * S * S2)
+
+
+def tile_list_cortex_rates_kernel(tc, tab_words, tab_scales, offs, tab2_words, tab2_scales, offs2,
+                                           w4_words, w4_scales, w1, g, base, out_0, out_1, out_2):
+    nc = tc.nc
+    with ExitStack() as ctx:
+        keep = ctx.enter_context(tc.tile_pool(name="keep", bufs=1))
+        work = ctx.enter_context(tc.tile_pool(name="work", bufs=2))
+        psum = ctx.enter_context(tc.psum_pool(name="psum", bufs=8))
+
+        def held(shape, dtype, name):
+            return keep.tile(shape, dtype, name=name, align_bytes=64)
+
+        idx = keep.tile([P, S // 16], U16, name="idx")
+        idx2 = keep.tile([P, S2 // 16], U16, name="idx2")
+        vsc_win = held([P, T], U8, "vsc_win")
+        w4sc_raw = held([P, H], U8, "w4sc_raw")
+        v2sc_win = held([P, T2], U8, "v2sc_win")
+        v2sc = held([P, S2], U8, "v2sc")
+        planes = held([P, 2, S + H], U8, "planes")
+        w4_raw = held([P, 2, 2 * H], U8, "w4_raw")
+        v_win = [held([P, T], I32, "v_win%d" % a) for a in range(2)]
+        v2_win = held([P, T2], I32, "v2_win")
+        w1_raw0 = held([P, 4, H], F32, "w1_raw0")
+        w1_raw1 = [held([P, 4, H // 2], F32, "w1_raw1_%d" % u) for u in range(2)]
+        g_sb = held([P, 4], F32, "g_sb")
+        base_sb = held([P, 2, 4], F32, "base_sb")
+        warm = held([P, 2], F32, "warm")
+
+        nc.vector.memset(warm[:, 0:1], 1.0)
+        for lo, hi in ((32, 64), (64, 128)):
+            nc.vector.memset(vsc_win[lo:hi, :].bitcast(I32), 0)
+        for lo, hi in ((32, 64), (64, 128)):
+            nc.vector.memset(w4sc_raw[lo:hi, :].bitcast(I32), 0)
+        nc.gpsimd.memset(v2sc_win[:].bitcast(I32), 0)
+        nc.gpsimd.memset(planes[:].rearrange("p a c -> p (a c)").bitcast(I32), 0)
+        nc.gpsimd.memset(v2sc[:].bitcast(I32), 0)
+        nc.scalar.activation(warm[:, 1:2], warm[:, 0:1], ACT.Abs_reciprocal_sqrt)
+
+        nc.sync.dma_start(idx[:], offs)
+        nc.sync.dma_start(vsc_win[0:32, :].bitcast(I32), tab_scales.rearrange("a q c -> q a c").bitcast(I32))
+        nc.sync.dma_start(w4sc_raw[0:32, :].bitcast(I32), w4_scales.rearrange("a q c -> q a c").bitcast(I32))
+        nc.sync.dma_start(w4_raw[:].bitcast(I32), w4_words.rearrange("a p c -> p a c").bitcast(I32))
+        nc.sync.dma_start(v_win[0][:], tab_words[0].rearrange("p t i -> p (t i)").bitcast(I32))
+        nc.sync.dma_start(idx2[:], offs2)
+        nc.sync.dma_start(v2sc_win[0:16, :].bitcast(I32), tab2_scales[0].bitcast(I32))
+        nc.sync.dma_start(g_sb[:], g.rearrange("(p t) -> p t", t=4))
+        nc.sync.dma_start(base_sb[:], base.rearrange("(g p t) -> p g t", g=2, t=4))
+        nc.sync.dma_start(w1_raw0[:], w1[0:512, :].rearrange("(p j) c -> p j c", j=4))
+        nc.sync.dma_start(v_win[1][:], tab_words[1].rearrange("p t i -> p (t i)").bitcast(I32))
+        for u in range(2):
+            nc.sync.dma_start(w1_raw1[u][:],
+                              w1[512:1024, u * 256:(u + 1) * 256].rearrange("(p j) c -> p j c", j=4))
+        nc.sync.dma_start(v2_win[:], tab2_words[0].rearrange("p t i -> p (t i)").bitcast(I32))
+
+        vsc_g = held([P, S], U8, "vsc_g")
+        stage = held([P, S + H], U8, "stage")
+        nc.vector.tensor_copy(vsc_g[:], vsc_win[:].indirect(idx[:]))
+        nc.vector.tensor_copy(stage[:, S:S + H].rearrange("p (t m) -> p m t", t=4),
+                              w4sc_raw[:].rearrange("p (m t) -> p m t", t=4))
+        nc.vector.tensor_copy(stage[:, 0:S].bitcast(I32), vsc_g[:].bitcast(I32))
+        for q4 in range(4):
+            nc.scalar.dma_start(planes[32 * q4:32 * q4 + 4, :, :].bitcast(I32),
+                                stage[8 * q4:8 * q4 + 8, :].bitcast(I32))
+        w4p = held([P, 2, 2 * H], U8, "w4p")
+        nc.vector.tensor_copy(w4p[:].bitcast(U16).rearrange("p a (t m) -> p a m t", t=4),
+                              w4_raw[:].bitcast(U16).rearrange("p a (m t) -> p a m t", t=4))
+
+        vg = [held([P, S], U32, "vg%d" % a) for a in range(2)]
+        nc.vector.tensor_copy(vg[0][:], v_win[0][:].bitcast(U32).indirect(idx[:]))
+
+        w1b = [held([P, 4 * H], BF16, "w1b%d" % a) for a in range(2)]
+        w1c = [held([P, H], U32, "w1c%d" % a) for a in range(2)]
+        w1s = [held([P, H], U8, "w1s%d" % a) for a in range(2)]
+
+        def dealt(a):
+            return w1b[a][:].rearrange("p (t m j) -> p m j t", t=4, j=4)
+
+        nc.scalar.activation(dealt(0), w1_raw0[:].rearrange("p j (m t) -> p m j t", t=4), ACT.Copy)
+        nc.vector.quantize_mx(out=w1c[0][:].bitcast(FP8X4), scales=w1s[0][:], in_=w1b[0][:])
+
+        v2sc_g = held([P, S2], U8, "v2sc_g")
+        v2sc_p = held([P, S2], U8, "v2sc_p")
+        nc.vector.tensor_copy(v2sc_g[:], v2sc_win[:].indirect(idx2[:]))
+        nc.vector.tensor_copy(v2sc_p[:].rearrange("p (g t m) -> p g m t", g=2, t=4),
+                              v2sc_g[:].rearrange("p (g m t) -> p g m t", g=2, t=4))
+        for q4 in range(4):
+            nc.sync.dma_start(v2sc[32 * q4:32 * q4 + 4, :].bitcast(I32), v2sc_p[4 * q4:4 * q4 + 4, :].bitcast(I32))
+
+        banks = [[psum.tile([P, 2, CH], F32, name="bank", tag="bank") for b in range(2)] for c in range(NCH)]
+
+        def stage_one(a, c, b, start, stop):
+            for tt in range(2):
+                t = 2 * b + tt
+                for n0 in range(0, CH, 128):
+                    cols = slice(c * CH + n0, c * CH + n0 + 128)
+                    nc.tensor.matmul_mx(out=banks[c][b][:, tt, n0:n0 + 128],
+                                        lhsT=w4p[:, a, 256 * t:256 * (t + 1)].bitcast(FP4X4),
+                                        lhsT_scale=planes[:, a, S + 128 * t:S + 128 * (t + 1)],
+                                        rhs=vg[a][:, cols].bitcast(FP8X4), rhs_scale=planes[:, a, cols],
+                                        start=(start and tt == 0 and n0 == 0), stop=False)
+            for tt in range(2):
+                t = 2 * b + tt
+                cols = slice(c * CH, (c + 1) * CH)
+                nc.tensor.matmul_mx(out=banks[c][b][:, tt, :],
+                                    lhsT=w1c[a][:, 128 * t:128 * (t + 1)].bitcast(FP8X4),
+                                    lhsT_scale=w1s[a][:, 128 * t:128 * (t + 1)],
+                                    rhs=vg[a][:, cols].bitcast(FP8X4), rhs_scale=planes[:, a, cols],
+                                    start=False, stop=(stop and tt == 1))
+
+        for c in range(NCH):
+            for b in range(2):
+                stage_one(0, c, b, True, False)
+
+        for u in range(2):
+            nc.vector.tensor_copy(vg[1][:, 512 * u:512 * (u + 1)],
+                                  v_win[1][:].bitcast(U32).indirect(idx[:, 32 * u:32 * (u + 1)]))
+        nc.scalar.activation(dealt(1)[:, 0:64], w1_raw1[0][:].rearrange("p j (m t) -> p m j t", t=4), ACT.Copy)
+        nc.scalar.activation(dealt(1)[:, 64:128], w1_raw1[1][:].rearrange("p j (m t) -> p m j t", t=4), ACT.Copy)
+        for b in range(2):
+            nc.vector.quantize_mx(out=w1c[1][:, 256 * b:256 * (b + 1)].bitcast(FP8X4),
+                                  scales=w1s[1][:, 256 * b:256 * (b + 1)],
+                                  in_=w1b[1][:, 1024 * b:1024 * (b + 1)])
+        for c in range(NCH):
+            for b in range(2):
+                stage_one(1, c, b, False, True)
+
+        v2g = held([P, S2], U32, "v2g")
+        v2p = held([P, S2], I32, "v2p")
+        for gi in range(2):
+            half = slice(512 * gi, 512 * (gi + 1))
+            nc.vector.tensor_copy(v2g[:, half], v2_win[:].bitcast(U32).indirect(idx2[:, 32 * gi:32 * (gi + 1)]))
+            nc.vector.tensor_copy(v2p[:, half].rearrange("p (t m) -> p m t", t=4),
+                                  v2g[:, half].bitcast(I32).rearrange("p (m t) -> p m t", t=4))
+
+        ysc = held([P, S], U8, "ysc")
+        hq = {}
+
+        def respond(c):
+            q = [work.tile([P, 2, CH], F32, name="q%d" % b) for b in range(2)]
+            s = [work.tile([P, 2, CH], F32, name="s%d" % b) for b in range(2)]
+            r = [work.tile([P, 2, CH], F32, name="r%d" % b) for b in range(2)]
+            hb = work.tile([P, 4, CH], BF16, name="hb")
+            hi = work.tile([P, 4 * CH], BF16, name="hi", align_bytes=64)
+            hc = work.tile([P, CH], U32, name="hc", align_bytes=64)
+            hs = work.tile([P, CH], U8, name="hs", align_bytes=64)
+            for b in range(2):
+                nc.scalar.activation(q[b][:], banks[c][b][:], ACT.Square)
+            for b in range(2):
+                nc.scalar.activation(s[b][:], q[b][:], ACT.Abs_reciprocal_sqrt, bias=SHIFT, scale=SHIFT)
+            for b in range(2):
+                nc.scalar.activation(r[b][:], s[b][:], ACT.Square, scale=math.sqrt(SHIFT))
+            for t in range(4):
+                nc.vector.scalar_tensor_tensor(hb[:, t, :], q[t // 2][:, t % 2, :], g_sb[:, t:t + 1],
+                                               r[t // 2][:, t % 2, :], ALU.mult, ALU.mult)
+            nc.vector.tensor_copy(hi[:].rearrange("p (c i t) -> p c t i", i=4, t=4),
+                                  hb[:].rearrange("p t (c i) -> p c t i", i=4))
+            nc.vector.quantize_mx(out=hc[:].bitcast(FP8X4), scales=hs[:], in_=hi[:])
+            hq[c] = (hc, hs)
+
+        def fire(c):
+            hc, hs = hq[c]
+            cols = slice(c * CH, (c + 1) * CH)
+            for gi in range(2):
+                y = work.tile([P, 4, CH], F32, name="y", bufs=4)
+                yb = work.tile([P, 4 * CH], BF16, name="yb", bufs=3, align_bytes=64)
+                yc = work.tile([P, CH], U32, name="yc", bufs=4, align_bytes=64)
+                for b in range(2):
+                    drive = psum.tile([P, 2, CH], F32, name="bank", tag="bank")
+                    for tt in range(2):
+                        m0 = 512 * gi + 128 * (2 * b + tt)
+                        nc.tensor.matmul_mx(out=drive[:, tt, :], lhsT=v2p[:, m0:m0 + 128].bitcast(FP8X4),
+                                            lhsT_scale=v2sc[:, m0:m0 + 128], rhs=hc[:].bitcast(FP8X4),
+                                            rhs_scale=hs[:], start=True, stop=True)
+                    nc.vector.tensor_tensor(y[:, 2 * b:2 * b + 2, :], drive[:],
+                                            base_sb[:, gi, 2 * b:2 * b + 2].unsqueeze(2).to_broadcast([P, 2, CH]),
+                                            ALU.max)
+                nc.sync.dma_start(out_0[512 * gi:512 * (gi + 1), cols].rearrange("(p t) j -> p t j", t=4), y[:])
+                dst = yb[:].rearrange("p (c i t) -> p c t i", i=4, t=4)
+                src = y[:].rearrange("p t (c i) -> p c t i", i=4)
+                if c == NCH - 1 and gi == 1:
+                    nc.vector.tensor_copy(dst, src)
+                else:
+                    nc.scalar.activation(dst, src, ACT.Copy)
+                nc.vector.quantize_mx(out=yc[:].bitcast(FP8X4), scales=ysc[4 * gi:P, cols], in_=yb[:])
+                nc.sync.dma_start(out_1[gi, :, cols, :].rearrange("p m t -> p (m t)").bitcast(I32),
+                                  yc[:].bitcast(I32))
+
+        respond(0)
+        for c in range(NCH):
+            if c + 1 < NCH:
+                respond(c + 1)
+            fire(c)
+        for q4 in range(4):
+            eng = nc.sync if q4 % 2 == 0 else nc.scalar
+            eng.dma_start(out_2[:, 4 * q4:4 * q4 + 4, :].bitcast(I32), ysc[32 * q4:32 * q4 + 8, :].bitcast(I32))

@@ -19,6 +19,7 @@ P = 128
 CH = 256
 NCH = S // CH
 SHIFT = 1.375
+W1_SPLIT = 44
 FLOPS = 2 * (2 * K * H * S + H * S * S2)
 
 
@@ -30,8 +31,8 @@ def tile_list_cortex_rates_kernel(tc, tab_words, tab_scales, offs, tab2_words, t
         work = ctx.enter_context(tc.tile_pool(name="work", bufs=2))
         psum = ctx.enter_context(tc.psum_pool(name="psum", bufs=8))
 
-        def held(shape, dtype, name):
-            return keep.tile(shape, dtype, name=name, align_bytes=64)
+        def held(shape, dtype, name, tag=None):
+            return keep.tile(shape, dtype, name=name, tag=tag or name, align_bytes=64)
 
         idx = keep.tile([P, S // 16], U16, name="idx")
         idx2 = keep.tile([P, S2 // 16], U16, name="idx2")
@@ -43,8 +44,7 @@ def tile_list_cortex_rates_kernel(tc, tab_words, tab_scales, offs, tab2_words, t
         w4_raw = held([P, 2, 2 * H], U8, "w4_raw")
         v_win = [held([P, T], I32, "v_win%d" % a) for a in range(2)]
         v2_win = held([P, T2], I32, "v2_win")
-        w1_raw0 = held([P, 4, H], F32, "w1_raw0")
-        w1_raw1 = [held([P, 4, H // 2], F32, "w1_raw1_%d" % u) for u in range(2)]
+        w1_raw = [held([P, 4, H], F32, "w1_raw%d" % a) for a in range(2)]
         g_sb = held([P, 4], F32, "g_sb")
         base_sb = held([P, 2, 4], F32, "base_sb")
         warm = held([P, 2], F32, "warm")
@@ -68,11 +68,9 @@ def tile_list_cortex_rates_kernel(tc, tab_words, tab_scales, offs, tab2_words, t
         nc.sync.dma_start(v2sc_win[0:16, :].bitcast(I32), tab2_scales[0].bitcast(I32))
         nc.sync.dma_start(g_sb[:], g.rearrange("(p t) -> p t", t=4))
         nc.sync.dma_start(base_sb[:], base.rearrange("(g p t) -> p g t", g=2, t=4))
-        nc.sync.dma_start(w1_raw0[:], w1[0:512, :].rearrange("(p j) c -> p j c", j=4))
+        nc.sync.dma_start(w1_raw[0][:], w1[0:512, :].rearrange("(p j) c -> p j c", j=4))
         nc.sync.dma_start(v_win[1][:], tab_words[1].rearrange("p t i -> p (t i)").bitcast(I32))
-        for u in range(2):
-            nc.sync.dma_start(w1_raw1[u][:],
-                              w1[512:1024, u * 256:(u + 1) * 256].rearrange("(p j) c -> p j c", j=4))
+        nc.sync.dma_start(w1_raw[1][:], w1[512:1024, :].rearrange("(p j) c -> p j c", j=4))
         nc.sync.dma_start(v2_win[:], tab2_words[0].rearrange("p t i -> p (t i)").bitcast(I32))
 
         vsc_g = held([P, S], U8, "vsc_g")
@@ -88,7 +86,7 @@ def tile_list_cortex_rates_kernel(tc, tab_words, tab_scales, offs, tab2_words, t
         nc.vector.tensor_copy(w4p[:].bitcast(U16).rearrange("p a (t m) -> p a m t", t=4),
                               w4_raw[:].bitcast(U16).rearrange("p a (m t) -> p a m t", t=4))
 
-        vg = [held([P, S], U32, "vg%d" % a) for a in range(2)]
+        vg = [held([P, S], U32, "vg0")]
         nc.vector.tensor_copy(vg[0][:], v_win[0][:].bitcast(U32).indirect(idx[:]))
 
         w1b = [held([P, 4 * H], BF16, "w1b%d" % a) for a in range(2)]
@@ -98,56 +96,58 @@ def tile_list_cortex_rates_kernel(tc, tab_words, tab_scales, offs, tab2_words, t
         def dealt(a):
             return w1b[a][:].rearrange("p (t m j) -> p m j t", t=4, j=4)
 
-        nc.scalar.activation(dealt(0), w1_raw0[:].rearrange("p j (m t) -> p m j t", t=4), ACT.Copy)
-        nc.vector.quantize_mx(out=w1c[0][:].bitcast(FP8X4), scales=w1s[0][:], in_=w1b[0][:])
+        def rows(a):
+            return w1_raw[a][:].rearrange("p j (m t) -> p m j t", t=4)
 
+        nc.scalar.activation(dealt(0), rows(0), ACT.Copy)
         v2sc_g = held([P, S2], U8, "v2sc_g")
-        v2sc_p = held([P, S2], U8, "v2sc_p")
         nc.vector.tensor_copy(v2sc_g[:], v2sc_win[:].indirect(idx2[:]))
+        nc.vector.quantize_mx(out=w1c[0][:].bitcast(FP8X4), scales=w1s[0][:], in_=w1b[0][:])
+        v2sc_p = held([P, S2], U8, "v2sc_p", tag="w1_raw0")
         nc.vector.tensor_copy(v2sc_p[:].rearrange("p (g t m) -> p g m t", g=2, t=4),
                               v2sc_g[:].rearrange("p (g m t) -> p g m t", g=2, t=4))
         for q4 in range(4):
             nc.sync.dma_start(v2sc[32 * q4:32 * q4 + 4, :].bitcast(I32), v2sc_p[4 * q4:4 * q4 + 4, :].bitcast(I32))
 
-        banks = [[psum.tile([P, 2, CH], F32, name="bank", tag="bank") for b in range(2)] for c in range(NCH)]
+        banks = [[psum.tile([P, 512], F32, name="bank", tag="bank") for t in range(4)] for u in range(2)]
 
-        def stage_one(a, c, b, start, stop):
-            for tt in range(2):
-                t = 2 * b + tt
-                for n0 in range(0, CH, 128):
-                    cols = slice(c * CH + n0, c * CH + n0 + 128)
-                    nc.tensor.matmul_mx(out=banks[c][b][:, tt, n0:n0 + 128],
-                                        lhsT=w4p[:, a, 256 * t:256 * (t + 1)].bitcast(FP4X4),
-                                        lhsT_scale=planes[:, a, S + 128 * t:S + 128 * (t + 1)],
-                                        rhs=vg[a][:, cols].bitcast(FP8X4), rhs_scale=planes[:, a, cols],
-                                        start=(start and tt == 0 and n0 == 0), stop=False)
-            for tt in range(2):
-                t = 2 * b + tt
-                cols = slice(c * CH, (c + 1) * CH)
-                nc.tensor.matmul_mx(out=banks[c][b][:, tt, :],
-                                    lhsT=w1c[a][:, 128 * t:128 * (t + 1)].bitcast(FP8X4),
-                                    lhsT_scale=w1s[a][:, 128 * t:128 * (t + 1)],
-                                    rhs=vg[a][:, cols].bitcast(FP8X4), rhs_scale=planes[:, a, cols],
-                                    start=False, stop=(stop and tt == 1))
+        def stored(a, u, t):
+            cols = slice(512 * u, 512 * (u + 1))
+            nc.tensor.matmul_mx(out=banks[u][t][:], lhsT=w4p[:, a, 256 * t:256 * (t + 1)].bitcast(FP4X4),
+                                lhsT_scale=planes[:, a, S + 128 * t:S + 128 * (t + 1)],
+                                rhs=vg[a][:, cols].bitcast(FP8X4), rhs_scale=planes[:, a, cols],
+                                start=(a == 0), stop=False)
 
-        for c in range(NCH):
-            for b in range(2):
-                stage_one(0, c, b, True, False)
+        def learned(a, u, t):
+            cols = slice(512 * u, 512 * (u + 1))
+            nc.tensor.matmul_mx(out=banks[u][t][:], lhsT=w1c[a][:, 128 * t:128 * (t + 1)].bitcast(FP8X4),
+                                lhsT_scale=w1s[a][:, 128 * t:128 * (t + 1)],
+                                rhs=vg[a][:, cols].bitcast(FP8X4), rhs_scale=planes[:, a, cols],
+                                start=False, stop=(a == 1))
 
+        for u in range(2):
+            for t in range(4):
+                stored(0, u, t)
+        for u in range(2):
+            for t in range(4):
+                learned(0, u, t)
+        vg.append(held([P, S], U32, "vg1", tag="w1b0"))
         for u in range(2):
             nc.vector.tensor_copy(vg[1][:, 512 * u:512 * (u + 1)],
                                   v_win[1][:].bitcast(U32).indirect(idx[:, 32 * u:32 * (u + 1)]))
-        nc.scalar.activation(dealt(1)[:, 0:64], w1_raw1[0][:].rearrange("p j (m t) -> p m j t", t=4), ACT.Copy)
-        nc.scalar.activation(dealt(1)[:, 64:128], w1_raw1[1][:].rearrange("p j (m t) -> p m j t", t=4), ACT.Copy)
+            for t in range(4):
+                stored(1, u, t)
+        nc.scalar.activation(dealt(1)[:, 0:W1_SPLIT], rows(1)[:, 0:W1_SPLIT], ACT.Copy)
+        nc.vector.tensor_copy(dealt(1)[:, W1_SPLIT:P], rows(1)[:, W1_SPLIT:P])
         for b in range(2):
             nc.vector.quantize_mx(out=w1c[1][:, 256 * b:256 * (b + 1)].bitcast(FP8X4),
                                   scales=w1s[1][:, 256 * b:256 * (b + 1)],
                                   in_=w1b[1][:, 1024 * b:1024 * (b + 1)])
-        for c in range(NCH):
-            for b in range(2):
-                stage_one(1, c, b, False, True)
+        for u in range(2):
+            for t in range(4):
+                learned(1, u, t)
 
-        v2g = held([P, S2], U32, "v2g")
+        v2g = held([P, S2], U32, "v2g", tag="w1b1")
         v2p = held([P, S2], I32, "v2p")
         for gi in range(2):
             half = slice(512 * gi, 512 * (gi + 1))
@@ -157,23 +157,26 @@ def tile_list_cortex_rates_kernel(tc, tab_words, tab_scales, offs, tab2_words, t
 
         ysc = held([P, S], U8, "ysc")
         hq = {}
+        squares = [[held([P, 2, 512], F32, "q%d_%d" % (u, b)) for b in range(2)] for u in range(2)]
 
         def respond(c):
-            q = [work.tile([P, 2, CH], F32, name="q%d" % b) for b in range(2)]
             s = [work.tile([P, 2, CH], F32, name="s%d" % b) for b in range(2)]
             r = [work.tile([P, 2, CH], F32, name="r%d" % b) for b in range(2)]
             hb = work.tile([P, 4, CH], BF16, name="hb")
             hi = work.tile([P, 4 * CH], BF16, name="hi", align_bytes=64)
             hc = work.tile([P, CH], U32, name="hc", align_bytes=64)
             hs = work.tile([P, CH], U8, name="hs", align_bytes=64)
+            u, cols = c // 2, slice((c % 2) * CH, (c % 2 + 1) * CH)
+            q = squares[u]
             for b in range(2):
-                nc.scalar.activation(q[b][:], banks[c][b][:], ACT.Square)
-            for b in range(2):
-                nc.scalar.activation(s[b][:], q[b][:], ACT.Abs_reciprocal_sqrt, bias=SHIFT, scale=SHIFT)
+                if c % 2 == 0:
+                    for tt in range(2):
+                        nc.scalar.activation(q[b][:, tt, :], banks[u][2 * b + tt][:], ACT.Square)
+                nc.scalar.activation(s[b][:], q[b][:, :, cols], ACT.Abs_reciprocal_sqrt, bias=SHIFT, scale=SHIFT)
             for b in range(2):
                 nc.scalar.activation(r[b][:], s[b][:], ACT.Square, scale=math.sqrt(SHIFT))
             for t in range(4):
-                nc.vector.scalar_tensor_tensor(hb[:, t, :], q[t // 2][:, t % 2, :], g_sb[:, t:t + 1],
+                nc.vector.scalar_tensor_tensor(hb[:, t, :], q[t // 2][:, t % 2, cols], g_sb[:, t:t + 1],
                                                r[t // 2][:, t % 2, :], ALU.mult, ALU.mult)
             nc.vector.tensor_copy(hi[:].rearrange("p (c i t) -> p c t i", i=4, t=4),
                                   hb[:].rearrange("p t (c i) -> p c t i", i=4))
@@ -188,7 +191,7 @@ def tile_list_cortex_rates_kernel(tc, tab_words, tab_scales, offs, tab2_words, t
                 yb = work.tile([P, 4 * CH], BF16, name="yb", bufs=3, align_bytes=64)
                 yc = work.tile([P, CH], U32, name="yc", bufs=4, align_bytes=64)
                 for b in range(2):
-                    drive = psum.tile([P, 2, CH], F32, name="bank", tag="bank")
+                    drive = psum.tile([P, 2, CH], F32, name="drive", tag="bank")
                     for tt in range(2):
                         m0 = 512 * gi + 128 * (2 * b + tt)
                         nc.tensor.matmul_mx(out=drive[:, tt, :], lhsT=v2p[:, m0:m0 + 128].bitcast(FP8X4),

@@ -19,7 +19,7 @@ P = 128
 CH = 256
 NCH = S // CH
 SHIFT = 1.375
-W1_SPLIT = 44
+W1_SPLIT = 64
 FLOPS = 2 * (2 * K * H * S + H * S * S2)
 
 
@@ -159,27 +159,40 @@ def tile_list_cortex_rates_kernel(tc, tab_words, tab_scales, offs, tab2_words, t
         hq = {}
         squares = [[held([P, 2, 512], F32, "q%d_%d" % (u, b)) for b in range(2)] for u in range(2)]
 
-        def respond(c):
-            s = [work.tile([P, 2, CH], F32, name="s%d" % b) for b in range(2)]
-            r = [work.tile([P, 2, CH], F32, name="r%d" % b) for b in range(2)]
-            hb = work.tile([P, 4, CH], BF16, name="hb")
-            hi = work.tile([P, 4 * CH], BF16, name="hi", align_bytes=64)
-            hc = work.tile([P, CH], U32, name="hc", align_bytes=64)
-            hs = work.tile([P, CH], U8, name="hs", align_bytes=64)
+        recips = {}
+
+        def curve(c):
             u, cols = c // 2, slice((c % 2) * CH, (c % 2 + 1) * CH)
             q = squares[u]
+            s = [work.tile([P, 2, CH], F32, name="s%d" % b) for b in range(2)]
+            r = [work.tile([P, 2, CH], F32, name="r%d" % b, bufs=NCH) for b in range(2)]
             for b in range(2):
-                if c % 2 == 0:
-                    for tt in range(2):
+                for tt in range(2):
+                    if u == 0:
+                        nc.scalar.activation(q[b][:, tt, cols], banks[u][2 * b + tt][:, cols], ACT.Square)
+                    elif c % 2 == 0:
                         nc.scalar.activation(q[b][:, tt, :], banks[u][2 * b + tt][:], ACT.Square)
                 nc.scalar.activation(s[b][:], q[b][:, :, cols], ACT.Abs_reciprocal_sqrt, bias=SHIFT, scale=SHIFT)
             for b in range(2):
                 nc.scalar.activation(r[b][:], s[b][:], ACT.Square, scale=math.sqrt(SHIFT))
+            recips[c] = r
+
+        def respond(c):
+            u, cols = c // 2, slice((c % 2) * CH, (c % 2 + 1) * CH)
+            q, r = squares[u], recips[c]
+            hb = work.tile([P, 4, CH], BF16, name="hb")
+            hi = work.tile([P, 4 * CH], BF16, name="hi", align_bytes=64)
+            hc = work.tile([P, CH], U32, name="hc", align_bytes=64)
+            hs = work.tile([P, CH], U8, name="hs", align_bytes=64)
             for t in range(4):
                 nc.vector.scalar_tensor_tensor(hb[:, t, :], q[t // 2][:, t % 2, cols], g_sb[:, t:t + 1],
                                                r[t // 2][:, t % 2, :], ALU.mult, ALU.mult)
-            nc.vector.tensor_copy(hi[:].rearrange("p (c i t) -> p c t i", i=4, t=4),
-                                  hb[:].rearrange("p t (c i) -> p c t i", i=4))
+            if c == 0:
+                nc.vector.tensor_copy(hi[:].rearrange("p (c i t) -> p c t i", i=4, t=4),
+                                      hb[:].rearrange("p t (c i) -> p c t i", i=4))
+            else:
+                nc.gpsimd.tensor_scalar(hi[:].rearrange("p (j t) -> p j t", t=4), hb[:].rearrange("p t j -> p j t"),
+                                        1.0, 0.0, ALU.mult, ALU.add)
             nc.vector.quantize_mx(out=hc[:].bitcast(FP8X4), scales=hs[:], in_=hi[:])
             hq[c] = (hc, hs)
 
@@ -187,9 +200,9 @@ def tile_list_cortex_rates_kernel(tc, tab_words, tab_scales, offs, tab2_words, t
             hc, hs = hq[c]
             cols = slice(c * CH, (c + 1) * CH)
             for gi in range(2):
-                y = work.tile([P, 4, CH], F32, name="y", bufs=4)
-                yb = work.tile([P, 4 * CH], BF16, name="yb", bufs=3, align_bytes=64)
-                yc = work.tile([P, CH], U32, name="yc", bufs=4, align_bytes=64)
+                y = work.tile([P, 4, CH], F32, name="y", bufs=2 * NCH)
+                yb = work.tile([P, 4 * CH], BF16, name="yb", bufs=2 * NCH, align_bytes=64)
+                yc = work.tile([P, CH], U32, name="yc", bufs=2 * NCH, align_bytes=64)
                 for b in range(2):
                     drive = psum.tile([P, 2, CH], F32, name="drive", tag="bank")
                     for tt in range(2):
@@ -205,12 +218,17 @@ def tile_list_cortex_rates_kernel(tc, tab_words, tab_scales, offs, tab2_words, t
                 src = y[:].rearrange("p t (c i) -> p c t i", i=4)
                 if c == NCH - 1 and gi == 1:
                     nc.vector.tensor_copy(dst, src)
+                elif c in (0, 1) and gi == 0:
+                    nc.gpsimd.tensor_scalar(yb[:].rearrange("p (j t) -> p j t", t=4), y[:].rearrange("p t j -> p j t"),
+                                            1.0, 0.0, ALU.mult, ALU.add)
                 else:
                     nc.scalar.activation(dst, src, ACT.Copy)
                 nc.vector.quantize_mx(out=yc[:].bitcast(FP8X4), scales=ysc[4 * gi:P, cols], in_=yb[:])
                 nc.sync.dma_start(out_1[gi, :, cols, :].rearrange("p m t -> p (m t)").bitcast(I32),
                                   yc[:].bitcast(I32))
 
+        for c in range(NCH):
+            curve(c)
         respond(0)
         for c in range(NCH):
             if c + 1 < NCH:

@@ -16,10 +16,11 @@ ALU = mybir.AluOpType
 
 K, T, S, H, T2, S2 = 1024, 4096, 1024, 512, 2048, 1024
 P = 128
-CH = 256
-NCH = S // CH
+PASS = 512
+CHUNK = 256
+CHUNKS = S // CHUNK
 SHIFT = 1.375
-W1_SPLIT = 64
+SCALAR_SHARE = 44
 FLOPS = 2 * (2 * K * H * S + H * S * S2)
 
 
@@ -34,206 +35,236 @@ def tile_list_cortex_rates_kernel(tc, tab_words, tab_scales, offs, tab2_words, t
         def held(shape, dtype, name, tag=None):
             return keep.tile(shape, dtype, name=name, tag=tag or name, align_bytes=64)
 
-        idx = keep.tile([P, S // 16], U16, name="idx")
-        idx2 = keep.tile([P, S2 // 16], U16, name="idx2")
-        vsc_win = held([P, T], U8, "vsc_win")
-        w4sc_raw = held([P, H], U8, "w4sc_raw")
-        v2sc_win = held([P, T2], U8, "v2sc_win")
-        v2sc = held([P, S2], U8, "v2sc")
-        planes = held([P, 2, S + H], U8, "planes")
+        images = keep.tile([P, S // 16], U16, name="images")
+        neurons = keep.tile([P, S2 // 16], U16, name="neurons")
+        v_scale_rows = held([P, T], U8, "v_scale_rows")
+        w4_scale_rows = held([P, H], U8, "w4_scale_rows")
+        v2_scale_rows = held([P, T2], U8, "v2_scale_rows")
+        v2_scales = held([P, S2], U8, "v2_scales")
+        k_scales = held([P, 2, S + H], U8, "k_scales")
         w4_raw = held([P, 2, 2 * H], U8, "w4_raw")
-        v_win = [held([P, T], I32, "v_win%d" % a) for a in range(2)]
-        v2_win = held([P, T2], I32, "v2_win")
+        v_table = [held([P, T], I32, "v_table%d" % a) for a in range(2)]
+        v2_table = held([P, T2], I32, "v2_table")
         w1_raw = [held([P, 4, H], F32, "w1_raw%d" % a) for a in range(2)]
-        g_sb = held([P, 4], F32, "g_sb")
-        base_sb = held([P, 2, 4], F32, "base_sb")
+        gain = held([P, 4], F32, "gain")
+        floor = held([P, 2, 4], F32, "floor")
         warm = held([P, 2], F32, "warm")
 
         nc.vector.memset(warm[:, 0:1], 1.0)
-        for lo, hi in ((32, 64), (64, 128)):
-            nc.vector.memset(vsc_win[lo:hi, :].bitcast(I32), 0)
-        for lo, hi in ((32, 64), (64, 128)):
-            nc.vector.memset(w4sc_raw[lo:hi, :].bitcast(I32), 0)
-        nc.gpsimd.memset(v2sc_win[:].bitcast(I32), 0)
-        nc.gpsimd.memset(planes[:].rearrange("p a c -> p (a c)").bitcast(I32), 0)
-        nc.gpsimd.memset(v2sc[:].bitcast(I32), 0)
+        for lo, hi in ((32, 64), (64, P)):
+            nc.vector.memset(v_scale_rows[lo:hi, :].bitcast(I32), 0)
+        for lo, hi in ((32, 64), (64, P)):
+            nc.vector.memset(w4_scale_rows[lo:hi, :].bitcast(I32), 0)
+        nc.gpsimd.memset(v2_scale_rows[:].bitcast(I32), 0)
+        nc.gpsimd.memset(k_scales[:].rearrange("p a c -> p (a c)").bitcast(I32), 0)
+        nc.gpsimd.memset(v2_scales[:].bitcast(I32), 0)
         nc.scalar.activation(warm[:, 1:2], warm[:, 0:1], ACT.Abs_reciprocal_sqrt)
 
-        nc.sync.dma_start(idx[:], offs)
-        nc.sync.dma_start(vsc_win[0:32, :].bitcast(I32), tab_scales.rearrange("a q c -> q a c").bitcast(I32))
-        nc.sync.dma_start(w4sc_raw[0:32, :].bitcast(I32), w4_scales.rearrange("a q c -> q a c").bitcast(I32))
+        nc.sync.dma_start(images[:], offs)
+        nc.sync.dma_start(v_scale_rows[0:32, :].bitcast(I32), tab_scales.rearrange("a q c -> q a c").bitcast(I32))
+        nc.sync.dma_start(w4_scale_rows[0:32, :].bitcast(I32), w4_scales.rearrange("a q c -> q a c").bitcast(I32))
         nc.sync.dma_start(w4_raw[:].bitcast(I32), w4_words.rearrange("a p c -> p a c").bitcast(I32))
-        nc.sync.dma_start(v_win[0][:], tab_words[0].rearrange("p t i -> p (t i)").bitcast(I32))
-        nc.sync.dma_start(idx2[:], offs2)
-        nc.sync.dma_start(v2sc_win[0:16, :].bitcast(I32), tab2_scales[0].bitcast(I32))
-        nc.sync.dma_start(g_sb[:], g.rearrange("(p t) -> p t", t=4))
-        nc.sync.dma_start(base_sb[:], base.rearrange("(g p t) -> p g t", g=2, t=4))
-        nc.sync.dma_start(w1_raw[0][:], w1[0:512, :].rearrange("(p j) c -> p j c", j=4))
-        nc.sync.dma_start(v_win[1][:], tab_words[1].rearrange("p t i -> p (t i)").bitcast(I32))
-        nc.sync.dma_start(w1_raw[1][:], w1[512:1024, :].rearrange("(p j) c -> p j c", j=4))
-        nc.sync.dma_start(v2_win[:], tab2_words[0].rearrange("p t i -> p (t i)").bitcast(I32))
+        nc.sync.dma_start(v_table[0][:], tab_words[0].rearrange("p t i -> p (t i)").bitcast(I32))
+        nc.sync.dma_start(neurons[:], offs2)
+        nc.sync.dma_start(v2_scale_rows[0:16, :].bitcast(I32), tab2_scales[0].bitcast(I32))
+        nc.sync.dma_start(gain[:], g.rearrange("(p t) -> p t", t=4))
+        nc.sync.dma_start(floor[:], base.rearrange("(a p t) -> p a t", a=2, t=4))
+        nc.sync.dma_start(w1_raw[0][:], w1[0:PASS, :].rearrange("(p j) c -> p j c", j=4))
+        nc.sync.dma_start(v_table[1][:], tab_words[1].rearrange("p t i -> p (t i)").bitcast(I32))
+        nc.sync.dma_start(w1_raw[1][:], w1[PASS:K, :].rearrange("(p j) c -> p j c", j=4))
+        nc.sync.dma_start(v2_table[:], tab2_words[0].rearrange("p t i -> p (t i)").bitcast(I32))
 
-        vsc_g = held([P, S], U8, "vsc_g")
-        stage = held([P, S + H], U8, "stage")
-        nc.vector.tensor_copy(vsc_g[:], vsc_win[:].indirect(idx[:]))
-        nc.vector.tensor_copy(stage[:, S:S + H].rearrange("p (t m) -> p m t", t=4),
-                              w4sc_raw[:].rearrange("p (m t) -> p m t", t=4))
-        nc.vector.tensor_copy(stage[:, 0:S].bitcast(I32), vsc_g[:].bitcast(I32))
-        for q4 in range(4):
-            nc.scalar.dma_start(planes[32 * q4:32 * q4 + 4, :, :].bitcast(I32),
-                                stage[8 * q4:8 * q4 + 8, :].bitcast(I32))
-        w4p = held([P, 2, 2 * H], U8, "w4p")
-        nc.vector.tensor_copy(w4p[:].bitcast(U16).rearrange("p a (t m) -> p a m t", t=4),
+        v_scale_picked = held([P, S], U8, "v_scale_picked")
+        staged = held([P, S + H], U8, "staged")
+        nc.vector.tensor_copy(v_scale_picked[:], v_scale_rows[:].indirect(images[:]))
+        nc.vector.tensor_copy(staged[:, S:S + H].rearrange("p (t m) -> p m t", t=4),
+                              w4_scale_rows[:].rearrange("p (m t) -> p m t", t=4))
+        nc.vector.tensor_copy(staged[:, 0:S].bitcast(I32), v_scale_picked[:].bitcast(I32))
+        for quad in range(4):
+            nc.scalar.dma_start(k_scales[32 * quad:32 * quad + 4, :, :].bitcast(I32),
+                                staged[8 * quad:8 * quad + 8, :].bitcast(I32))
+        w4_dealt = held([P, 2, 2 * H], U8, "w4_dealt")
+        nc.vector.tensor_copy(w4_dealt[:].bitcast(U16).rearrange("p a (t m) -> p a m t", t=4),
                               w4_raw[:].bitcast(U16).rearrange("p a (m t) -> p a m t", t=4))
 
-        vg = [held([P, S], U32, "vg0")]
-        nc.vector.tensor_copy(vg[0][:], v_win[0][:].bitcast(U32).indirect(idx[:]))
+        v_picked = [held([P, S], U32, "v_picked0")]
+        nc.vector.tensor_copy(v_picked[0][:], v_table[0][:].bitcast(U32).indirect(images[:]))
 
-        w1b = [held([P, 4 * H], BF16, "w1b%d" % a) for a in range(2)]
-        w1c = [held([P, H], U32, "w1c%d" % a) for a in range(2)]
-        w1s = [held([P, H], U8, "w1s%d" % a) for a in range(2)]
+        w1_woven = [held([P, 4 * H], BF16, "w1_woven%d" % a) for a in range(2)]
+        w1_codes = [held([P, H], U32, "w1_codes%d" % a) for a in range(2)]
+        w1_scales = [held([P, H], U8, "w1_scales%d" % a) for a in range(2)]
 
-        def dealt(a):
-            return w1b[a][:].rearrange("p (t m j) -> p m j t", t=4, j=4)
+        def w1_target(a):
+            return w1_woven[a][:].rearrange("p (t m j) -> p m j t", t=4, j=4)
 
-        def rows(a):
+        def w1_source(a):
             return w1_raw[a][:].rearrange("p j (m t) -> p m j t", t=4)
 
-        nc.scalar.activation(dealt(0), rows(0), ACT.Copy)
-        v2sc_g = held([P, S2], U8, "v2sc_g")
-        nc.vector.tensor_copy(v2sc_g[:], v2sc_win[:].indirect(idx2[:]))
-        nc.vector.quantize_mx(out=w1c[0][:].bitcast(FP8X4), scales=w1s[0][:], in_=w1b[0][:])
-        v2sc_p = held([P, S2], U8, "v2sc_p", tag="w1_raw0")
-        nc.vector.tensor_copy(v2sc_p[:].rearrange("p (g t m) -> p g m t", g=2, t=4),
-                              v2sc_g[:].rearrange("p (g m t) -> p g m t", g=2, t=4))
-        for q4 in range(4):
-            nc.sync.dma_start(v2sc[32 * q4:32 * q4 + 4, :].bitcast(I32), v2sc_p[4 * q4:4 * q4 + 4, :].bitcast(I32))
+        nc.scalar.activation(w1_target(0), w1_source(0), ACT.Copy)
+        v2_scale_picked = held([P, S2], U8, "v2_scale_picked")
+        nc.vector.tensor_copy(v2_scale_picked[:], v2_scale_rows[:].indirect(neurons[:]))
+        nc.vector.quantize_mx(out=w1_codes[0][:].bitcast(FP8X4), scales=w1_scales[0][:], in_=w1_woven[0][:])
+        v2_scale_dealt = held([P, S2], U8, "v2_scale_dealt", tag="w1_raw0")
+        nc.vector.tensor_copy(v2_scale_dealt[:].rearrange("p (a t m) -> p a m t", a=2, t=4),
+                              v2_scale_picked[:].rearrange("p (a m t) -> p a m t", a=2, t=4))
+        for quad in range(4):
+            nc.sync.dma_start(v2_scales[32 * quad:32 * quad + 4, :].bitcast(I32),
+                              v2_scale_dealt[4 * quad:4 * quad + 4, :].bitcast(I32))
 
-        banks = [[psum.tile([P, 512], F32, name="bank", tag="bank") for t in range(4)] for u in range(2)]
+        banks = [[psum.tile([P, PASS], F32, name="bank", tag="bank") for t in range(4)] for u in range(2)]
 
-        def stored(a, u, t):
-            cols = slice(512 * u, 512 * (u + 1))
-            nc.tensor.matmul_mx(out=banks[u][t][:], lhsT=w4p[:, a, 256 * t:256 * (t + 1)].bitcast(FP4X4),
-                                lhsT_scale=planes[:, a, S + 128 * t:S + 128 * (t + 1)],
-                                rhs=vg[a][:, cols].bitcast(FP8X4), rhs_scale=planes[:, a, cols],
-                                start=(a == 0), stop=False)
+        def stored_pass(a, u, t, start=False, stop=False):
+            cols = slice(PASS * u, PASS * (u + 1))
+            nc.tensor.matmul_mx(out=banks[u][t][:], lhsT=w4_dealt[:, a, 2 * P * t:2 * P * (t + 1)].bitcast(FP4X4),
+                                lhsT_scale=k_scales[:, a, S + P * t:S + P * (t + 1)],
+                                rhs=v_picked[a][:, cols].bitcast(FP8X4), rhs_scale=k_scales[:, a, cols],
+                                start=start, stop=stop)
 
-        def learned(a, u, t):
-            cols = slice(512 * u, 512 * (u + 1))
-            nc.tensor.matmul_mx(out=banks[u][t][:], lhsT=w1c[a][:, 128 * t:128 * (t + 1)].bitcast(FP8X4),
-                                lhsT_scale=w1s[a][:, 128 * t:128 * (t + 1)],
-                                rhs=vg[a][:, cols].bitcast(FP8X4), rhs_scale=planes[:, a, cols],
-                                start=False, stop=(a == 1))
+        def learned_pass(a, u, t, stop=False):
+            cols = slice(PASS * u, PASS * (u + 1))
+            nc.tensor.matmul_mx(out=banks[u][t][:], lhsT=w1_codes[a][:, P * t:P * (t + 1)].bitcast(FP8X4),
+                                lhsT_scale=w1_scales[a][:, P * t:P * (t + 1)],
+                                rhs=v_picked[a][:, cols].bitcast(FP8X4), rhs_scale=k_scales[:, a, cols],
+                                start=False, stop=stop)
 
         for u in range(2):
             for t in range(4):
-                stored(0, u, t)
+                stored_pass(0, u, t, start=True)
         for u in range(2):
             for t in range(4):
-                learned(0, u, t)
-        vg.append(held([P, S], U32, "vg1", tag="w1b0"))
+                learned_pass(0, u, t)
+        v_picked.append(held([P, S], U32, "v_picked1", tag="w1_woven0"))
         for u in range(2):
-            nc.vector.tensor_copy(vg[1][:, 512 * u:512 * (u + 1)],
-                                  v_win[1][:].bitcast(U32).indirect(idx[:, 32 * u:32 * (u + 1)]))
-            for t in range(4):
-                stored(1, u, t)
-        nc.scalar.activation(dealt(1)[:, 0:W1_SPLIT], rows(1)[:, 0:W1_SPLIT], ACT.Copy)
-        nc.vector.tensor_copy(dealt(1)[:, W1_SPLIT:P], rows(1)[:, W1_SPLIT:P])
-        for b in range(2):
-            nc.vector.quantize_mx(out=w1c[1][:, 256 * b:256 * (b + 1)].bitcast(FP8X4),
-                                  scales=w1s[1][:, 256 * b:256 * (b + 1)],
-                                  in_=w1b[1][:, 1024 * b:1024 * (b + 1)])
-        for u in range(2):
-            for t in range(4):
-                learned(1, u, t)
+            nc.vector.tensor_copy(v_picked[1][:, PASS * u:PASS * (u + 1)],
+                                  v_table[1][:].bitcast(U32).indirect(images[:, 32 * u:32 * (u + 1)]))
+        for t in range(4):
+            stored_pass(1, 0, t)
+        nc.scalar.activation(w1_target(1)[:, 0:SCALAR_SHARE], w1_source(1)[:, 0:SCALAR_SHARE], ACT.Copy)
+        nc.vector.tensor_copy(w1_target(1)[:, SCALAR_SHARE:P], w1_source(1)[:, SCALAR_SHARE:P])
+        for pair in range(2):
+            cols = slice(2 * P * pair, 2 * P * (pair + 1))
+            nc.vector.quantize_mx(out=w1_codes[1][:, cols].bitcast(FP8X4), scales=w1_scales[1][:, cols],
+                                  in_=w1_woven[1][:, 8 * P * pair:8 * P * (pair + 1)])
+        for t in range(4):
+            learned_pass(1, 0, t, stop=True)
+        for t in range(4):
+            learned_pass(1, 1, t)
+            stored_pass(1, 1, t, stop=True)
 
-        v2g = held([P, S2], U32, "v2g", tag="w1b1")
-        v2p = held([P, S2], I32, "v2p")
-        for gi in range(2):
-            half = slice(512 * gi, 512 * (gi + 1))
-            nc.vector.tensor_copy(v2g[:, half], v2_win[:].bitcast(U32).indirect(idx2[:, 32 * gi:32 * (gi + 1)]))
-            nc.vector.tensor_copy(v2p[:, half].rearrange("p (t m) -> p m t", t=4),
-                                  v2g[:, half].bitcast(I32).rearrange("p (m t) -> p m t", t=4))
+        v2_picked = held([P, S2], U32, "v2_picked", tag="w1_woven1")
+        v2_dealt = held([P, S2], I32, "v2_dealt")
+        for a in range(2):
+            nc.vector.tensor_copy(v2_picked[:, PASS * a:PASS * (a + 1)],
+                                  v2_table[:].bitcast(U32).indirect(neurons[:, 32 * a:32 * (a + 1)]))
 
-        ysc = held([P, S], U8, "ysc")
-        hq = {}
-        squares = [[held([P, 2, 512], F32, "q%d_%d" % (u, b)) for b in range(2)] for u in range(2)]
+        def deal_v2(a):
+            cols = slice(PASS * a, PASS * (a + 1))
+            nc.vector.tensor_copy(v2_dealt[:, cols].rearrange("p (t m) -> p m t", t=4),
+                                  v2_picked[:, cols].bitcast(I32).rearrange("p (m t) -> p m t", t=4))
 
-        recips = {}
+        y_scales = held([P, S], U8, "y_scales")
+        squares = [[held([P, 2, PASS], F32, "square%d_%d" % (u, pair)) for pair in range(2)] for u in range(2)]
+        inverses = {}
 
         def curve(c):
-            u, cols = c // 2, slice((c % 2) * CH, (c % 2 + 1) * CH)
-            q = squares[u]
-            s = [work.tile([P, 2, CH], F32, name="s%d" % b) for b in range(2)]
-            r = [work.tile([P, 2, CH], F32, name="r%d" % b, bufs=NCH) for b in range(2)]
-            for b in range(2):
-                for tt in range(2):
+            u, cols = c // 2, slice((c % 2) * CHUNK, (c % 2 + 1) * CHUNK)
+            root = [work.tile([P, 2, CHUNK], F32, name="root%d" % pair) for pair in range(2)]
+            inverse = [work.tile([P, 2, CHUNK], F32, name="inverse%d" % pair, bufs=CHUNKS) for pair in range(2)]
+            for pair in range(2):
+                for n in range(2):
                     if u == 0:
-                        nc.scalar.activation(q[b][:, tt, cols], banks[u][2 * b + tt][:, cols], ACT.Square)
+                        nc.scalar.activation(squares[u][pair][:, n, cols], banks[u][2 * pair + n][:, cols],
+                                             ACT.Square)
                     elif c % 2 == 0:
-                        nc.scalar.activation(q[b][:, tt, :], banks[u][2 * b + tt][:], ACT.Square)
-                nc.scalar.activation(s[b][:], q[b][:, :, cols], ACT.Abs_reciprocal_sqrt, bias=SHIFT, scale=SHIFT)
-            for b in range(2):
-                nc.scalar.activation(r[b][:], s[b][:], ACT.Square, scale=math.sqrt(SHIFT))
-            recips[c] = r
+                        nc.scalar.activation(squares[u][pair][:, n, :], banks[u][2 * pair + n][:], ACT.Square)
+                nc.scalar.activation(root[pair][:], squares[u][pair][:, :, cols], ACT.Abs_reciprocal_sqrt,
+                                     bias=SHIFT, scale=SHIFT)
+            for pair in range(2):
+                nc.scalar.activation(inverse[pair][:], root[pair][:], ACT.Square, scale=math.sqrt(SHIFT))
+            inverses[c] = inverse
+
+        def woven_view(tile):
+            return tile[:].rearrange("p (c i t) -> p c t i", i=4, t=4)
+
+        def sliced_view(tile):
+            return tile[:].rearrange("p t (c i) -> p c t i", i=4)
+
+        h_sliced = [held([P, 4, CHUNK], BF16, "h_sliced%d" % c) for c in range(CHUNKS)]
+        h_woven = [held([P, 4 * CHUNK], BF16, "h_woven%d" % c) for c in range(CHUNKS)]
+        h_codes = [held([P, CHUNK], U32, "h_codes%d" % c) for c in range(CHUNKS)]
+        h_scales = [held([P, CHUNK], U8, "h_scales%d" % c) for c in range(CHUNKS)]
+        y = [[held([P, 4, CHUNK], F32, "y%d_%d" % (c, a)) for a in range(2)] for c in range(CHUNKS)]
+        y_woven = [[held([P, 4 * CHUNK], BF16, "y_woven%d_%d" % (c, a)) for a in range(2)] for c in range(CHUNKS)]
+        y_codes = [[held([P, CHUNK], U32, "y_codes%d_%d" % (c, a)) for a in range(2)] for c in range(CHUNKS)]
 
         def respond(c):
-            u, cols = c // 2, slice((c % 2) * CH, (c % 2 + 1) * CH)
-            q, r = squares[u], recips[c]
-            hb = work.tile([P, 4, CH], BF16, name="hb")
-            hi = work.tile([P, 4 * CH], BF16, name="hi", align_bytes=64)
-            hc = work.tile([P, CH], U32, name="hc", align_bytes=64)
-            hs = work.tile([P, CH], U8, name="hs", align_bytes=64)
+            u, cols = c // 2, slice((c % 2) * CHUNK, (c % 2 + 1) * CHUNK)
             for t in range(4):
-                nc.vector.scalar_tensor_tensor(hb[:, t, :], q[t // 2][:, t % 2, cols], g_sb[:, t:t + 1],
-                                               r[t // 2][:, t % 2, :], ALU.mult, ALU.mult)
-            if c == 0:
-                nc.vector.tensor_copy(hi[:].rearrange("p (c i t) -> p c t i", i=4, t=4),
-                                      hb[:].rearrange("p t (c i) -> p c t i", i=4))
-            else:
-                nc.gpsimd.tensor_scalar(hi[:].rearrange("p (j t) -> p j t", t=4), hb[:].rearrange("p t j -> p j t"),
-                                        1.0, 0.0, ALU.mult, ALU.add)
-            nc.vector.quantize_mx(out=hc[:].bitcast(FP8X4), scales=hs[:], in_=hi[:])
-            hq[c] = (hc, hs)
+                nc.vector.scalar_tensor_tensor(h_sliced[c][:, t, :], squares[u][t // 2][:, t % 2, cols],
+                                               gain[:, t:t + 1], inverses[c][t // 2][:, t % 2, :],
+                                               ALU.mult, ALU.mult)
 
-        def fire(c):
-            hc, hs = hq[c]
-            cols = slice(c * CH, (c + 1) * CH)
-            for gi in range(2):
-                y = work.tile([P, 4, CH], F32, name="y", bufs=2 * NCH)
-                yb = work.tile([P, 4 * CH], BF16, name="yb", bufs=2 * NCH, align_bytes=64)
-                yc = work.tile([P, CH], U32, name="yc", bufs=2 * NCH, align_bytes=64)
-                for b in range(2):
-                    drive = psum.tile([P, 2, CH], F32, name="drive", tag="bank")
-                    for tt in range(2):
-                        m0 = 512 * gi + 128 * (2 * b + tt)
-                        nc.tensor.matmul_mx(out=drive[:, tt, :], lhsT=v2p[:, m0:m0 + 128].bitcast(FP8X4),
-                                            lhsT_scale=v2sc[:, m0:m0 + 128], rhs=hc[:].bitcast(FP8X4),
-                                            rhs_scale=hs[:], start=True, stop=True)
-                    nc.vector.tensor_tensor(y[:, 2 * b:2 * b + 2, :], drive[:],
-                                            base_sb[:, gi, 2 * b:2 * b + 2].unsqueeze(2).to_broadcast([P, 2, CH]),
-                                            ALU.max)
-                nc.sync.dma_start(out_0[512 * gi:512 * (gi + 1), cols].rearrange("(p t) j -> p t j", t=4), y[:])
-                dst = yb[:].rearrange("p (c i t) -> p c t i", i=4, t=4)
-                src = y[:].rearrange("p t (c i) -> p c t i", i=4)
-                if c == NCH - 1 and gi == 1:
-                    nc.vector.tensor_copy(dst, src)
-                elif c in (0, 1) and gi == 0:
-                    nc.gpsimd.tensor_scalar(yb[:].rearrange("p (j t) -> p j t", t=4), y[:].rearrange("p t j -> p j t"),
-                                            1.0, 0.0, ALU.mult, ALU.add)
-                else:
-                    nc.scalar.activation(dst, src, ACT.Copy)
-                nc.vector.quantize_mx(out=yc[:].bitcast(FP8X4), scales=ysc[4 * gi:P, cols], in_=yb[:])
-                nc.sync.dma_start(out_1[gi, :, cols, :].rearrange("p m t -> p (m t)").bitcast(I32),
-                                  yc[:].bitcast(I32))
+        def weave_h(c):
+            nc.vector.tensor_copy(woven_view(h_woven[c]), sliced_view(h_sliced[c]))
 
-        for c in range(NCH):
+        def quantise_h(c):
+            nc.vector.quantize_mx(out=h_codes[c][:].bitcast(FP8X4), scales=h_scales[c][:], in_=h_woven[c][:])
+
+        def fire(c, a, pair):
+            drive = psum.tile([P, 2, CHUNK], F32, name="drive", tag="bank")
+            for n in range(2):
+                cols = slice(PASS * a + P * (2 * pair + n), PASS * a + P * (2 * pair + n + 1))
+                nc.tensor.matmul_mx(out=drive[:, n, :], lhsT=v2_dealt[:, cols].bitcast(FP8X4),
+                                    lhsT_scale=v2_scales[:, cols], rhs=h_codes[c][:].bitcast(FP8X4),
+                                    rhs_scale=h_scales[c][:], start=True, stop=True)
+            slices = slice(2 * pair, 2 * pair + 2)
+            nc.vector.tensor_tensor(y[c][a][:, slices, :], drive[:],
+                                    floor[:, a, slices].unsqueeze(2).to_broadcast([P, 2, CHUNK]), ALU.max)
+
+        def store_y(c, a):
+            rows = out_0[PASS * a:PASS * (a + 1), c * CHUNK:(c + 1) * CHUNK]
+            nc.sync.dma_start(rows.rearrange("(p t) j -> p t j", t=4), y[c][a][:])
+
+        def quantise_y(c, a):
+            cols = slice(c * CHUNK, (c + 1) * CHUNK)
+            nc.vector.quantize_mx(out=y_codes[c][a][:].bitcast(FP8X4), scales=y_scales[4 * a:P, cols],
+                                  in_=y_woven[c][a][:])
+            nc.sync.dma_start(out_1[a, :, cols, :].rearrange("p m t -> p (m t)").bitcast(I32),
+                              y_codes[c][a][:].bitcast(I32))
+
+        def weave_y_on_scalar(c, a):
+            nc.scalar.activation(woven_view(y_woven[c][a]), sliced_view(y[c][a]), ACT.Copy)
+
+        for c in range(CHUNKS):
             curve(c)
         respond(0)
-        for c in range(NCH):
-            if c + 1 < NCH:
-                respond(c + 1)
-            fire(c)
-        for q4 in range(4):
-            eng = nc.sync if q4 % 2 == 0 else nc.scalar
-            eng.dma_start(out_2[:, 4 * q4:4 * q4 + 4, :].bitcast(I32), ysc[32 * q4:32 * q4 + 8, :].bitcast(I32))
+        deal_v2(0)
+        weave_h(0)
+        deal_v2(1)
+        quantise_h(0)
+        for c in range(CHUNKS - 1):
+            respond(c + 1)
+            fire(c, 0, 0)
+            weave_h(c + 1)
+            fire(c, 0, 1)
+            store_y(c, 0)
+            quantise_h(c + 1)
+            fire(c, 1, 0)
+            fire(c, 1, 1)
+            store_y(c, 1)
+            for a in range(2):
+                weave_y_on_scalar(c, a)
+                quantise_y(c, a)
+        last = CHUNKS - 1
+        for a in range(2):
+            fire(last, a, 0)
+            fire(last, a, 1)
+            store_y(last, a)
+        weave_y_on_scalar(last, 0)
+        nc.vector.tensor_copy(woven_view(y_woven[last][1]), sliced_view(y[last][1]))
+        for a in range(2):
+            quantise_y(last, a)
+        for quad in range(4):
+            queue = nc.sync if quad % 2 == 0 else nc.scalar
+            queue.dma_start(out_2[:, 4 * quad:4 * quad + 4, :].bitcast(I32),
+                            y_scales[32 * quad:32 * quad + 8, :].bitcast(I32))

@@ -67,12 +67,12 @@ def tile_list_cortex_rates_kernel(tc, tab_words, tab_scales, offs, tab2_words, t
         nc.sync.dma_start(v_table[0][:], tab_words[0].rearrange("p t i -> p (t i)").bitcast(I32))
         nc.sync.dma_start(neurons[:], offs2)
         nc.sync.dma_start(v2_scale_rows[0:16, :].bitcast(I32), tab2_scales[0].bitcast(I32))
-        nc.sync.dma_start(gain[:], g.rearrange("(p t) -> p t", t=4))
-        nc.sync.dma_start(floor[:], base.rearrange("(a p t) -> p a t", a=2, t=4))
         nc.sync.dma_start(w1_raw[0][:], w1[0:PASS, :].rearrange("(p j) c -> p j c", j=4))
         nc.sync.dma_start(v_table[1][:], tab_words[1].rearrange("p t i -> p (t i)").bitcast(I32))
         nc.sync.dma_start(w1_raw[1][:], w1[PASS:K, :].rearrange("(p j) c -> p j c", j=4))
         nc.sync.dma_start(v2_table[:], tab2_words[0].rearrange("p t i -> p (t i)").bitcast(I32))
+        nc.sync.dma_start(gain[:], g.rearrange("(p t) -> p t", t=4))
+        nc.sync.dma_start(floor[:], base.rearrange("(a p t) -> p a t", a=2, t=4))
 
         v_scale_picked = held([P, S], U8, "v_scale_picked")
         staged = held([P, S + H], U8, "staged")
@@ -139,15 +139,22 @@ def tile_list_cortex_rates_kernel(tc, tab_words, tab_scales, offs, tab2_words, t
                                   v_table[1][:].bitcast(U32).indirect(images[:, 32 * u:32 * (u + 1)]))
         for t in range(4):
             stored_pass(1, 0, t)
-        nc.scalar.activation(w1_target(1)[:, 0:SCALAR_SHARE], w1_source(1)[:, 0:SCALAR_SHARE], ACT.Copy)
-        nc.vector.tensor_copy(w1_target(1)[:, SCALAR_SHARE:P], w1_source(1)[:, SCALAR_SHARE:P])
+        nc.scalar.activation(w1_target(1)[:, 0:SCALAR_SHARE, :, 0:2], w1_source(1)[:, 0:SCALAR_SHARE, :, 0:2], ACT.Copy)
+        nc.vector.tensor_copy(w1_target(1)[:, SCALAR_SHARE:P, :, 0:2], w1_source(1)[:, SCALAR_SHARE:P, :, 0:2])
+        nc.scalar.activation(w1_target(1)[:, 0:SCALAR_SHARE, :, 2:4], w1_source(1)[:, 0:SCALAR_SHARE, :, 2:4], ACT.Copy)
         for pair in range(2):
             cols = slice(2 * P * pair, 2 * P * (pair + 1))
+            if pair == 1:
+                nc.vector.tensor_copy(w1_target(1)[:, SCALAR_SHARE:P, :, 2:4], w1_source(1)[:, SCALAR_SHARE:P, :, 2:4])
             nc.vector.quantize_mx(out=w1_codes[1][:, cols].bitcast(FP8X4), scales=w1_scales[1][:, cols],
                                   in_=w1_woven[1][:, 8 * P * pair:8 * P * (pair + 1)])
+        for t in range(2):
+            stored_pass(1, 1, t)
         for t in range(4):
             learned_pass(1, 0, t, stop=True)
-        for t in range(4):
+        for t in range(2):
+            learned_pass(1, 1, t, stop=True)
+        for t in range(2, 4):
             learned_pass(1, 1, t)
             stored_pass(1, 1, t, stop=True)
 

@@ -29,7 +29,6 @@ def tile_list_cortex_rates_kernel(tc, tab_words, tab_scales, offs, tab2_words, t
     nc = tc.nc
     with ExitStack() as ctx:
         keep = ctx.enter_context(tc.tile_pool(name="keep", bufs=1))
-        work = ctx.enter_context(tc.tile_pool(name="work", bufs=2))
         psum = ctx.enter_context(tc.psum_pool(name="psum", bufs=8))
 
         def held(shape, dtype, name, tag=None):
@@ -71,8 +70,8 @@ def tile_list_cortex_rates_kernel(tc, tab_words, tab_scales, offs, tab2_words, t
         nc.sync.dma_start(v_table[1][:], tab_words[1].rearrange("p t i -> p (t i)").bitcast(I32))
         nc.sync.dma_start(w1_raw[1][:], w1[PASS:K, :].rearrange("(p j) c -> p j c", j=4))
         nc.sync.dma_start(v2_table[:], tab2_words[0].rearrange("p t i -> p (t i)").bitcast(I32))
-        nc.sync.dma_start(gain[:], g.rearrange("(p t) -> p t", t=4))
-        nc.sync.dma_start(floor[:], base.rearrange("(a p t) -> p a t", a=2, t=4))
+        nc.scalar.dma_start(gain[:], g.rearrange("(p t) -> p t", t=4))
+        nc.scalar.dma_start(floor[:], base.rearrange("(a p t) -> p a t", a=2, t=4))
 
         v_scale_picked = held([P, S], U8, "v_scale_picked")
         staged = held([P, S + H], U8, "staged")
@@ -88,7 +87,9 @@ def tile_list_cortex_rates_kernel(tc, tab_words, tab_scales, offs, tab2_words, t
                               w4_raw[:].bitcast(U16).rearrange("p a (m t) -> p a m t", t=4))
 
         v_picked = [held([P, S], U32, "v_picked0")]
-        nc.vector.tensor_copy(v_picked[0][:], v_table[0][:].bitcast(U32).indirect(images[:]))
+        for u in range(2):
+            nc.vector.tensor_copy(v_picked[0][:, PASS * u:PASS * (u + 1)],
+                                  v_table[0][:].bitcast(U32).indirect(images[:, 32 * u:32 * (u + 1)]))
 
         w1_woven = [held([P, 4 * H], BF16, "w1_woven%d" % a) for a in range(2)]
         w1_codes = [held([P, H], U32, "w1_codes%d" % a) for a in range(2)]
@@ -108,7 +109,7 @@ def tile_list_cortex_rates_kernel(tc, tab_words, tab_scales, offs, tab2_words, t
         nc.vector.tensor_copy(v2_scale_dealt[:].rearrange("p (a t m) -> p a m t", a=2, t=4),
                               v2_scale_picked[:].rearrange("p (a m t) -> p a m t", a=2, t=4))
         for quad in range(4):
-            nc.sync.dma_start(v2_scales[32 * quad:32 * quad + 4, :].bitcast(I32),
+            nc.scalar.dma_start(v2_scales[32 * quad:32 * quad + 4, :].bitcast(I32),
                               v2_scale_dealt[4 * quad:4 * quad + 4, :].bitcast(I32))
 
         banks = [[psum.tile([P, PASS], F32, name="bank", tag="bank") for t in range(4)] for u in range(2)]
@@ -148,13 +149,9 @@ def tile_list_cortex_rates_kernel(tc, tab_words, tab_scales, offs, tab2_words, t
                 nc.vector.tensor_copy(w1_target(1)[:, SCALAR_SHARE:P, :, 2:4], w1_source(1)[:, SCALAR_SHARE:P, :, 2:4])
             nc.vector.quantize_mx(out=w1_codes[1][:, cols].bitcast(FP8X4), scales=w1_scales[1][:, cols],
                                   in_=w1_woven[1][:, 8 * P * pair:8 * P * (pair + 1)])
-        for t in range(2):
-            stored_pass(1, 1, t)
         for t in range(4):
             learned_pass(1, 0, t, stop=True)
-        for t in range(2):
-            learned_pass(1, 1, t, stop=True)
-        for t in range(2, 4):
+        for t in range(4):
             learned_pass(1, 1, t)
             stored_pass(1, 1, t, stop=True)
 
@@ -169,109 +166,125 @@ def tile_list_cortex_rates_kernel(tc, tab_words, tab_scales, offs, tab2_words, t
             nc.vector.tensor_copy(v2_dealt[:, cols].rearrange("p (t m) -> p m t", t=4),
                                   v2_picked[:, cols].bitcast(I32).rearrange("p (m t) -> p m t", t=4))
 
-        y_scales = held([P, S], U8, "y_scales")
+        y_scales = held([P, 2, S], U8, "y_scales")
         squares = [[held([P, 2, PASS], F32, "square%d_%d" % (u, pair)) for pair in range(2)] for u in range(2)]
-        inverses = {}
+        pieces = [(c * CHUNK, CHUNK) for c in range(CHUNKS)]
+        roots = [[held([P, 2, w], F32, "root%d_%d" % (c, pair)) for pair in range(2)] for c, (j, w) in enumerate(pieces)]
+        inverses = [[held([P, 2, w], F32, "inverse%d_%d" % (c, pair)) for pair in range(2)] for c, (j, w) in enumerate(pieces)]
 
         def curve(c):
-            u, cols = c // 2, slice((c % 2) * CHUNK, (c % 2 + 1) * CHUNK)
-            root = [work.tile([P, 2, CHUNK], F32, name="root%d" % pair) for pair in range(2)]
-            inverse = [work.tile([P, 2, CHUNK], F32, name="inverse%d" % pair, bufs=CHUNKS) for pair in range(2)]
+            first, width = pieces[c]
+            u, cols = first // PASS, slice(first % PASS, first % PASS + width)
             for pair in range(2):
                 for n in range(2):
                     if u == 0:
-                        nc.scalar.activation(squares[u][pair][:, n, cols], banks[u][2 * pair + n][:, cols],
-                                             ACT.Square)
+                        nc.scalar.activation(squares[u][pair][:, n, cols], banks[u][2 * pair + n][:, cols], ACT.Square)
                     elif c % 2 == 0:
                         nc.scalar.activation(squares[u][pair][:, n, :], banks[u][2 * pair + n][:], ACT.Square)
-                nc.scalar.activation(root[pair][:], squares[u][pair][:, :, cols], ACT.Abs_reciprocal_sqrt,
+                nc.scalar.activation(roots[c][pair][:], squares[u][pair][:, :, cols], ACT.Abs_reciprocal_sqrt,
                                      bias=SHIFT, scale=SHIFT)
             for pair in range(2):
-                nc.scalar.activation(inverse[pair][:], root[pair][:], ACT.Square, scale=math.sqrt(SHIFT))
-            inverses[c] = inverse
+                nc.scalar.activation(inverses[c][pair][:], roots[c][pair][:], ACT.Square, scale=math.sqrt(SHIFT))
 
-        def woven_view(tile):
-            return tile[:].rearrange("p (c i t) -> p c t i", i=4, t=4)
+        def woven_view(ap):
+            return ap.rearrange("p (c i t) -> p c t i", i=4, t=4)
 
-        def sliced_view(tile):
-            return tile[:].rearrange("p t (c i) -> p c t i", i=4)
+        def sliced_view(ap):
+            return ap.rearrange("p t (c i) -> p c t i", i=4)
 
-        h_sliced = [held([P, 4, CHUNK], BF16, "h_sliced%d" % c) for c in range(CHUNKS)]
-        h_woven = [held([P, 4 * CHUNK], BF16, "h_woven%d" % c) for c in range(CHUNKS)]
-        h_codes = [held([P, CHUNK], U32, "h_codes%d" % c) for c in range(CHUNKS)]
-        h_scales = [held([P, CHUNK], U8, "h_scales%d" % c) for c in range(CHUNKS)]
-        y = [[held([P, 4, CHUNK], F32, "y%d_%d" % (c, a)) for a in range(2)] for c in range(CHUNKS)]
-        y_woven = [[held([P, 4 * CHUNK], BF16, "y_woven%d_%d" % (c, a)) for a in range(2)] for c in range(CHUNKS)]
-        y_codes = [[held([P, CHUNK], U32, "y_codes%d_%d" % (c, a)) for a in range(2)] for c in range(CHUNKS)]
+        h_sliced = [held([P, 4, w], BF16, "h_sliced%d" % c) for c, (j, w) in enumerate(pieces)]
+        h_woven = [held([P, 4 * w], BF16, "h_woven%d" % c) for c, (j, w) in enumerate(pieces)]
+        h_codes = [held([P, w], U32, "h_codes%d" % c) for c, (j, w) in enumerate(pieces)]
+        h_scales = [held([P, w], U8, "h_scales%d" % c) for c, (j, w) in enumerate(pieces)]
+        units = [(c, 0, CHUNK, a) for c in range(CHUNKS) for a in range(2)]
+        y = [held([P, 4, unit[2]], F32, "y%d" % n) for n, unit in enumerate(units)]
+        y_woven = [held([P, 4 * unit[2]], BF16, "y_woven%d" % n) for n, unit in enumerate(units)]
+        y_codes = held([P, 2, S], U32, "y_codes")
 
-        def respond(c):
-            u, cols = c // 2, slice((c % 2) * CHUNK, (c % 2 + 1) * CHUNK)
-            for t in range(4):
+        def respond(c, slices):
+            first, width = pieces[c]
+            u, cols = first // PASS, slice(first % PASS, first % PASS + width)
+            for t in slices:
                 nc.vector.scalar_tensor_tensor(h_sliced[c][:, t, :], squares[u][t // 2][:, t % 2, cols],
                                                gain[:, t:t + 1], inverses[c][t // 2][:, t % 2, :],
                                                ALU.mult, ALU.mult)
 
         def weave_h(c):
-            nc.vector.tensor_copy(woven_view(h_woven[c]), sliced_view(h_sliced[c]))
+            nc.vector.tensor_copy(woven_view(h_woven[c][:]), sliced_view(h_sliced[c][:]))
 
         def quantise_h(c):
             nc.vector.quantize_mx(out=h_codes[c][:].bitcast(FP8X4), scales=h_scales[c][:], in_=h_woven[c][:])
 
-        def fire(c, a, pair):
-            drive = psum.tile([P, 2, CHUNK], F32, name="drive", tag="bank")
-            for n in range(2):
-                cols = slice(PASS * a + P * (2 * pair + n), PASS * a + P * (2 * pair + n + 1))
-                nc.tensor.matmul_mx(out=drive[:, n, :], lhsT=v2_dealt[:, cols].bitcast(FP8X4),
-                                    lhsT_scale=v2_scales[:, cols], rhs=h_codes[c][:].bitcast(FP8X4),
-                                    rhs_scale=h_scales[c][:], start=True, stop=True)
-            slices = slice(2 * pair, 2 * pair + 2)
-            nc.vector.tensor_tensor(y[c][a][:, slices, :], drive[:],
-                                    floor[:, a, slices].unsqueeze(2).to_broadcast([P, 2, CHUNK]), ALU.max)
+        def image_columns(n):
+            c, start, width, a = units[n]
+            return slice(pieces[c][0] + start, pieces[c][0] + start + width)
 
-        def store_y(c, a):
-            rows = out_0[PASS * a:PASS * (a + 1), c * CHUNK:(c + 1) * CHUNK]
-            nc.sync.dma_start(rows.rearrange("(p t) j -> p t j", t=4), y[c][a][:])
+        def fire(n, bank):
+            c, start, width, a = units[n]
+            count = PASS // width
+            drive = psum.tile([P, count, width], F32, name="drive", tag="bank")
+            for i in range(count):
+                t = count * bank + i
+                cols = slice(PASS * a + P * t, PASS * a + P * (t + 1))
+                nc.tensor.matmul_mx(out=drive[:, i, :], lhsT=v2_dealt[:, cols].bitcast(FP8X4),
+                                    lhsT_scale=v2_scales[:, cols],
+                                    rhs=h_codes[c][:, start:start + width].bitcast(FP8X4),
+                                    rhs_scale=h_scales[c][:, start:start + width], start=True, stop=True)
+            slices = slice(count * bank, count * (bank + 1))
+            nc.vector.tensor_tensor(y[n][:, slices, :], drive[:],
+                                    floor[:, a, slices].unsqueeze(2).to_broadcast([P, count, width]), ALU.max)
 
-        def quantise_y(c, a):
-            cols = slice(c * CHUNK, (c + 1) * CHUNK)
-            nc.vector.quantize_mx(out=y_codes[c][a][:].bitcast(FP8X4), scales=y_scales[4 * a:P, cols],
-                                  in_=y_woven[c][a][:])
-            nc.sync.dma_start(out_1[a, :, cols, :].rearrange("p m t -> p (m t)").bitcast(I32),
-                              y_codes[c][a][:].bitcast(I32))
+        def store_y(n):
+            a = units[n][3]
+            rows = out_0[PASS * a:PASS * (a + 1), image_columns(n)]
+            nc.sync.dma_start(rows.rearrange("(p t) j -> p t j", t=4), y[n][:])
 
-        def weave_y_on_scalar(c, a):
-            nc.scalar.activation(woven_view(y_woven[c][a]), sliced_view(y[c][a]), ACT.Copy)
+        def quantise_y(n):
+            a, cols = units[n][3], image_columns(n)
+            nc.vector.quantize_mx(out=y_codes[:, a, cols].bitcast(FP8X4), scales=y_scales[:, a, cols],
+                                  in_=y_woven[n][:])
+
+        def store_codes(groups, cols, queue):
+            queue.dma_start(out_1[groups, :, cols, :].rearrange("a p m t -> p a (m t)").bitcast(I32),
+                              y_codes[:, groups, cols].bitcast(I32))
+
+        def weave_y_on_scalar(n):
+            nc.scalar.activation(woven_view(y_woven[n][:]), sliced_view(y[n][:]), ACT.Copy)
+
+        def weave_y_on_vector(n):
+            nc.vector.tensor_copy(woven_view(y_woven[n][:]), sliced_view(y[n][:]))
 
         for c in range(CHUNKS):
             curve(c)
-        respond(0)
+        respond(0, range(4))
         deal_v2(0)
         weave_h(0)
         deal_v2(1)
         quantise_h(0)
         for c in range(CHUNKS - 1):
-            respond(c + 1)
-            fire(c, 0, 0)
+            respond(c + 1, range(4))
+            fire(2 * c, 0)
             weave_h(c + 1)
-            fire(c, 0, 1)
-            store_y(c, 0)
+            fire(2 * c, 1)
+            store_y(2 * c)
             quantise_h(c + 1)
-            fire(c, 1, 0)
-            fire(c, 1, 1)
-            store_y(c, 1)
-            for a in range(2):
-                weave_y_on_scalar(c, a)
-                quantise_y(c, a)
-        last = CHUNKS - 1
-        for a in range(2):
-            fire(last, a, 0)
-            fire(last, a, 1)
-            store_y(last, a)
-        weave_y_on_scalar(last, 0)
-        nc.vector.tensor_copy(woven_view(y_woven[last][1]), sliced_view(y[last][1]))
-        for a in range(2):
-            quantise_y(last, a)
+            fire(2 * c + 1, 0)
+            fire(2 * c + 1, 1)
+            store_y(2 * c + 1)
+            for n in (2 * c, 2 * c + 1):
+                weave_y_on_scalar(n)
+                quantise_y(n)
+            store_codes(slice(0, 2), slice(c * CHUNK, (c + 1) * CHUNK), nc.sync)
+        for n in (6, 7):
+            fire(n, 0)
+            fire(n, 1)
+            store_y(n)
+        weave_y_on_scalar(6)
+        weave_y_on_vector(7)
+        quantise_y(6)
+        quantise_y(7)
+        store_codes(slice(0, 2), slice(3 * CHUNK, S), nc.scalar)
         for quad in range(4):
             queue = nc.sync if quad % 2 == 0 else nc.scalar
-            queue.dma_start(out_2[:, 4 * quad:4 * quad + 4, :].bitcast(I32),
-                            y_scales[32 * quad:32 * quad + 8, :].bitcast(I32))
+            queue.dma_start(out_2[:, 4 * quad:4 * quad + 4, :].rearrange("a n c -> n a c").bitcast(I32),
+                            y_scales[32 * quad:32 * quad + 4, :, :].bitcast(I32))

@@ -183,7 +183,7 @@ def tile_list_cortex_rates_kernel(tc, tab_words, tab_scales, offs, tab2_words, t
                         nc.scalar.activation(squares[u][pair][:, n, :], banks[u][2 * pair + n][:], ACT.Square)
                 nc.scalar.activation(roots[c][pair][:], squares[u][pair][:, :, cols], ACT.Abs_reciprocal_sqrt,
                                      bias=SHIFT, scale=SHIFT)
-            for pair in range(2):
+            for pair in range(2 if c > 0 else 0):
                 nc.scalar.activation(inverses[c][pair][:], roots[c][pair][:], ACT.Square, scale=math.sqrt(SHIFT))
 
         def woven_view(ap):
@@ -234,10 +234,10 @@ def tile_list_cortex_rates_kernel(tc, tab_words, tab_scales, offs, tab2_words, t
             nc.vector.tensor_tensor(y[n][:, slices, :], drive[:],
                                     floor[:, a, slices].unsqueeze(2).to_broadcast([P, count, width]), ALU.max)
 
-        def store_y(n):
+        def store_y(n, slices=slice(0, 4)):
             a = units[n][3]
             rows = out_0[PASS * a:PASS * (a + 1), image_columns(n)]
-            nc.sync.dma_start(rows.rearrange("(p t) j -> p t j", t=4), y[n][:])
+            nc.sync.dma_start(rows.rearrange("(p t) j -> p t j", t=4)[:, slices, :], y[n][:, slices, :])
 
         def quantise_y(n):
             a, cols = units[n][3], image_columns(n)
@@ -256,7 +256,14 @@ def tile_list_cortex_rates_kernel(tc, tab_words, tab_scales, offs, tab2_words, t
 
         for c in range(CHUNKS):
             curve(c)
-        respond(0, range(4))
+        for pair in range(2):
+            for n in range(2):
+                t = 2 * pair + n
+                nc.vector.scalar_tensor_tensor(inverses[0][pair][:, n, :], roots[0][pair][:, n, :], gain[:, t:t + 1],
+                                               roots[0][pair][:, n, :], ALU.mult, ALU.mult)
+        for pair in range(2):
+            nc.vector.scalar_tensor_tensor(h_sliced[0][:, 2 * pair:2 * pair + 2, :], inverses[0][pair][:], SHIFT,
+                                           squares[0][pair][:, :, 0:CHUNK], ALU.mult, ALU.mult)
         deal_v2(0)
         weave_h(0)
         deal_v2(1)
@@ -275,15 +282,18 @@ def tile_list_cortex_rates_kernel(tc, tab_words, tab_scales, offs, tab2_words, t
                 weave_y_on_scalar(n)
                 quantise_y(n)
             store_codes(slice(0, 2), slice(c * CHUNK, (c + 1) * CHUNK), nc.sync)
-        for n in (6, 7):
-            fire(n, 0)
-            fire(n, 1)
-            store_y(n)
+        fire(6, 0)
+        fire(6, 1)
+        store_y(6)
+        for bank in range(2):
+            fire(7, bank)
+            store_y(7, slice(2 * bank, 2 * bank + 2))
         weave_y_on_scalar(6)
         weave_y_on_vector(7)
         quantise_y(6)
+        store_codes(slice(0, 1), slice(3 * CHUNK, S), nc.scalar)
         quantise_y(7)
-        store_codes(slice(0, 2), slice(3 * CHUNK, S), nc.scalar)
+        store_codes(slice(1, 2), slice(3 * CHUNK, S), nc.scalar)
         for quad in range(4):
             queue = nc.sync if quad % 2 == 0 else nc.scalar
             queue.dma_start(out_2[:, 4 * quad:4 * quad + 4, :].rearrange("a n c -> n a c").bitcast(I32),

@@ -198,7 +198,7 @@ def tile_list_cortex_rates_kernel(tc, tab_words, tab_scales, offs, tab2_words, t
         h_scales = [held([P, w], U8, "h_scales%d" % c) for c, (j, w) in enumerate(pieces)]
         units = [(c, 0, CHUNK, a) for c in range(CHUNKS) for a in range(2)]
         y = [held([P, 4, unit[2]], F32, "y%d" % n) for n, unit in enumerate(units)]
-        y_woven = [held([P, 4 * unit[2]], BF16, "y_woven%d" % n) for n, unit in enumerate(units)]
+        y_woven = {}
         y_codes = held([P, 2, S], U32, "y_codes")
 
         def respond(c, slices):
@@ -248,10 +248,20 @@ def tile_list_cortex_rates_kernel(tc, tab_words, tab_scales, offs, tab2_words, t
             queue.dma_start(out_1[groups, :, cols, :].rearrange("a p m t -> p a (m t)").bitcast(I32),
                               y_codes[:, groups, cols].bitcast(I32))
 
+        def weave_h_on_scalar(c):
+            nc.scalar.copy(woven_view(h_woven[c][:]), sliced_view(h_sliced[c][:]))
+
+        def weave_y_on_gpsimd(n):
+            y_woven[n] = held([P, 4 * CHUNK], BF16, "y_woven%d" % n, tag="inverse2_1")
+            nc.gpsimd.tensor_scalar(y_woven[n][:].rearrange("p (m t) -> p m t", t=4), y[n][:].rearrange("p t m -> p m t"),
+                                    1.0, -0.0, ALU.mult, ALU.add)
+
         def weave_y_on_scalar(n):
+            y_woven[n] = held([P, 4 * CHUNK], BF16, "y_woven%d" % n)
             nc.scalar.activation(woven_view(y_woven[n][:]), sliced_view(y[n][:]), ACT.Copy)
 
         def weave_y_on_vector(n):
+            y_woven[n] = held([P, 4 * CHUNK], BF16, "y_woven%d" % n)
             nc.vector.tensor_copy(woven_view(y_woven[n][:]), sliced_view(y[n][:]))
 
         for c in range(CHUNKS):
@@ -268,20 +278,42 @@ def tile_list_cortex_rates_kernel(tc, tab_words, tab_scales, offs, tab2_words, t
         weave_h(0)
         deal_v2(1)
         quantise_h(0)
-        for c in range(CHUNKS - 1):
-            respond(c + 1, range(4))
-            fire(2 * c, 0)
-            weave_h(c + 1)
-            fire(2 * c, 1)
-            store_y(2 * c)
-            quantise_h(c + 1)
-            fire(2 * c + 1, 0)
-            fire(2 * c + 1, 1)
-            store_y(2 * c + 1)
+        respond(1, range(4))
+        fire(0, 0)
+        weave_h(1)
+        fire(0, 1)
+        store_y(0)
+        quantise_h(1)
+        fire(1, 0)
+        fire(1, 1)
+        store_y(1)
+
+        def fire_chunk(c):
             for n in (2 * c, 2 * c + 1):
-                weave_y_on_scalar(n)
-                quantise_y(n)
-            store_codes(slice(0, 2), slice(c * CHUNK, (c + 1) * CHUNK), nc.sync)
+                fire(n, 0)
+                fire(n, 1)
+                store_y(n)
+
+        respond(2, range(4))
+        weave_y_on_gpsimd(0)
+        weave_h_on_scalar(2)
+        fire_chunk(1)
+        weave_y_on_scalar(1)
+        quantise_h(2)
+        respond(3, range(4))
+        quantise_y(0)
+        weave_y_on_gpsimd(2)
+        weave_h_on_scalar(3)
+        fire_chunk(2)
+        weave_y_on_scalar(3)
+        quantise_h(3)
+        quantise_y(1)
+        store_codes(slice(0, 2), slice(0, CHUNK), nc.sync)
+        quantise_y(3)
+        quantise_y(2)
+        store_codes(slice(0, 2), slice(CHUNK, 2 * CHUNK), nc.sync)
+        weave_y_on_gpsimd(4)
+        weave_y_on_scalar(5)
         fire(6, 0)
         fire(6, 1)
         store_y(6)
@@ -289,7 +321,10 @@ def tile_list_cortex_rates_kernel(tc, tab_words, tab_scales, offs, tab2_words, t
             fire(7, bank)
             store_y(7, slice(2 * bank, 2 * bank + 2))
         weave_y_on_scalar(6)
+        quantise_y(4)
         weave_y_on_vector(7)
+        quantise_y(5)
+        store_codes(slice(0, 2), slice(2 * CHUNK, 3 * CHUNK), nc.sync)
         quantise_y(6)
         store_codes(slice(0, 1), slice(3 * CHUNK, S), nc.scalar)
         quantise_y(7)

@@ -172,15 +172,23 @@ def tile_list_cortex_rates_kernel(tc, tab_words, tab_scales, offs, tab2_words, t
         roots = [[held([P, 2, w], F32, "root%d_%d" % (c, pair)) for pair in range(2)] for c, (j, w) in enumerate(pieces)]
         inverses = [[held([P, 2, w], F32, "inverse%d_%d" % (c, pair)) for pair in range(2)] for c, (j, w) in enumerate(pieces)]
 
+        first_square = held([P, 4, CHUNK], F32, "first_square")
+        first_inverse = held([P, 4, CHUNK], F32, "first_inverse")
+        shifted_gain = held([P, 4], F32, "shifted_gain")
+        nc.vector.tensor_scalar(shifted_gain[:], gain[:], SHIFT, None, ALU.mult)
+
         def curve(c):
             first, width = pieces[c]
             u, cols = first // PASS, slice(first % PASS, first % PASS + width)
             for pair in range(2):
+                if c == 0:
+                    for n in range(2):
+                        nc.scalar.activation(first_square[:, 2 * pair + n, :], banks[u][2 * pair + n][:, cols], ACT.Square)
+                    nc.scalar.activation(roots[c][pair][:], first_square[:, 2 * pair:2 * pair + 2, :],
+                                         ACT.Abs_reciprocal_sqrt, bias=SHIFT, scale=SHIFT)
+                    continue
                 for n in range(2):
-                    if u == 0:
-                        nc.scalar.activation(squares[u][pair][:, n, cols], banks[u][2 * pair + n][:, cols], ACT.Square)
-                    elif c % 2 == 0:
-                        nc.scalar.activation(squares[u][pair][:, n, :], banks[u][2 * pair + n][:], ACT.Square)
+                    nc.scalar.activation(squares[u][pair][:, n, cols], banks[u][2 * pair + n][:, cols], ACT.Square)
                 nc.scalar.activation(roots[c][pair][:], squares[u][pair][:, :, cols], ACT.Abs_reciprocal_sqrt,
                                      bias=SHIFT, scale=SHIFT)
             for pair in range(2 if c > 0 else 0):
@@ -248,13 +256,13 @@ def tile_list_cortex_rates_kernel(tc, tab_words, tab_scales, offs, tab2_words, t
             queue.dma_start(out_1[groups, :, cols, :].rearrange("a p m t -> p a (m t)").bitcast(I32),
                               y_codes[:, groups, cols].bitcast(I32))
 
-        def weave_h_on_scalar(c):
-            nc.scalar.copy(woven_view(h_woven[c][:]), sliced_view(h_sliced[c][:]))
+        def weave_on_gpsimd(woven, sliced):
+            nc.gpsimd.tensor_scalar(woven.rearrange("p (m t) -> p m t", t=4), sliced.rearrange("p t m -> p m t"),
+                                    1.0, -0.0, ALU.mult, ALU.add)
 
         def weave_y_on_gpsimd(n):
-            y_woven[n] = held([P, 4 * CHUNK], BF16, "y_woven%d" % n, tag="inverse2_1")
-            nc.gpsimd.tensor_scalar(y_woven[n][:].rearrange("p (m t) -> p m t", t=4), y[n][:].rearrange("p t m -> p m t"),
-                                    1.0, -0.0, ALU.mult, ALU.add)
+            y_woven[n] = held([P, 4 * CHUNK], BF16, "y_woven%d" % n, tag="y_woven2")
+            weave_on_gpsimd(y_woven[n][:], y[n][:])
 
         def weave_y_on_scalar(n):
             y_woven[n] = held([P, 4 * CHUNK], BF16, "y_woven%d" % n)
@@ -269,49 +277,30 @@ def tile_list_cortex_rates_kernel(tc, tab_words, tab_scales, offs, tab2_words, t
         for pair in range(2):
             for n in range(2):
                 t = 2 * pair + n
-                nc.vector.scalar_tensor_tensor(inverses[0][pair][:, n, :], roots[0][pair][:, n, :], gain[:, t:t + 1],
+                nc.vector.scalar_tensor_tensor(first_inverse[:, t, :], roots[0][pair][:, n, :], shifted_gain[:, t:t + 1],
                                                roots[0][pair][:, n, :], ALU.mult, ALU.mult)
-        for pair in range(2):
-            nc.vector.scalar_tensor_tensor(h_sliced[0][:, 2 * pair:2 * pair + 2, :], inverses[0][pair][:], SHIFT,
-                                           squares[0][pair][:, :, 0:CHUNK], ALU.mult, ALU.mult)
         deal_v2(0)
-        weave_h(0)
+        nc.vector.tensor_tensor(woven_view(h_woven[0][:]), sliced_view(first_inverse[:]), sliced_view(first_square[:]),
+                                ALU.mult)
         deal_v2(1)
         quantise_h(0)
-        respond(1, range(4))
-        fire(0, 0)
-        weave_h(1)
-        fire(0, 1)
-        store_y(0)
-        quantise_h(1)
-        fire(1, 0)
-        fire(1, 1)
-        store_y(1)
-
         def fire_chunk(c):
             for n in (2 * c, 2 * c + 1):
                 fire(n, 0)
                 fire(n, 1)
                 store_y(n)
 
-        respond(2, range(4))
-        weave_y_on_gpsimd(0)
-        weave_h_on_scalar(2)
-        fire_chunk(1)
-        weave_y_on_scalar(1)
-        quantise_h(2)
-        respond(3, range(4))
+        for c in range(CHUNKS - 1):
+            respond(c + 1, range(4))
+            weave_on_gpsimd(h_woven[c + 1][:], h_sliced[c + 1][:])
+            fire_chunk(c)
+            quantise_h(c + 1)
+        for n in range(4):
+            weave_y_on_scalar(n)
         quantise_y(0)
-        weave_y_on_gpsimd(2)
-        weave_h_on_scalar(3)
-        fire_chunk(2)
-        weave_y_on_scalar(3)
-        quantise_h(3)
         quantise_y(1)
         store_codes(slice(0, 2), slice(0, CHUNK), nc.sync)
-        quantise_y(3)
         quantise_y(2)
-        store_codes(slice(0, 2), slice(CHUNK, 2 * CHUNK), nc.sync)
         weave_y_on_gpsimd(4)
         weave_y_on_scalar(5)
         fire(6, 0)
@@ -321,8 +310,10 @@ def tile_list_cortex_rates_kernel(tc, tab_words, tab_scales, offs, tab2_words, t
             fire(7, bank)
             store_y(7, slice(2 * bank, 2 * bank + 2))
         weave_y_on_scalar(6)
-        quantise_y(4)
+        quantise_y(3)
+        store_codes(slice(0, 2), slice(CHUNK, 2 * CHUNK), nc.sync)
         weave_y_on_vector(7)
+        quantise_y(4)
         quantise_y(5)
         store_codes(slice(0, 2), slice(2 * CHUNK, 3 * CHUNK), nc.sync)
         quantise_y(6)

@@ -112,34 +112,37 @@ def tile_list_cortex_rates_kernel(tc, tab_words, tab_scales, offs, tab2_words, t
             nc.scalar.dma_start(v2_scales[32 * quad:32 * quad + 4, :].bitcast(I32),
                               v2_scale_dealt[4 * quad:4 * quad + 4, :].bitcast(I32))
 
-        banks = [[psum.tile([P, PASS], F32, name="bank", tag="bank") for t in range(4)] for u in range(2)]
+        banks = [[psum.tile([P, 2, CHUNK], F32, name="bank", tag="bank") for pair in range(2)] for c in range(CHUNKS)]
 
-        def stored_pass(a, u, t, start=False, stop=False):
-            cols = slice(PASS * u, PASS * (u + 1))
-            nc.tensor.matmul_mx(out=banks[u][t][:], lhsT=w4_dealt[:, a, 2 * P * t:2 * P * (t + 1)].bitcast(FP4X4),
+        def stored_pass(a, c, t, start=False, stop=False):
+            cols = slice(CHUNK * c, CHUNK * (c + 1))
+            nc.tensor.matmul_mx(out=banks[c][t // 2][:, t % 2, :],
+                                lhsT=w4_dealt[:, a, 2 * P * t:2 * P * (t + 1)].bitcast(FP4X4),
                                 lhsT_scale=k_scales[:, a, S + P * t:S + P * (t + 1)],
                                 rhs=v_picked[a][:, cols].bitcast(FP8X4), rhs_scale=k_scales[:, a, cols],
                                 start=start, stop=stop)
 
-        def learned_pass(a, u, t, stop=False):
-            cols = slice(PASS * u, PASS * (u + 1))
-            nc.tensor.matmul_mx(out=banks[u][t][:], lhsT=w1_codes[a][:, P * t:P * (t + 1)].bitcast(FP8X4),
+        def learned_pass(a, c, t, stop=False):
+            cols = slice(CHUNK * c, CHUNK * (c + 1))
+            nc.tensor.matmul_mx(out=banks[c][t // 2][:, t % 2, :],
+                                lhsT=w1_codes[a][:, P * t:P * (t + 1)].bitcast(FP8X4),
                                 lhsT_scale=w1_scales[a][:, P * t:P * (t + 1)],
                                 rhs=v_picked[a][:, cols].bitcast(FP8X4), rhs_scale=k_scales[:, a, cols],
                                 start=False, stop=stop)
 
-        for u in range(2):
+        for c in range(CHUNKS):
             for t in range(4):
-                stored_pass(0, u, t, start=True)
-        for u in range(2):
+                stored_pass(0, c, t, start=(t % 2 == 0))
+        for c in range(CHUNKS):
             for t in range(4):
-                learned_pass(0, u, t)
+                learned_pass(0, c, t)
         v_picked.append(held([P, S], U32, "v_picked1", tag="w1_woven0"))
         for u in range(2):
             nc.vector.tensor_copy(v_picked[1][:, PASS * u:PASS * (u + 1)],
                                   v_table[1][:].bitcast(U32).indirect(images[:, 32 * u:32 * (u + 1)]))
-        for t in range(4):
-            stored_pass(1, 0, t)
+        for c in range(CHUNKS - 1):
+            for t in range(4):
+                stored_pass(1, c, t)
         nc.scalar.activation(w1_target(1)[:, 0:SCALAR_SHARE, :, 0:2], w1_source(1)[:, 0:SCALAR_SHARE, :, 0:2], ACT.Copy)
         nc.vector.tensor_copy(w1_target(1)[:, SCALAR_SHARE:P, :, 0:2], w1_source(1)[:, SCALAR_SHARE:P, :, 0:2])
         nc.scalar.activation(w1_target(1)[:, 0:SCALAR_SHARE, :, 2:4], w1_source(1)[:, 0:SCALAR_SHARE, :, 2:4], ACT.Copy)
@@ -149,11 +152,12 @@ def tile_list_cortex_rates_kernel(tc, tab_words, tab_scales, offs, tab2_words, t
                 nc.vector.tensor_copy(w1_target(1)[:, SCALAR_SHARE:P, :, 2:4], w1_source(1)[:, SCALAR_SHARE:P, :, 2:4])
             nc.vector.quantize_mx(out=w1_codes[1][:, cols].bitcast(FP8X4), scales=w1_scales[1][:, cols],
                                   in_=w1_woven[1][:, 8 * P * pair:8 * P * (pair + 1)])
+        for c in range(CHUNKS - 1):
+            for t in range(4):
+                learned_pass(1, c, t, stop=(t % 2 == 1))
         for t in range(4):
-            learned_pass(1, 0, t, stop=True)
-        for t in range(4):
-            learned_pass(1, 1, t)
-            stored_pass(1, 1, t, stop=True)
+            learned_pass(1, CHUNKS - 1, t)
+            stored_pass(1, CHUNKS - 1, t, stop=(t % 2 == 1))
 
         v2_picked = held([P, S2], U32, "v2_picked", tag="w1_woven1")
         v2_dealt = held([P, S2], I32, "v2_dealt")
@@ -167,7 +171,7 @@ def tile_list_cortex_rates_kernel(tc, tab_words, tab_scales, offs, tab2_words, t
                                   v2_picked[:, cols].bitcast(I32).rearrange("p (m t) -> p m t", t=4))
 
         y_scales = held([P, 2, S], U8, "y_scales")
-        squares = [[held([P, 2, PASS], F32, "square%d_%d" % (u, pair)) for pair in range(2)] for u in range(2)]
+        squares = [[held([P, 2, CHUNK], F32, "square%d_%d" % (c, pair)) for pair in range(2)] for c in range(CHUNKS)]
         pieces = [(c * CHUNK, CHUNK) for c in range(CHUNKS)]
         roots = [[held([P, 2, w], F32, "root%d_%d" % (c, pair)) for pair in range(2)] for c, (j, w) in enumerate(pieces)]
         inverses = [[held([P, 2, w], F32, "inverse%d_%d" % (c, pair)) for pair in range(2)] for c, (j, w) in enumerate(pieces)]
@@ -178,19 +182,11 @@ def tile_list_cortex_rates_kernel(tc, tab_words, tab_scales, offs, tab2_words, t
         nc.vector.tensor_scalar(shifted_gain[:], gain[:], SHIFT, None, ALU.mult)
 
         def curve(c):
-            first, width = pieces[c]
-            u, cols = first // PASS, slice(first % PASS, first % PASS + width)
+            square = [first_square[:, 2 * pair:2 * pair + 2, :] if c == 0 else squares[c][pair][:] for pair in range(2)]
             for pair in range(2):
-                if c == 0:
-                    for n in range(2):
-                        nc.scalar.activation(first_square[:, 2 * pair + n, :], banks[u][2 * pair + n][:, cols], ACT.Square)
-                    nc.scalar.activation(roots[c][pair][:], first_square[:, 2 * pair:2 * pair + 2, :],
-                                         ACT.Abs_reciprocal_sqrt, bias=SHIFT, scale=SHIFT)
-                    continue
-                for n in range(2):
-                    nc.scalar.activation(squares[u][pair][:, n, cols], banks[u][2 * pair + n][:, cols], ACT.Square)
-                nc.scalar.activation(roots[c][pair][:], squares[u][pair][:, :, cols], ACT.Abs_reciprocal_sqrt,
-                                     bias=SHIFT, scale=SHIFT)
+                nc.scalar.activation(square[pair], banks[c][pair][:], ACT.Square)
+            for pair in range(2):
+                nc.scalar.activation(roots[c][pair][:], square[pair], ACT.Abs_reciprocal_sqrt, bias=SHIFT, scale=SHIFT)
             for pair in range(2 if c > 0 else 0):
                 nc.scalar.activation(inverses[c][pair][:], roots[c][pair][:], ACT.Square, scale=math.sqrt(SHIFT))
 
@@ -210,10 +206,8 @@ def tile_list_cortex_rates_kernel(tc, tab_words, tab_scales, offs, tab2_words, t
         y_codes = held([P, 2, S], U32, "y_codes")
 
         def respond(c, slices):
-            first, width = pieces[c]
-            u, cols = first // PASS, slice(first % PASS, first % PASS + width)
             for t in slices:
-                nc.vector.scalar_tensor_tensor(h_sliced[c][:, t, :], squares[u][t // 2][:, t % 2, cols],
+                nc.vector.scalar_tensor_tensor(h_sliced[c][:, t, :], squares[c][t // 2][:, t % 2, :],
                                                gain[:, t:t + 1], inverses[c][t // 2][:, t % 2, :],
                                                ALU.mult, ALU.mult)
 
@@ -299,8 +293,9 @@ def tile_list_cortex_rates_kernel(tc, tab_words, tab_scales, offs, tab2_words, t
             weave_y_on_scalar(n)
         quantise_y(0)
         quantise_y(1)
-        store_codes(slice(0, 2), slice(0, CHUNK), nc.sync)
+        quantise_y(3)
         quantise_y(2)
+        store_codes(slice(0, 2), slice(0, PASS), nc.sync)
         weave_y_on_gpsimd(4)
         weave_y_on_scalar(5)
         fire(6, 0)
@@ -310,16 +305,13 @@ def tile_list_cortex_rates_kernel(tc, tab_words, tab_scales, offs, tab2_words, t
             fire(7, bank)
             store_y(7, slice(2 * bank, 2 * bank + 2))
         weave_y_on_scalar(6)
-        quantise_y(3)
-        store_codes(slice(0, 2), slice(CHUNK, 2 * CHUNK), nc.sync)
-        weave_y_on_vector(7)
         quantise_y(4)
-        quantise_y(5)
-        store_codes(slice(0, 2), slice(2 * CHUNK, 3 * CHUNK), nc.sync)
+        weave_y_on_vector(7)
         quantise_y(6)
-        store_codes(slice(0, 1), slice(3 * CHUNK, S), nc.scalar)
+        store_codes(slice(0, 1), slice(PASS, S), nc.scalar)
+        quantise_y(5)
         quantise_y(7)
-        store_codes(slice(1, 2), slice(3 * CHUNK, S), nc.scalar)
+        store_codes(slice(1, 2), slice(PASS, S), nc.scalar)
         for quad in range(4):
             queue = nc.sync if quad % 2 == 0 else nc.scalar
             queue.dma_start(out_2[:, 4 * quad:4 * quad + 4, :].rearrange("a n c -> n a c").bitcast(I32),

@@ -19,8 +19,9 @@ P = 128
 PASS = 512
 CHUNK = 256
 CHUNKS = S // CHUNK
+UNITS = 2 * CHUNKS
 SHIFT = 1.375
-SCALAR_SHARE = 44
+SCALAR_SHARE = 20
 FLOPS = 2 * (2 * K * H * S + H * S * S2)
 
 
@@ -44,7 +45,8 @@ def tile_list_cortex_rates_kernel(tc, tab_words, tab_scales, offs, tab2_words, t
         w4_raw = held([P, 2, 2 * H], U8, "w4_raw")
         v_table = [held([P, T], I32, "v_table%d" % a) for a in range(2)]
         v2_table = held([P, T2], I32, "v2_table")
-        w1_raw = [held([P, 4, H], F32, "w1_raw%d" % a) for a in range(2)]
+        w1_raw = held([P, 4, H], F32, "w1_raw0")
+        w1_late = [held([P, 4, H // 2], F32, "w1_late%d" % half) for half in range(2)]
         gain = held([P, 4], F32, "gain")
         floor = held([P, 2, 4], F32, "floor")
         warm = held([P, 2], F32, "warm")
@@ -66,9 +68,11 @@ def tile_list_cortex_rates_kernel(tc, tab_words, tab_scales, offs, tab2_words, t
         nc.sync.dma_start(v_table[0][:], tab_words[0].rearrange("p t i -> p (t i)").bitcast(I32))
         nc.sync.dma_start(neurons[:], offs2)
         nc.sync.dma_start(v2_scale_rows[0:16, :].bitcast(I32), tab2_scales[0].bitcast(I32))
-        nc.sync.dma_start(w1_raw[0][:], w1[0:PASS, :].rearrange("(p j) c -> p j c", j=4))
+        nc.sync.dma_start(w1_raw[:], w1[0:PASS, :].rearrange("(p j) c -> p j c", j=4))
         nc.sync.dma_start(v_table[1][:], tab_words[1].rearrange("p t i -> p (t i)").bitcast(I32))
-        nc.sync.dma_start(w1_raw[1][:], w1[PASS:K, :].rearrange("(p j) c -> p j c", j=4))
+        for half in range(2):
+            nc.sync.dma_start(w1_late[half][:],
+                              w1[PASS:K, H // 2 * half:H // 2 * (half + 1)].rearrange("(p j) c -> p j c", j=4))
         nc.sync.dma_start(v2_table[:], tab2_words[0].rearrange("p t i -> p (t i)").bitcast(I32))
         nc.scalar.dma_start(gain[:], g.rearrange("(p t) -> p t", t=4))
         nc.scalar.dma_start(floor[:], base.rearrange("(a p t) -> p a t", a=2, t=4))
@@ -98,10 +102,10 @@ def tile_list_cortex_rates_kernel(tc, tab_words, tab_scales, offs, tab2_words, t
         def w1_target(a):
             return w1_woven[a][:].rearrange("p (t m j) -> p m j t", t=4, j=4)
 
-        def w1_source(a):
-            return w1_raw[a][:].rearrange("p j (m t) -> p m j t", t=4)
+        def w1_source(raw):
+            return raw[:].rearrange("p j (m t) -> p m j t", t=4)
 
-        nc.scalar.activation(w1_target(0), w1_source(0), ACT.Copy)
+        nc.scalar.activation(w1_target(0), w1_source(w1_raw), ACT.Copy)
         v2_scale_picked = held([P, S2], U8, "v2_scale_picked")
         nc.vector.tensor_copy(v2_scale_picked[:], v2_scale_rows[:].indirect(neurons[:]))
         nc.vector.quantize_mx(out=w1_codes[0][:].bitcast(FP8X4), scales=w1_scales[0][:], in_=w1_woven[0][:])
@@ -143,13 +147,14 @@ def tile_list_cortex_rates_kernel(tc, tab_words, tab_scales, offs, tab2_words, t
         for c in range(CHUNKS - 1):
             for t in range(4):
                 stored_pass(1, c, t)
-        nc.scalar.activation(w1_target(1)[:, 0:SCALAR_SHARE, :, 0:2], w1_source(1)[:, 0:SCALAR_SHARE, :, 0:2], ACT.Copy)
-        nc.vector.tensor_copy(w1_target(1)[:, SCALAR_SHARE:P, :, 0:2], w1_source(1)[:, SCALAR_SHARE:P, :, 0:2])
-        nc.scalar.activation(w1_target(1)[:, 0:SCALAR_SHARE, :, 2:4], w1_source(1)[:, 0:SCALAR_SHARE, :, 2:4], ACT.Copy)
+        nc.scalar.activation(w1_target(1)[:, 0:P // 2], w1_source(w1_late[0]), ACT.Copy)
+        last_target, last_source = w1_target(1)[:, P // 2:P], w1_source(w1_late[1])
+        for pair in range(2):
+            slices = slice(2 * pair, 2 * pair + 2)
+            nc.scalar.activation(last_target[:, 0:SCALAR_SHARE, :, slices], last_source[:, 0:SCALAR_SHARE, :, slices], ACT.Copy)
+            nc.vector.tensor_copy(last_target[:, SCALAR_SHARE:, :, slices], last_source[:, SCALAR_SHARE:, :, slices])
         for pair in range(2):
             cols = slice(2 * P * pair, 2 * P * (pair + 1))
-            if pair == 1:
-                nc.vector.tensor_copy(w1_target(1)[:, SCALAR_SHARE:P, :, 2:4], w1_source(1)[:, SCALAR_SHARE:P, :, 2:4])
             nc.vector.quantize_mx(out=w1_codes[1][:, cols].bitcast(FP8X4), scales=w1_scales[1][:, cols],
                                   in_=w1_woven[1][:, 8 * P * pair:8 * P * (pair + 1)])
         for c in range(CHUNKS - 1):
@@ -170,25 +175,21 @@ def tile_list_cortex_rates_kernel(tc, tab_words, tab_scales, offs, tab2_words, t
             nc.vector.tensor_copy(v2_dealt[:, cols].rearrange("p (t m) -> p m t", t=4),
                                   v2_picked[:, cols].bitcast(I32).rearrange("p (m t) -> p m t", t=4))
 
-        y_scales = held([P, 2, S], U8, "y_scales")
-        squares = [[held([P, 2, CHUNK], F32, "square%d_%d" % (c, pair)) for pair in range(2)] for c in range(CHUNKS)]
-        pieces = [(c * CHUNK, CHUNK) for c in range(CHUNKS)]
-        roots = [[held([P, 2, w], F32, "root%d_%d" % (c, pair)) for pair in range(2)] for c, (j, w) in enumerate(pieces)]
-        inverses = [[held([P, 2, w], F32, "inverse%d_%d" % (c, pair)) for pair in range(2)] for c, (j, w) in enumerate(pieces)]
+        def pair_tiles(name, c):
+            return [held([P, 2, CHUNK], F32, "%s%d_%d" % (name, c, pair))[:] for pair in range(2)]
 
         first_square = held([P, 4, CHUNK], F32, "first_square")
-        first_inverse = held([P, 4, CHUNK], F32, "first_inverse")
-        shifted_gain = held([P, 4], F32, "shifted_gain")
-        nc.vector.tensor_scalar(shifted_gain[:], gain[:], SHIFT, None, ALU.mult)
-
-        def curve(c):
-            square = [first_square[:, 2 * pair:2 * pair + 2, :] if c == 0 else squares[c][pair][:] for pair in range(2)]
+        squares = [[first_square[:, 0:2, :], first_square[:, 2:4, :]]] + [pair_tiles("square", c) for c in range(1, CHUNKS)]
+        roots = [pair_tiles("root", c) for c in range(CHUNKS)]
+        inverses = {c: pair_tiles("inverse", c) for c in range(1, CHUNKS)}
+        for c in range(CHUNKS):
             for pair in range(2):
-                nc.scalar.activation(square[pair], banks[c][pair][:], ACT.Square)
+                nc.scalar.activation(squares[c][pair], banks[c][pair][:], ACT.Square)
             for pair in range(2):
-                nc.scalar.activation(roots[c][pair][:], square[pair], ACT.Abs_reciprocal_sqrt, bias=SHIFT, scale=SHIFT)
-            for pair in range(2 if c > 0 else 0):
-                nc.scalar.activation(inverses[c][pair][:], roots[c][pair][:], ACT.Square, scale=math.sqrt(SHIFT))
+                nc.scalar.activation(roots[c][pair], squares[c][pair], ACT.Abs_reciprocal_sqrt, bias=SHIFT, scale=SHIFT)
+            if c in inverses:
+                for pair in range(2):
+                    nc.scalar.activation(inverses[c][pair], roots[c][pair], ACT.Square, scale=math.sqrt(SHIFT))
 
         def woven_view(ap):
             return ap.rearrange("p (c i t) -> p c t i", i=4, t=4)
@@ -196,117 +197,98 @@ def tile_list_cortex_rates_kernel(tc, tab_words, tab_scales, offs, tab2_words, t
         def sliced_view(ap):
             return ap.rearrange("p t (c i) -> p c t i", i=4)
 
-        h_sliced = [held([P, 4, w], BF16, "h_sliced%d" % c) for c, (j, w) in enumerate(pieces)]
-        h_woven = [held([P, 4 * w], BF16, "h_woven%d" % c) for c, (j, w) in enumerate(pieces)]
-        h_codes = [held([P, w], U32, "h_codes%d" % c) for c, (j, w) in enumerate(pieces)]
-        h_scales = [held([P, w], U8, "h_scales%d" % c) for c, (j, w) in enumerate(pieces)]
-        units = [(c, 0, CHUNK, a) for c in range(CHUNKS) for a in range(2)]
-        y = [held([P, 4, unit[2]], F32, "y%d" % n) for n, unit in enumerate(units)]
-        y_woven = {}
-        y_codes = held([P, 2, S], U32, "y_codes")
-
-        def respond(c, slices):
-            for t in slices:
-                nc.vector.scalar_tensor_tensor(h_sliced[c][:, t, :], squares[c][t // 2][:, t % 2, :],
-                                               gain[:, t:t + 1], inverses[c][t // 2][:, t % 2, :],
-                                               ALU.mult, ALU.mult)
-
-        def weave_h(c):
-            nc.vector.tensor_copy(woven_view(h_woven[c][:]), sliced_view(h_sliced[c][:]))
-
-        def quantise_h(c):
-            nc.vector.quantize_mx(out=h_codes[c][:].bitcast(FP8X4), scales=h_scales[c][:], in_=h_woven[c][:])
-
-        def image_columns(n):
-            c, start, width, a = units[n]
-            return slice(pieces[c][0] + start, pieces[c][0] + start + width)
-
-        def fire(n, bank):
-            c, start, width, a = units[n]
-            count = PASS // width
-            drive = psum.tile([P, count, width], F32, name="drive", tag="bank")
-            for i in range(count):
-                t = count * bank + i
-                cols = slice(PASS * a + P * t, PASS * a + P * (t + 1))
-                nc.tensor.matmul_mx(out=drive[:, i, :], lhsT=v2_dealt[:, cols].bitcast(FP8X4),
-                                    lhsT_scale=v2_scales[:, cols],
-                                    rhs=h_codes[c][:, start:start + width].bitcast(FP8X4),
-                                    rhs_scale=h_scales[c][:, start:start + width], start=True, stop=True)
-            slices = slice(count * bank, count * (bank + 1))
-            nc.vector.tensor_tensor(y[n][:, slices, :], drive[:],
-                                    floor[:, a, slices].unsqueeze(2).to_broadcast([P, count, width]), ALU.max)
-
-        def store_y(n, slices=slice(0, 4)):
-            a = units[n][3]
-            rows = out_0[PASS * a:PASS * (a + 1), image_columns(n)]
-            nc.sync.dma_start(rows.rearrange("(p t) j -> p t j", t=4)[:, slices, :], y[n][:, slices, :])
-
-        def quantise_y(n):
-            a, cols = units[n][3], image_columns(n)
-            nc.vector.quantize_mx(out=y_codes[:, a, cols].bitcast(FP8X4), scales=y_scales[:, a, cols],
-                                  in_=y_woven[n][:])
-
-        def store_codes(groups, cols, queue):
-            queue.dma_start(out_1[groups, :, cols, :].rearrange("a p m t -> p a (m t)").bitcast(I32),
-                              y_codes[:, groups, cols].bitcast(I32))
-
         def weave_on_gpsimd(woven, sliced):
             nc.gpsimd.tensor_scalar(woven.rearrange("p (m t) -> p m t", t=4), sliced.rearrange("p t m -> p m t"),
                                     1.0, -0.0, ALU.mult, ALU.add)
 
-        def weave_y_on_gpsimd(n):
-            y_woven[n] = held([P, 4 * CHUNK], BF16, "y_woven%d" % n, tag="y_woven2")
-            weave_on_gpsimd(y_woven[n][:], y[n][:])
+        h_woven = [held([P, 4 * CHUNK], BF16, "h_woven%d" % c) for c in range(CHUNKS)]
+        h_codes = [held([P, CHUNK], U32, "h_codes%d" % c) for c in range(CHUNKS)]
+        h_scales = [held([P, CHUNK], U8, "h_scales%d" % c) for c in range(CHUNKS)]
 
-        def weave_y_on_scalar(n):
-            y_woven[n] = held([P, 4 * CHUNK], BF16, "y_woven%d" % n)
-            nc.scalar.activation(woven_view(y_woven[n][:]), sliced_view(y[n][:]), ACT.Copy)
+        def quantise_h(c):
+            nc.vector.quantize_mx(out=h_codes[c][:].bitcast(FP8X4), scales=h_scales[c][:], in_=h_woven[c][:])
 
-        def weave_y_on_vector(n):
-            y_woven[n] = held([P, 4 * CHUNK], BF16, "y_woven%d" % n)
-            nc.vector.tensor_copy(woven_view(y_woven[n][:]), sliced_view(y[n][:]))
-
-        for c in range(CHUNKS):
-            curve(c)
-        for pair in range(2):
-            for n in range(2):
-                t = 2 * pair + n
-                nc.vector.scalar_tensor_tensor(first_inverse[:, t, :], roots[0][pair][:, n, :], shifted_gain[:, t:t + 1],
-                                               roots[0][pair][:, n, :], ALU.mult, ALU.mult)
+        shifted_gain = held([P, 4], F32, "shifted_gain")
+        first_inverse = held([P, 4, CHUNK], F32, "first_inverse")
+        nc.vector.tensor_scalar(shifted_gain[:], gain[:], SHIFT, None, ALU.mult)
+        for t in range(4):
+            root = roots[0][t // 2][:, t % 2, :]
+            nc.vector.scalar_tensor_tensor(first_inverse[:, t, :], root, shifted_gain[:, t:t + 1], root, ALU.mult, ALU.mult)
         deal_v2(0)
         nc.vector.tensor_tensor(woven_view(h_woven[0][:]), sliced_view(first_inverse[:]), sliced_view(first_square[:]),
                                 ALU.mult)
         deal_v2(1)
         quantise_h(0)
-        def fire_chunk(c):
-            for n in (2 * c, 2 * c + 1):
-                fire(n, 0)
-                fire(n, 1)
-                store_y(n)
+
+        def respond(c):
+            h_sliced = held([P, 4, CHUNK], BF16, "h_sliced%d" % c)
+            for t in range(4):
+                nc.vector.scalar_tensor_tensor(h_sliced[:, t, :], squares[c][t // 2][:, t % 2, :], gain[:, t:t + 1],
+                                               inverses[c][t // 2][:, t % 2, :], ALU.mult, ALU.mult)
+            weave_on_gpsimd(h_woven[c][:], h_sliced[:])
+
+        y = [held([P, 4, CHUNK], F32, "y%d" % n) for n in range(UNITS)]
+        y_woven = {}
+        y_codes = held([P, 2, S], U32, "y_codes")
+        y_scales = held([P, 2, S], U8, "y_scales")
+
+        def store_y(n, slices):
+            rows = out_0[PASS * (n % 2):PASS * (n % 2 + 1), CHUNK * (n // 2):CHUNK * (n // 2 + 1)]
+            nc.sync.dma_start(rows.rearrange("(p t) j -> p t j", t=4)[:, slices, :], y[n][:, slices, :])
+
+        def fire(c):
+            for a in range(2):
+                n = 2 * c + a
+                for pair in range(2):
+                    drive = psum.tile([P, 2, CHUNK], F32, name="drive", tag="bank")
+                    for i in range(2):
+                        cols = slice(PASS * a + P * (2 * pair + i), PASS * a + P * (2 * pair + i + 1))
+                        nc.tensor.matmul_mx(out=drive[:, i, :], lhsT=v2_dealt[:, cols].bitcast(FP8X4),
+                                            lhsT_scale=v2_scales[:, cols], rhs=h_codes[c][:].bitcast(FP8X4),
+                                            rhs_scale=h_scales[c][:], start=True, stop=True)
+                    slices = slice(2 * pair, 2 * pair + 2)
+                    nc.vector.tensor_tensor(y[n][:, slices, :], drive[:],
+                                            floor[:, a, slices].unsqueeze(2).to_broadcast([P, 2, CHUNK]), ALU.max)
+                    if c >= 2:
+                        store_y(n, slices)
+                if c < 2:
+                    store_y(n, slice(0, 4))
+
+        def woven_y(n, tag=None):
+            y_woven[n] = held([P, 4 * CHUNK], BF16, "y_woven%d" % n, tag=tag)
+            return y_woven[n][:]
+
+        def weave_y_on_scalar(n):
+            nc.scalar.activation(woven_view(woven_y(n)), sliced_view(y[n][:]), ACT.Copy)
+
+        def quantise_y(n):
+            a, cols = n % 2, slice(CHUNK * (n // 2), CHUNK * (n // 2 + 1))
+            nc.vector.quantize_mx(out=y_codes[:, a, cols].bitcast(FP8X4), scales=y_scales[:, a, cols],
+                                  in_=y_woven[n][:])
+
+        def store_codes(groups, cols, queue):
+            queue.dma_start(out_1[groups, :, cols, :].rearrange("a p m t -> p a (m t)").bitcast(I32),
+                            y_codes[:, groups, cols].bitcast(I32))
 
         for c in range(CHUNKS - 1):
-            respond(c + 1, range(4))
-            weave_on_gpsimd(h_woven[c + 1][:], h_sliced[c + 1][:])
-            fire_chunk(c)
+            respond(c + 1)
+            fire(c)
             quantise_h(c + 1)
-        for n in range(4):
-            weave_y_on_scalar(n)
-        quantise_y(0)
-        quantise_y(1)
-        quantise_y(3)
-        quantise_y(2)
-        store_codes(slice(0, 2), slice(0, PASS), nc.sync)
-        weave_y_on_gpsimd(4)
+        for a in range(2):
+            weave_y_on_scalar(a)
+            weave_y_on_scalar(2 + a)
+        for a in range(2):
+            quantise_y(a)
+            quantise_y(2 + a)
+            store_codes(slice(a, a + 1), slice(0, PASS), nc.sync)
+        weave_on_gpsimd(woven_y(4, tag="y_woven3"), y[4][:])
         weave_y_on_scalar(5)
-        fire(6, 0)
-        fire(6, 1)
-        store_y(6)
-        for bank in range(2):
-            fire(7, bank)
-            store_y(7, slice(2 * bank, 2 * bank + 2))
+        fire(CHUNKS - 1)
         weave_y_on_scalar(6)
         quantise_y(4)
-        weave_y_on_vector(7)
+        last_woven, last_sliced, half = woven_view(woven_y(7)), sliced_view(y[7][:]), CHUNK // 8
+        nc.vector.tensor_copy(last_woven[:, 0:half], last_sliced[:, 0:half])
+        nc.scalar.activation(last_woven[:, half:], last_sliced[:, half:], ACT.Copy)
         quantise_y(6)
         store_codes(slice(0, 1), slice(PASS, S), nc.scalar)
         quantise_y(5)

@@ -21,12 +21,12 @@ CHUNK = 256
 CHUNKS = S // CHUNK
 UNITS = 2 * CHUNKS
 SHIFT = 1.375
-SCALAR_SHARE = 20
+V2_ROW = 4
 FLOPS = 2 * (2 * K * H * S + H * S * S2)
 
 
 def tile_list_cortex_rates_kernel(tc, tab_words, tab_scales, offs, tab2_words, tab2_scales, offs2,
-                                           w4_words, w4_scales, w1, g, base, out_0, out_1, out_2):
+                                               w4_words, w4_scales, w1, g, base, out_0, out_1, out_2):
     nc = tc.nc
     with ExitStack() as ctx:
         keep = ctx.enter_context(tc.tile_pool(name="keep", bufs=1))
@@ -43,10 +43,8 @@ def tile_list_cortex_rates_kernel(tc, tab_words, tab_scales, offs, tab2_words, t
         v2_scales = held([P, S2], U8, "v2_scales")
         k_scales = held([P, 2, S + H], U8, "k_scales")
         w4_raw = held([P, 2, 2 * H], U8, "w4_raw")
-        v_table = [held([P, T], I32, "v_table%d" % a) for a in range(2)]
-        v2_table = held([P, T2], I32, "v2_table")
-        w1_raw = held([P, 4, H], F32, "w1_raw0")
-        w1_late = [held([P, 4, H // 2], F32, "w1_late%d" % half) for half in range(2)]
+        v_table = [held([P, T], I32, "v_table0")]
+        w1_raw = [held([P, 4, H], F32, "w1_raw0")]
         gain = held([P, 4], F32, "gain")
         floor = held([P, 2, 4], F32, "floor")
         warm = held([P, 2], F32, "warm")
@@ -61,21 +59,22 @@ def tile_list_cortex_rates_kernel(tc, tab_words, tab_scales, offs, tab2_words, t
         nc.gpsimd.memset(v2_scales[:].bitcast(I32), 0)
         nc.scalar.activation(warm[:, 1:2], warm[:, 0:1], ACT.Abs_reciprocal_sqrt)
 
+        def load_w1(a):
+            nc.sync.dma_start(w1_raw[a][:], w1[PASS * a:PASS * (a + 1), :].rearrange("(p j) c -> p j c", j=4))
+
+        def load_words(tile, words):
+            nc.sync.dma_start(tile[:], words.rearrange("p t i -> p (t i)").bitcast(I32))
+
         nc.sync.dma_start(images[:], offs)
         nc.sync.dma_start(v_scale_rows[0:32, :].bitcast(I32), tab_scales.rearrange("a q c -> q a c").bitcast(I32))
         nc.sync.dma_start(w4_scale_rows[0:32, :].bitcast(I32), w4_scales.rearrange("a q c -> q a c").bitcast(I32))
         nc.sync.dma_start(w4_raw[:].bitcast(I32), w4_words.rearrange("a p c -> p a c").bitcast(I32))
-        nc.sync.dma_start(v_table[0][:], tab_words[0].rearrange("p t i -> p (t i)").bitcast(I32))
         nc.sync.dma_start(neurons[:], offs2)
+        load_w1(0)
+        load_words(v_table[0], tab_words[0])
         nc.sync.dma_start(v2_scale_rows[0:16, :].bitcast(I32), tab2_scales[0].bitcast(I32))
-        nc.sync.dma_start(w1_raw[:], w1[0:PASS, :].rearrange("(p j) c -> p j c", j=4))
-        nc.sync.dma_start(v_table[1][:], tab_words[1].rearrange("p t i -> p (t i)").bitcast(I32))
-        for half in range(2):
-            nc.sync.dma_start(w1_late[half][:],
-                              w1[PASS:K, H // 2 * half:H // 2 * (half + 1)].rearrange("(p j) c -> p j c", j=4))
-        nc.sync.dma_start(v2_table[:], tab2_words[0].rearrange("p t i -> p (t i)").bitcast(I32))
-        nc.scalar.dma_start(gain[:], g.rearrange("(p t) -> p t", t=4))
-        nc.scalar.dma_start(floor[:], base.rearrange("(a p t) -> p a t", a=2, t=4))
+        nc.gpsimd.dma_start(gain[:], g.rearrange("(p t) -> p t", t=4))
+        nc.gpsimd.dma_start(floor[:], base.rearrange("(a p t) -> p a t", a=2, t=4))
 
         v_scale_picked = held([P, S], U8, "v_scale_picked")
         staged = held([P, S + H], U8, "staged")
@@ -84,47 +83,60 @@ def tile_list_cortex_rates_kernel(tc, tab_words, tab_scales, offs, tab2_words, t
                               w4_scale_rows[:].rearrange("p (m t) -> p m t", t=4))
         nc.vector.tensor_copy(staged[:, 0:S].bitcast(I32), v_scale_picked[:].bitcast(I32))
         for quad in range(4):
-            nc.scalar.dma_start(k_scales[32 * quad:32 * quad + 4, :, :].bitcast(I32),
-                                staged[8 * quad:8 * quad + 8, :].bitcast(I32))
+            nc.sync.dma_start(k_scales[32 * quad:32 * quad + 4, :, :].bitcast(I32),
+                              staged[8 * quad:8 * quad + 8, :].bitcast(I32))
+        w1_raw.append(held([P, 4, H], F32, "w1_raw1", tag="v_scale_picked"))
+        load_w1(1)
         w4_dealt = held([P, 2, 2 * H], U8, "w4_dealt")
         nc.vector.tensor_copy(w4_dealt[:].bitcast(U16).rearrange("p a (t m) -> p a m t", t=4),
                               w4_raw[:].bitcast(U16).rearrange("p a (m t) -> p a m t", t=4))
-
-        v_picked = [held([P, S], U32, "v_picked0")]
-        for u in range(2):
-            nc.vector.tensor_copy(v_picked[0][:, PASS * u:PASS * (u + 1)],
-                                  v_table[0][:].bitcast(U32).indirect(images[:, 32 * u:32 * (u + 1)]))
+        v_table.append(held([P, T], I32, "v_table1", tag="w4_raw"))
+        load_words(v_table[1], tab_words[1])
 
         w1_woven = [held([P, 4 * H], BF16, "w1_woven%d" % a) for a in range(2)]
         w1_codes = [held([P, H], U32, "w1_codes%d" % a) for a in range(2)]
         w1_scales = [held([P, H], U8, "w1_scales%d" % a) for a in range(2)]
 
-        def w1_target(a):
-            return w1_woven[a][:].rearrange("p (t m j) -> p m j t", t=4, j=4)
+        def round_w1(a):
+            nc.scalar.activation(w1_woven[a][:].rearrange("p (t m j) -> p m j t", t=4, j=4),
+                                 w1_raw[a][:].rearrange("p j (m t) -> p m j t", t=4), ACT.Copy)
 
-        def w1_source(raw):
-            return raw[:].rearrange("p j (m t) -> p m j t", t=4)
+        def quantise_w1(a):
+            nc.vector.quantize_mx(out=w1_codes[a][:].bitcast(FP8X4), scales=w1_scales[a][:], in_=w1_woven[a][:])
 
-        nc.scalar.activation(w1_target(0), w1_source(w1_raw), ACT.Copy)
+        v_picked = [held([P, S], U32, "v_picked%d" % a) for a in range(2)]
+
+        def pick_images(a, lo, hi):
+            nc.vector.tensor_copy(v_picked[a][:, lo:hi],
+                                  v_table[a][:].bitcast(U32).indirect(images[:, lo // 16:hi // 16]))
+
+        round_w1(0)
+        quantise_w1(0)
+        for lo in (0, PASS):
+            pick_images(0, lo, lo + PASS)
+        v2_table = held([P, T2], I32, "v2_table", tag="v_table0")
+        load_words(v2_table, tab2_words[0])
+        round_w1(1)
         v2_scale_picked = held([P, S2], U8, "v2_scale_picked")
+        v2_scale_dealt = held([P, S2], U8, "v2_scale_dealt")
         nc.vector.tensor_copy(v2_scale_picked[:], v2_scale_rows[:].indirect(neurons[:]))
-        nc.vector.quantize_mx(out=w1_codes[0][:].bitcast(FP8X4), scales=w1_scales[0][:], in_=w1_woven[0][:])
-        v2_scale_dealt = held([P, S2], U8, "v2_scale_dealt", tag="w1_raw0")
+        quantise_w1(1)
         nc.vector.tensor_copy(v2_scale_dealt[:].rearrange("p (a t m) -> p a m t", a=2, t=4),
                               v2_scale_picked[:].rearrange("p (a m t) -> p a m t", a=2, t=4))
         for quad in range(4):
-            nc.scalar.dma_start(v2_scales[32 * quad:32 * quad + 4, :].bitcast(I32),
+            first = 32 * quad + V2_ROW
+            nc.sync.dma_start(v2_scales[first:first + 4, :].bitcast(I32),
                               v2_scale_dealt[4 * quad:4 * quad + 4, :].bitcast(I32))
 
         banks = [[psum.tile([P, 2, CHUNK], F32, name="bank", tag="bank") for pair in range(2)] for c in range(CHUNKS)]
 
-        def stored_pass(a, c, t, start=False, stop=False):
+        def stored_pass(a, c, t, start=False):
             cols = slice(CHUNK * c, CHUNK * (c + 1))
             nc.tensor.matmul_mx(out=banks[c][t // 2][:, t % 2, :],
                                 lhsT=w4_dealt[:, a, 2 * P * t:2 * P * (t + 1)].bitcast(FP4X4),
                                 lhsT_scale=k_scales[:, a, S + P * t:S + P * (t + 1)],
                                 rhs=v_picked[a][:, cols].bitcast(FP8X4), rhs_scale=k_scales[:, a, cols],
-                                start=start, stop=stop)
+                                start=start, stop=False)
 
         def learned_pass(a, c, t, stop=False):
             cols = slice(CHUNK * c, CHUNK * (c + 1))
@@ -137,34 +149,15 @@ def tile_list_cortex_rates_kernel(tc, tab_words, tab_scales, offs, tab2_words, t
         for c in range(CHUNKS):
             for t in range(4):
                 stored_pass(0, c, t, start=(t % 2 == 0))
+                learned_pass(0, c, t)
+        for lo, hi in ((0, CHUNK), (CHUNK, PASS), (PASS, S)):
+            pick_images(1, lo, hi)
         for c in range(CHUNKS):
             for t in range(4):
-                learned_pass(0, c, t)
-        v_picked.append(held([P, S], U32, "v_picked1", tag="w1_woven0"))
-        for u in range(2):
-            nc.vector.tensor_copy(v_picked[1][:, PASS * u:PASS * (u + 1)],
-                                  v_table[1][:].bitcast(U32).indirect(images[:, 32 * u:32 * (u + 1)]))
-        for c in range(CHUNKS - 1):
-            for t in range(4):
                 stored_pass(1, c, t)
-        nc.scalar.activation(w1_target(1)[:, 0:P // 2], w1_source(w1_late[0]), ACT.Copy)
-        last_target, last_source = w1_target(1)[:, P // 2:P], w1_source(w1_late[1])
-        for pair in range(2):
-            slices = slice(2 * pair, 2 * pair + 2)
-            nc.scalar.activation(last_target[:, 0:SCALAR_SHARE, :, slices], last_source[:, 0:SCALAR_SHARE, :, slices], ACT.Copy)
-            nc.vector.tensor_copy(last_target[:, SCALAR_SHARE:, :, slices], last_source[:, SCALAR_SHARE:, :, slices])
-        for pair in range(2):
-            cols = slice(2 * P * pair, 2 * P * (pair + 1))
-            nc.vector.quantize_mx(out=w1_codes[1][:, cols].bitcast(FP8X4), scales=w1_scales[1][:, cols],
-                                  in_=w1_woven[1][:, 8 * P * pair:8 * P * (pair + 1)])
-        for c in range(CHUNKS - 1):
-            for t in range(4):
                 learned_pass(1, c, t, stop=(t % 2 == 1))
-        for t in range(4):
-            learned_pass(1, CHUNKS - 1, t)
-            stored_pass(1, CHUNKS - 1, t, stop=(t % 2 == 1))
 
-        v2_picked = held([P, S2], U32, "v2_picked", tag="w1_woven1")
+        v2_picked = held([P, S2], U32, "v2_picked")
         v2_dealt = held([P, S2], I32, "v2_dealt")
         for a in range(2):
             nc.vector.tensor_copy(v2_picked[:, PASS * a:PASS * (a + 1)],
@@ -184,12 +177,12 @@ def tile_list_cortex_rates_kernel(tc, tab_words, tab_scales, offs, tab2_words, t
         inverses = {c: pair_tiles("inverse", c) for c in range(1, CHUNKS)}
         for c in range(CHUNKS):
             for pair in range(2):
-                nc.scalar.activation(squares[c][pair], banks[c][pair][:], ACT.Square)
+                nc.scalar.activation(squares[c][pair], banks[c][pair][:], ACT.Square, scale=math.sqrt(SHIFT))
             for pair in range(2):
-                nc.scalar.activation(roots[c][pair], squares[c][pair], ACT.Abs_reciprocal_sqrt, bias=SHIFT, scale=SHIFT)
+                nc.scalar.activation(roots[c][pair], squares[c][pair], ACT.Abs_reciprocal_sqrt, bias=SHIFT)
             if c in inverses:
                 for pair in range(2):
-                    nc.scalar.activation(inverses[c][pair], roots[c][pair], ACT.Square, scale=math.sqrt(SHIFT))
+                    nc.scalar.activation(inverses[c][pair], roots[c][pair], ACT.Square)
 
         def woven_view(ap):
             return ap.rearrange("p (c i t) -> p c t i", i=4, t=4)
@@ -208,12 +201,10 @@ def tile_list_cortex_rates_kernel(tc, tab_words, tab_scales, offs, tab2_words, t
         def quantise_h(c):
             nc.vector.quantize_mx(out=h_codes[c][:].bitcast(FP8X4), scales=h_scales[c][:], in_=h_woven[c][:])
 
-        shifted_gain = held([P, 4], F32, "shifted_gain")
         first_inverse = held([P, 4, CHUNK], F32, "first_inverse")
-        nc.vector.tensor_scalar(shifted_gain[:], gain[:], SHIFT, None, ALU.mult)
         for t in range(4):
             root = roots[0][t // 2][:, t % 2, :]
-            nc.vector.scalar_tensor_tensor(first_inverse[:, t, :], root, shifted_gain[:, t:t + 1], root, ALU.mult, ALU.mult)
+            nc.vector.scalar_tensor_tensor(first_inverse[:, t, :], root, gain[:, t:t + 1], root, ALU.mult, ALU.mult)
         deal_v2(0)
         nc.vector.tensor_tensor(woven_view(h_woven[0][:]), sliced_view(first_inverse[:]), sliced_view(first_square[:]),
                                 ALU.mult)
@@ -244,7 +235,7 @@ def tile_list_cortex_rates_kernel(tc, tab_words, tab_scales, offs, tab2_words, t
                     for i in range(2):
                         cols = slice(PASS * a + P * (2 * pair + i), PASS * a + P * (2 * pair + i + 1))
                         nc.tensor.matmul_mx(out=drive[:, i, :], lhsT=v2_dealt[:, cols].bitcast(FP8X4),
-                                            lhsT_scale=v2_scales[:, cols], rhs=h_codes[c][:].bitcast(FP8X4),
+                                            lhsT_scale=v2_scales[V2_ROW:P, cols], rhs=h_codes[c][:].bitcast(FP8X4),
                                             rhs_scale=h_scales[c][:], start=True, stop=True)
                     slices = slice(2 * pair, 2 * pair + 2)
                     nc.vector.tensor_tensor(y[n][:, slices, :], drive[:],

@@ -22,6 +22,7 @@ CHUNKS = S // CHUNK
 UNITS = 2 * CHUNKS
 SHIFT = 1.375
 V2_ROW = 4
+GPSIMD_SHARE = 96
 FLOPS = 2 * (2 * K * H * S + H * S * S2)
 
 
@@ -70,8 +71,8 @@ def tile_list_cortex_rates_kernel(tc, tab_words, tab_scales, offs, tab2_words, t
         nc.sync.dma_start(w4_scale_rows[0:32, :].bitcast(I32), w4_scales.rearrange("a q c -> q a c").bitcast(I32))
         nc.sync.dma_start(w4_raw[:].bitcast(I32), w4_words.rearrange("a p c -> p a c").bitcast(I32))
         nc.sync.dma_start(neurons[:], offs2)
-        load_w1(0)
         load_words(v_table[0], tab_words[0])
+        load_w1(0)
         nc.sync.dma_start(v2_scale_rows[0:16, :].bitcast(I32), tab2_scales[0].bitcast(I32))
         nc.gpsimd.dma_start(gain[:], g.rearrange("(p t) -> p t", t=4))
         nc.gpsimd.dma_start(floor[:], base.rearrange("(a p t) -> p a t", a=2, t=4))
@@ -110,11 +111,11 @@ def tile_list_cortex_rates_kernel(tc, tab_words, tab_scales, offs, tab2_words, t
             nc.vector.tensor_copy(v_picked[a][:, lo:hi],
                                   v_table[a][:].bitcast(U32).indirect(images[:, lo // 16:hi // 16]))
 
-        round_w1(0)
-        quantise_w1(0)
         for lo in (0, PASS):
             pick_images(0, lo, lo + PASS)
-        v2_table = held([P, T2], I32, "v2_table", tag="v_table0")
+        round_w1(0)
+        quantise_w1(0)
+        v2_table = held([P, T2], I32, "v2_table", tag="w1_raw0")
         load_words(v2_table, tab2_words[0])
         round_w1(1)
         v2_scale_picked = held([P, S2], U8, "v2_scale_picked")
@@ -146,13 +147,14 @@ def tile_list_cortex_rates_kernel(tc, tab_words, tab_scales, offs, tab2_words, t
                                 rhs=v_picked[a][:, cols].bitcast(FP8X4), rhs_scale=k_scales[:, a, cols],
                                 start=False, stop=stop)
 
-        for c in range(CHUNKS):
-            for t in range(4):
-                stored_pass(0, c, t, start=(t % 2 == 0))
-                learned_pass(0, c, t)
         for lo, hi in ((0, CHUNK), (CHUNK, PASS), (PASS, S)):
             pick_images(1, lo, hi)
         for c in range(CHUNKS):
+            for t in range(4):
+                stored_pass(0, c, t, start=(t % 2 == 0))
+        for c in range(CHUNKS):
+            for t in range(4):
+                learned_pass(0, c, t)
             for t in range(4):
                 stored_pass(1, c, t)
                 learned_pass(1, c, t, stop=(t % 2 == 1))
@@ -249,8 +251,11 @@ def tile_list_cortex_rates_kernel(tc, tab_words, tab_scales, offs, tab2_words, t
             y_woven[n] = held([P, 4 * CHUNK], BF16, "y_woven%d" % n, tag=tag)
             return y_woven[n][:]
 
-        def weave_y_on_scalar(n):
-            nc.scalar.activation(woven_view(woven_y(n)), sliced_view(y[n][:]), ACT.Copy)
+        def weave_y_on_scalar(n, lo=0):
+            nc.scalar.activation(woven_view(y_woven[n][:, 4 * lo:]), sliced_view(y[n][:, :, lo:]), ACT.Copy)
+
+        def weave_y_head_on_gpsimd(n):
+            weave_on_gpsimd(woven_y(n)[:, 0:4 * GPSIMD_SHARE], y[n][:, :, 0:GPSIMD_SHARE])
 
         def quantise_y(n):
             a, cols = n % 2, slice(CHUNK * (n // 2), CHUNK * (n // 2 + 1))
@@ -264,18 +269,22 @@ def tile_list_cortex_rates_kernel(tc, tab_words, tab_scales, offs, tab2_words, t
         for c in range(CHUNKS - 1):
             respond(c + 1)
             fire(c)
+            weave_y_head_on_gpsimd(2 * c)
             quantise_h(c + 1)
-        for a in range(2):
-            weave_y_on_scalar(a)
-            weave_y_on_scalar(2 + a)
+        for n in (0, 2):
+            weave_y_on_scalar(n, GPSIMD_SHARE)
+        for n in (1, 3):
+            woven_y(n)
+            weave_y_on_scalar(n)
         for a in range(2):
             quantise_y(a)
             quantise_y(2 + a)
             store_codes(slice(a, a + 1), slice(0, PASS), nc.sync)
-        weave_on_gpsimd(woven_y(4, tag="y_woven3"), y[4][:])
-        weave_y_on_scalar(5)
+        weave_on_gpsimd(woven_y(5, tag="y_woven3"), y[5][:])
+        weave_y_on_scalar(4, GPSIMD_SHARE)
         fire(CHUNKS - 1)
-        weave_y_on_scalar(6)
+        weave_y_head_on_gpsimd(6)
+        weave_y_on_scalar(6, GPSIMD_SHARE)
         quantise_y(4)
         last_woven, last_sliced, half = woven_view(woven_y(7)), sliced_view(y[7][:]), CHUNK // 8
         nc.vector.tensor_copy(last_woven[:, 0:half], last_sliced[:, 0:half])

@@ -22,7 +22,8 @@ CHUNKS = S // CHUNK
 UNITS = 2 * CHUNKS
 SHIFT = 1.375
 V2_ROW = 4
-GPSIMD_SHARE = 96
+HEAD = 64
+VECTOR_SHARE = 128
 FLOPS = 2 * (2 * K * H * S + H * S * S2)
 
 
@@ -220,18 +221,19 @@ def tile_list_cortex_rates_kernel(tc, tab_words, tab_scales, offs, tab2_words, t
                                                inverses[c][t // 2][:, t % 2, :], ALU.mult, ALU.mult)
             weave_on_gpsimd(h_woven[c][:], h_sliced[:])
 
-        y = [held([P, 4, CHUNK], F32, "y%d" % n) for n in range(UNITS)]
-        y_woven = {}
+        y = [[held([P, 4, PASS], F32, "y%d_%d" % (half, a)) for a in range(2)] for half in range(2)]
+        y_woven = [[held([P, 4 * PASS], BF16, "y_woven0_%d" % a) for a in range(2)],
+                   [held([P, 4 * PASS], BF16, "y_woven1_0")]]
         y_codes = held([P, 2, S], U32, "y_codes")
         y_scales = held([P, 2, S], U8, "y_scales")
 
-        def store_y(n, slices):
-            rows = out_0[PASS * (n % 2):PASS * (n % 2 + 1), CHUNK * (n // 2):CHUNK * (n // 2 + 1)]
-            nc.sync.dma_start(rows.rearrange("(p t) j -> p t j", t=4)[:, slices, :], y[n][:, slices, :])
+        def store_y(c, a, slices):
+            rows = out_0[PASS * a:PASS * (a + 1), CHUNK * c:CHUNK * (c + 1)]
+            cols = slice(CHUNK * (c % 2), CHUNK * (c % 2 + 1))
+            nc.sync.dma_start(rows.rearrange("(p t) j -> p t j", t=4)[:, slices, :], y[c // 2][a][:, slices, cols])
 
         def fire(c):
             for a in range(2):
-                n = 2 * c + a
                 for pair in range(2):
                     drive = psum.tile([P, 2, CHUNK], F32, name="drive", tag="bank")
                     for i in range(2):
@@ -240,60 +242,56 @@ def tile_list_cortex_rates_kernel(tc, tab_words, tab_scales, offs, tab2_words, t
                                             lhsT_scale=v2_scales[V2_ROW:P, cols], rhs=h_codes[c][:].bitcast(FP8X4),
                                             rhs_scale=h_scales[c][:], start=True, stop=True)
                     slices = slice(2 * pair, 2 * pair + 2)
-                    nc.vector.tensor_tensor(y[n][:, slices, :], drive[:],
+                    nc.vector.tensor_tensor(y[c // 2][a][:, slices, CHUNK * (c % 2):CHUNK * (c % 2 + 1)], drive[:],
                                             floor[:, a, slices].unsqueeze(2).to_broadcast([P, 2, CHUNK]), ALU.max)
                     if c >= 2:
-                        store_y(n, slices)
+                        store_y(c, a, slices)
                 if c < 2:
-                    store_y(n, slice(0, 4))
+                    store_y(c, a, slice(0, 4))
 
-        def woven_y(n, tag=None):
-            y_woven[n] = held([P, 4 * CHUNK], BF16, "y_woven%d" % n, tag=tag)
-            return y_woven[n][:]
+        def woven_part(half, a, lo, hi):
+            return y_woven[half][a][:, 4 * lo:4 * hi], y[half][a][:, :, lo:hi]
 
-        def weave_y_on_scalar(n, lo=0):
-            nc.scalar.activation(woven_view(y_woven[n][:, 4 * lo:]), sliced_view(y[n][:, :, lo:]), ACT.Copy)
+        def weave_y_on_scalar(half, a, lo, hi):
+            woven, sliced = woven_part(half, a, lo, hi)
+            nc.scalar.activation(woven_view(woven), sliced_view(sliced), ACT.Copy)
 
-        def weave_y_head_on_gpsimd(n):
-            weave_on_gpsimd(woven_y(n)[:, 0:4 * GPSIMD_SHARE], y[n][:, :, 0:GPSIMD_SHARE])
-
-        def quantise_y(n):
-            a, cols = n % 2, slice(CHUNK * (n // 2), CHUNK * (n // 2 + 1))
+        def quantise_y(half, a, lo, hi):
+            cols = slice(PASS * half + lo, PASS * half + hi)
             nc.vector.quantize_mx(out=y_codes[:, a, cols].bitcast(FP8X4), scales=y_scales[:, a, cols],
-                                  in_=y_woven[n][:])
+                                  in_=y_woven[half][a][:, 4 * lo:4 * hi])
 
         def store_codes(groups, cols, queue):
             queue.dma_start(out_1[groups, :, cols, :].rearrange("a p m t -> p a (m t)").bitcast(I32),
                             y_codes[:, groups, cols].bitcast(I32))
 
+        heads = [(0, 0, 0, HEAD), (0, 0, CHUNK, CHUNK + HEAD), (1, 0, 0, HEAD)]
         for c in range(CHUNKS - 1):
             respond(c + 1)
             fire(c)
-            weave_y_head_on_gpsimd(2 * c)
+            weave_on_gpsimd(*woven_part(*heads[c]))
             quantise_h(c + 1)
-        for n in (0, 2):
-            weave_y_on_scalar(n, GPSIMD_SHARE)
-        for n in (1, 3):
-            woven_y(n)
-            weave_y_on_scalar(n)
+        weave_y_on_scalar(0, 0, HEAD, CHUNK)
+        weave_y_on_scalar(0, 0, CHUNK + HEAD, PASS)
+        weave_y_on_scalar(0, 1, 0, PASS)
         for a in range(2):
-            quantise_y(a)
-            quantise_y(2 + a)
+            quantise_y(0, a, 0, PASS)
             store_codes(slice(a, a + 1), slice(0, PASS), nc.sync)
-        weave_on_gpsimd(woven_y(5, tag="y_woven3"), y[5][:])
-        weave_y_on_scalar(4, GPSIMD_SHARE)
+        y_woven[1].append(held([P, 4 * PASS], BF16, "y_woven1_1", tag="y_woven0_1"))
+        weave_on_gpsimd(*woven_part(1, 1, 0, CHUNK))
+        weave_y_on_scalar(1, 0, HEAD, CHUNK)
         fire(CHUNKS - 1)
-        weave_y_head_on_gpsimd(6)
-        weave_y_on_scalar(6, GPSIMD_SHARE)
-        quantise_y(4)
-        last_woven, last_sliced, half = woven_view(woven_y(7)), sliced_view(y[7][:]), CHUNK // 8
-        nc.vector.tensor_copy(last_woven[:, 0:half], last_sliced[:, 0:half])
-        nc.scalar.activation(last_woven[:, half:], last_sliced[:, half:], ACT.Copy)
-        quantise_y(6)
-        store_codes(slice(0, 1), slice(PASS, S), nc.scalar)
-        quantise_y(5)
-        quantise_y(7)
-        store_codes(slice(1, 2), slice(PASS, S), nc.scalar)
+        weave_on_gpsimd(*woven_part(1, 0, CHUNK, CHUNK + HEAD))
+        weave_y_on_scalar(1, 0, CHUNK + HEAD, PASS)
+        quantise_y(1, 0, 0, CHUNK)
+        woven, sliced = woven_part(1, 1, CHUNK, CHUNK + VECTOR_SHARE)
+        nc.vector.tensor_copy(woven_view(woven), sliced_view(sliced))
+        weave_y_on_scalar(1, 1, CHUNK + VECTOR_SHARE, PASS)
+        quantise_y(1, 1, 0, CHUNK)
+        store_codes(slice(0, 2), slice(PASS, PASS + CHUNK), nc.sync)
+        for a in range(2):
+            quantise_y(1, a, CHUNK, PASS)
+            store_codes(slice(a, a + 1), slice(PASS + CHUNK, S), nc.scalar if a else nc.sync)
         for quad in range(4):
             queue = nc.sync if quad % 2 == 0 else nc.scalar
             queue.dma_start(out_2[:, 4 * quad:4 * quad + 4, :].rearrange("a n c -> n a c").bitcast(I32),

@@ -32,7 +32,7 @@ def tile_list_cortex_rates_kernel(tc, tab_words, tab_scales, offs, tab2_words, t
     nc = tc.nc
     with ExitStack() as ctx:
         keep = ctx.enter_context(tc.tile_pool(name="keep", bufs=1))
-        psum = ctx.enter_context(tc.psum_pool(name="psum", bufs=8))
+        psum = ctx.enter_context(tc.psum_pool(name="psum", bufs=1))
 
         def held(shape, dtype, name, tag=None):
             return keep.tile(shape, dtype, name=name, tag=tag or name, align_bytes=64)
@@ -130,7 +130,7 @@ def tile_list_cortex_rates_kernel(tc, tab_words, tab_scales, offs, tab2_words, t
             nc.sync.dma_start(v2_scales[first:first + 4, :].bitcast(I32),
                               v2_scale_dealt[4 * quad:4 * quad + 4, :].bitcast(I32))
 
-        banks = [[psum.tile([P, 2, CHUNK], F32, name="bank", tag="bank") for pair in range(2)] for c in range(CHUNKS)]
+        banks = [[psum.tile([P, 2, CHUNK], F32, name="bank%d" % (2 * c + pair)) for pair in range(2)] for c in range(CHUNKS)]
 
         def stored_pass(a, c, t, start=False):
             cols = slice(CHUNK * c, CHUNK * (c + 1))
@@ -174,17 +174,18 @@ def tile_list_cortex_rates_kernel(tc, tab_words, tab_scales, offs, tab2_words, t
         def pair_tiles(name, c):
             return [held([P, 2, CHUNK], F32, "%s%d_%d" % (name, c, pair))[:] for pair in range(2)]
 
-        first_square = held([P, 4, CHUNK], F32, "first_square")
-        squares = [[first_square[:, 0:2, :], first_square[:, 2:4, :]]] + [pair_tiles("square", c) for c in range(1, CHUNKS)]
+        squares = [pair_tiles("square", c) for c in range(CHUNKS)]
         roots = [pair_tiles("root", c) for c in range(CHUNKS)]
-        inverses = {c: pair_tiles("inverse", c) for c in range(1, CHUNKS)}
+        inverses = [pair_tiles("inverse", c) for c in range(CHUNKS)]
         for c in range(CHUNKS):
             for pair in range(2):
                 nc.scalar.activation(squares[c][pair], banks[c][pair][:], ACT.Square, scale=math.sqrt(SHIFT))
             for pair in range(2):
                 nc.scalar.activation(roots[c][pair], squares[c][pair], ACT.Abs_reciprocal_sqrt, bias=SHIFT)
-            if c in inverses:
-                for pair in range(2):
+            for pair in range(2):
+                if (c, pair) == (0, 0):
+                    nc.gpsimd.tensor_tensor(inverses[c][pair], roots[c][pair], roots[c][pair], ALU.mult)
+                else:
                     nc.scalar.activation(inverses[c][pair], roots[c][pair], ACT.Square)
 
         def woven_view(ap):
@@ -204,24 +205,22 @@ def tile_list_cortex_rates_kernel(tc, tab_words, tab_scales, offs, tab2_words, t
         def quantise_h(c):
             nc.vector.quantize_mx(out=h_codes[c][:].bitcast(FP8X4), scales=h_scales[c][:], in_=h_woven[c][:])
 
-        first_inverse = held([P, 4, CHUNK], F32, "first_inverse")
-        for t in range(4):
-            root = roots[0][t // 2][:, t % 2, :]
-            nc.vector.scalar_tensor_tensor(first_inverse[:, t, :], root, gain[:, t:t + 1], root, ALU.mult, ALU.mult)
-        deal_v2(0)
-        nc.vector.tensor_tensor(woven_view(h_woven[0][:]), sliced_view(first_inverse[:]), sliced_view(first_square[:]),
-                                ALU.mult)
-        deal_v2(1)
-        quantise_h(0)
-
-        def respond(c):
-            h_sliced = held([P, 4, CHUNK], BF16, "h_sliced%d" % c)
+        def respond(c, tag=None):
+            h_sliced = held([P, 4, CHUNK], BF16, "h_sliced%d" % c, tag=tag)
             for t in range(4):
                 nc.vector.scalar_tensor_tensor(h_sliced[:, t, :], squares[c][t // 2][:, t % 2, :], gain[:, t:t + 1],
                                                inverses[c][t // 2][:, t % 2, :], ALU.mult, ALU.mult)
-            weave_on_gpsimd(h_woven[c][:], h_sliced[:])
+            return h_sliced[:]
 
-        y = [[held([P, 4, PASS], F32, "y%d_%d" % (half, a)) for a in range(2)] for half in range(2)]
+        first_sliced = respond(0)
+        deal_v2(0)
+        nc.vector.tensor_copy(woven_view(h_woven[0][:]), sliced_view(first_sliced))
+        deal_v2(1)
+        quantise_h(0)
+
+        y = [[held([P, 4, PASS], F32, "y%d_0" % half, tag="root%d_1" % (2 * half + 1)),
+              held([P, 4, PASS], F32, "y%d_1" % half)] for half in range(2)]
+        turns = [(0, 1, 2, 3), (6, 4, 5, 7)]
         y_woven = [[held([P, 4 * PASS], BF16, "y_woven0_%d" % a) for a in range(2)],
                    [held([P, 4 * PASS], BF16, "y_woven1_0")]]
         y_codes = held([P, 2, S], U32, "y_codes")
@@ -235,7 +234,7 @@ def tile_list_cortex_rates_kernel(tc, tab_words, tab_scales, offs, tab2_words, t
         def fire(c):
             for a in range(2):
                 for pair in range(2):
-                    drive = psum.tile([P, 2, CHUNK], F32, name="drive", tag="bank")
+                    drive = psum.tile([P, 2, CHUNK], F32, name="drive", tag="bank%d" % turns[c % 2][2 * a + pair])
                     for i in range(2):
                         cols = slice(PASS * a + P * (2 * pair + i), PASS * a + P * (2 * pair + i + 1))
                         nc.tensor.matmul_mx(out=drive[:, i, :], lhsT=v2_dealt[:, cols].bitcast(FP8X4),
@@ -267,7 +266,7 @@ def tile_list_cortex_rates_kernel(tc, tab_words, tab_scales, offs, tab2_words, t
 
         heads = [(0, 0, 0, HEAD), (0, 0, CHUNK, CHUNK + HEAD), (1, 0, 0, HEAD)]
         for c in range(CHUNKS - 1):
-            respond(c + 1)
+            weave_on_gpsimd(h_woven[c + 1][:], respond(c + 1, tag="h_sliced0" if c == 0 else None))
             fire(c)
             weave_on_gpsimd(*woven_part(*heads[c]))
             quantise_h(c + 1)

@@ -177,16 +177,34 @@ def tile_list_cortex_rates_kernel(tc, tab_words, tab_scales, offs, tab2_words, t
         squares = [pair_tiles("square", c) for c in range(CHUNKS)]
         roots = [pair_tiles("root", c) for c in range(CHUNKS)]
         inverses = [pair_tiles("inverse", c) for c in range(CHUNKS)]
-        for c in range(CHUNKS):
+
+        def square(c, pair, part=slice(0, 2)):
+            nc.scalar.activation(squares[c][pair][:, part, :], banks[c][pair][:, part, :], ACT.Square,
+                                 scale=math.sqrt(SHIFT))
+
+        def root(c, pair, part=slice(0, 2)):
+            nc.scalar.activation(roots[c][pair][:, part, :], squares[c][pair][:, part, :], ACT.Abs_reciprocal_sqrt,
+                                 bias=SHIFT)
+
+        def invert(c, pair):
+            nc.scalar.activation(inverses[c][pair], roots[c][pair], ACT.Square)
+
+        for step in (square, root):
+            for i in range(2):
+                step(0, 0, slice(i, i + 1))
+        nc.gpsimd.tensor_tensor(inverses[0][0], roots[0][0], roots[0][0], ALU.mult)
+        square(0, 1)
+        square(1, 0)
+        root(0, 1)
+        square(1, 1)
+        invert(0, 1)
+        for step in (root, invert):
             for pair in range(2):
-                nc.scalar.activation(squares[c][pair], banks[c][pair][:], ACT.Square, scale=math.sqrt(SHIFT))
-            for pair in range(2):
-                nc.scalar.activation(roots[c][pair], squares[c][pair], ACT.Abs_reciprocal_sqrt, bias=SHIFT)
-            for pair in range(2):
-                if (c, pair) == (0, 0):
-                    nc.gpsimd.tensor_tensor(inverses[c][pair], roots[c][pair], roots[c][pair], ALU.mult)
-                else:
-                    nc.scalar.activation(inverses[c][pair], roots[c][pair], ACT.Square)
+                step(1, pair)
+        for c in range(2, CHUNKS):
+            for step in (square, root, invert):
+                for pair in range(2):
+                    step(c, pair)
 
         def woven_view(ap):
             return ap.rearrange("p (c i t) -> p c t i", i=4, t=4)

@@ -24,6 +24,7 @@ SHIFT = 1.375
 V2_ROW = 4
 HEAD = 64
 VECTOR_SHARE = 128
+QUADS = (0, 2, 1, 3)
 FLOPS = 2 * (2 * K * H * S + H * S * S2)
 
 
@@ -84,7 +85,7 @@ def tile_list_cortex_rates_kernel(tc, tab_words, tab_scales, offs, tab2_words, t
         nc.vector.tensor_copy(staged[:, S:S + H].rearrange("p (t m) -> p m t", t=4),
                               w4_scale_rows[:].rearrange("p (m t) -> p m t", t=4))
         nc.vector.tensor_copy(staged[:, 0:S].bitcast(I32), v_scale_picked[:].bitcast(I32))
-        for quad in range(4):
+        for quad in QUADS:
             nc.sync.dma_start(k_scales[32 * quad:32 * quad + 4, :, :].bitcast(I32),
                               staged[8 * quad:8 * quad + 8, :].bitcast(I32))
         w1_raw.append(held([P, 4, H], F32, "w1_raw1", tag="v_scale_picked"))
@@ -125,7 +126,7 @@ def tile_list_cortex_rates_kernel(tc, tab_words, tab_scales, offs, tab2_words, t
         quantise_w1(1)
         nc.vector.tensor_copy(v2_scale_dealt[:].rearrange("p (a t m) -> p a m t", a=2, t=4),
                               v2_scale_picked[:].rearrange("p (a m t) -> p a m t", a=2, t=4))
-        for quad in range(4):
+        for quad in QUADS:
             first = 32 * quad + V2_ROW
             nc.sync.dma_start(v2_scales[first:first + 4, :].bitcast(I32),
                               v2_scale_dealt[4 * quad:4 * quad + 4, :].bitcast(I32))
@@ -309,7 +310,7 @@ def tile_list_cortex_rates_kernel(tc, tab_words, tab_scales, offs, tab2_words, t
         for a in range(2):
             quantise_y(1, a, CHUNK, PASS)
             store_codes(slice(a, a + 1), slice(PASS + CHUNK, S), nc.scalar if a else nc.sync)
-        for quad in range(4):
-            queue = nc.sync if quad % 2 == 0 else nc.scalar
+        for quad in QUADS:
+            queue = nc.sync if quad < 2 else nc.scalar
             queue.dma_start(out_2[:, 4 * quad:4 * quad + 4, :].rearrange("a n c -> n a c").bitcast(I32),
                             y_scales[32 * quad:32 * quad + 4, :, :].bitcast(I32))

@@ -24,6 +24,7 @@ SHIFT = 1.375
 V2_ROW = 4
 HEAD = 64
 VECTOR_SHARE = 128
+SCALAR_SHARE = 20
 QUADS = (0, 2, 1, 3)
 FLOPS = 2 * (2 * K * H * S + H * S * S2)
 
@@ -47,7 +48,7 @@ def tile_list_cortex_rates_kernel(tc, tab_words, tab_scales, offs, tab2_words, t
         k_scales = held([P, 2, S + H], U8, "k_scales")
         w4_raw = held([P, 2, 2 * H], U8, "w4_raw")
         v_table = [held([P, T], I32, "v_table0")]
-        w1_raw = [held([P, 4, H], F32, "w1_raw0")]
+        w1_raw = held([P, 4, H], F32, "w1_raw")
         gain = held([P, 4], F32, "gain")
         floor = held([P, 2, 4], F32, "floor")
         warm = held([P, 2], F32, "warm")
@@ -62,8 +63,8 @@ def tile_list_cortex_rates_kernel(tc, tab_words, tab_scales, offs, tab2_words, t
         nc.gpsimd.memset(v2_scales[:].bitcast(I32), 0)
         nc.scalar.activation(warm[:, 1:2], warm[:, 0:1], ACT.Abs_reciprocal_sqrt)
 
-        def load_w1(a):
-            nc.sync.dma_start(w1_raw[a][:], w1[PASS * a:PASS * (a + 1), :].rearrange("(p j) c -> p j c", j=4))
+        def load_w1(tile, a, lo, hi):
+            nc.sync.dma_start(tile[:], w1[PASS * a:PASS * (a + 1), lo:hi].rearrange("(p j) c -> p j c", j=4))
 
         def load_words(tile, words):
             nc.sync.dma_start(tile[:], words.rearrange("p t i -> p (t i)").bitcast(I32))
@@ -74,7 +75,7 @@ def tile_list_cortex_rates_kernel(tc, tab_words, tab_scales, offs, tab2_words, t
         nc.sync.dma_start(w4_raw[:].bitcast(I32), w4_words.rearrange("a p c -> p a c").bitcast(I32))
         nc.sync.dma_start(neurons[:], offs2)
         load_words(v_table[0], tab_words[0])
-        load_w1(0)
+        load_w1(w1_raw, 0, 0, H)
         nc.sync.dma_start(v2_scale_rows[0:16, :].bitcast(I32), tab2_scales[0].bitcast(I32))
         nc.gpsimd.dma_start(gain[:], g.rearrange("(p t) -> p t", t=4))
         nc.gpsimd.dma_start(floor[:], base.rearrange("(a p t) -> p a t", a=2, t=4))
@@ -88,42 +89,50 @@ def tile_list_cortex_rates_kernel(tc, tab_words, tab_scales, offs, tab2_words, t
         for quad in QUADS:
             nc.sync.dma_start(k_scales[32 * quad:32 * quad + 4, :, :].bitcast(I32),
                               staged[8 * quad:8 * quad + 8, :].bitcast(I32))
-        w1_raw.append(held([P, 4, H], F32, "w1_raw1", tag="v_scale_picked"))
-        load_w1(1)
+        v_table.append(held([P, T], I32, "v_table1", tag="v_scale_picked"))
+        load_words(v_table[1], tab_words[1])
         w4_dealt = held([P, 2, 2 * H], U8, "w4_dealt")
         nc.vector.tensor_copy(w4_dealt[:].bitcast(U16).rearrange("p a (t m) -> p a m t", t=4),
                               w4_raw[:].bitcast(U16).rearrange("p a (m t) -> p a m t", t=4))
-        v_table.append(held([P, T], I32, "v_table1", tag="w4_raw"))
-        load_words(v_table[1], tab_words[1])
+        half_raw = [held([P, 4, H // 2], F32, "half_raw0", tag="w4_raw"),
+                    held([P, 4, H // 2], F32, "half_raw1", tag="staged")]
+        for half in range(2):
+            load_w1(half_raw[half], 1, half * H // 2, (half + 1) * H // 2)
 
-        w1_woven = [held([P, 4 * H], BF16, "w1_woven%d" % a) for a in range(2)]
+        w1_woven = held([P, 4 * H], BF16, "w1_woven")
+        half_woven = [held([P, 4, 2 * P], BF16, "half_woven%d" % half) for half in range(2)]
         w1_codes = [held([P, H], U32, "w1_codes%d" % a) for a in range(2)]
         w1_scales = [held([P, H], U8, "w1_scales%d" % a) for a in range(2)]
 
-        def round_w1(a):
-            nc.scalar.activation(w1_woven[a][:].rearrange("p (t m j) -> p m j t", t=4, j=4),
-                                 w1_raw[a][:].rearrange("p j (m t) -> p m j t", t=4), ACT.Copy)
+        def share(half, lo, hi):
+            return (half_woven[half][:].rearrange("p t (m j) -> p m j t", j=4)[:, lo:hi],
+                    half_raw[half][:].rearrange("p j (m t) -> p m j t", t=4)[:, lo:hi])
 
-        def quantise_w1(a):
-            nc.vector.quantize_mx(out=w1_codes[a][:].bitcast(FP8X4), scales=w1_scales[a][:], in_=w1_woven[a][:])
+        def round_half(half):
+            nc.scalar.activation(*share(half, 0, SCALAR_SHARE), ACT.Copy)
+            nc.vector.tensor_copy(*share(half, SCALAR_SHARE, P // 2))
 
-        v_picked = [held([P, S], U32, "v_picked%d" % a) for a in range(2)]
+        def quantise_half(half):
+            for t in range(4):
+                cols = slice(P * t + half * P // 2, P * t + (half + 1) * P // 2)
+                nc.vector.quantize_mx(out=w1_codes[1][:, cols].bitcast(FP8X4), scales=w1_scales[1][:, cols],
+                                      in_=half_woven[half][:, t, :])
 
-        def pick_images(a, lo, hi):
-            nc.vector.tensor_copy(v_picked[a][:, lo:hi],
-                                  v_table[a][:].bitcast(U32).indirect(images[:, lo // 16:hi // 16]))
+        v_picked = [held([P, S], U32, "v_picked0"), held([P, PASS], U32, "v_picked1")]
+
+        def pick_images(picked, a, lo, hi):
+            nc.vector.tensor_copy(picked, v_table[a][:].bitcast(U32).indirect(images[:, lo // 16:hi // 16]))
 
         for lo in (0, PASS):
-            pick_images(0, lo, lo + PASS)
-        round_w1(0)
-        quantise_w1(0)
-        v2_table = held([P, T2], I32, "v2_table", tag="w1_raw0")
+            pick_images(v_picked[0][:, lo:lo + PASS], 0, lo, lo + PASS)
+        nc.scalar.activation(w1_woven[:].rearrange("p (t m j) -> p m j t", t=4, j=4),
+                             w1_raw[:].rearrange("p j (m t) -> p m j t", t=4), ACT.Copy)
+        nc.vector.quantize_mx(out=w1_codes[0][:].bitcast(FP8X4), scales=w1_scales[0][:], in_=w1_woven[:])
+        v2_table = held([P, T2], I32, "v2_table", tag="w1_raw")
         load_words(v2_table, tab2_words[0])
-        round_w1(1)
         v2_scale_picked = held([P, S2], U8, "v2_scale_picked")
         v2_scale_dealt = held([P, S2], U8, "v2_scale_dealt")
         nc.vector.tensor_copy(v2_scale_picked[:], v2_scale_rows[:].indirect(neurons[:]))
-        quantise_w1(1)
         nc.vector.tensor_copy(v2_scale_dealt[:].rearrange("p (a t m) -> p a m t", a=2, t=4),
                               v2_scale_picked[:].rearrange("p (a m t) -> p a m t", a=2, t=4))
         for quad in QUADS:
@@ -131,14 +140,20 @@ def tile_list_cortex_rates_kernel(tc, tab_words, tab_scales, offs, tab2_words, t
             nc.sync.dma_start(v2_scales[first:first + 4, :].bitcast(I32),
                               v2_scale_dealt[4 * quad:4 * quad + 4, :].bitcast(I32))
 
-        banks = [[psum.tile([P, 2, CHUNK], F32, name="bank%d" % (2 * c + pair)) for pair in range(2)] for c in range(CHUNKS)]
+        banks = [[psum.tile([P, 2, CHUNK], F32, name="bank%d" % (2 * c + pair)) for pair in range(2)]
+                 for c in range(CHUNKS - 1)]
+
+        def picked_words(a, c):
+            if a == 1 and c >= 2:
+                return v_late[:, CHUNK * (c - 2):CHUNK * (c - 1)].bitcast(FP8X4)
+            return v_picked[a][:, CHUNK * c:CHUNK * (c + 1)].bitcast(FP8X4)
 
         def stored_pass(a, c, t, start=False):
             cols = slice(CHUNK * c, CHUNK * (c + 1))
             nc.tensor.matmul_mx(out=banks[c][t // 2][:, t % 2, :],
                                 lhsT=w4_dealt[:, a, 2 * P * t:2 * P * (t + 1)].bitcast(FP4X4),
                                 lhsT_scale=k_scales[:, a, S + P * t:S + P * (t + 1)],
-                                rhs=v_picked[a][:, cols].bitcast(FP8X4), rhs_scale=k_scales[:, a, cols],
+                                rhs=picked_words(a, c), rhs_scale=k_scales[:, a, cols],
                                 start=start, stop=False)
 
         def learned_pass(a, c, t, stop=False):
@@ -146,19 +161,29 @@ def tile_list_cortex_rates_kernel(tc, tab_words, tab_scales, offs, tab2_words, t
             nc.tensor.matmul_mx(out=banks[c][t // 2][:, t % 2, :],
                                 lhsT=w1_codes[a][:, P * t:P * (t + 1)].bitcast(FP8X4),
                                 lhsT_scale=w1_scales[a][:, P * t:P * (t + 1)],
-                                rhs=v_picked[a][:, cols].bitcast(FP8X4), rhs_scale=k_scales[:, a, cols],
+                                rhs=picked_words(a, c), rhs_scale=k_scales[:, a, cols],
                                 start=False, stop=stop)
 
-        for lo, hi in ((0, CHUNK), (CHUNK, PASS), (PASS, S)):
-            pick_images(1, lo, hi)
-        for c in range(CHUNKS):
-            for t in range(4):
-                stored_pass(0, c, t, start=(t % 2 == 0))
-        for c in range(CHUNKS):
-            for t in range(4):
-                learned_pass(0, c, t)
+        pick_images(v_picked[1][:], 1, 0, PASS)
+        for half in range(2):
+            round_half(half)
+            quantise_half(half)
+        v_late = held([P, PASS], U32, "v_late", tag="half_woven1")
+        pick_images(v_late[:], 1, PASS, S)
+        for one_pass in (stored_pass, learned_pass):
+            for c in range(CHUNKS - 1):
+                for t in range(4):
+                    if one_pass == stored_pass:
+                        stored_pass(0, c, t, start=(t % 2 == 0))
+                    else:
+                        learned_pass(0, c, t)
+        for c in range(2):
             for t in range(4):
                 stored_pass(1, c, t)
+        for c in range(CHUNKS - 1):
+            for t in range(4):
+                if c >= 2:
+                    stored_pass(1, c, t)
                 learned_pass(1, c, t, stop=(t % 2 == 1))
 
         v2_picked = held([P, S2], U32, "v2_picked")
@@ -187,25 +212,27 @@ def tile_list_cortex_rates_kernel(tc, tab_words, tab_scales, offs, tab2_words, t
             nc.scalar.activation(roots[c][pair][:, part, :], squares[c][pair][:, part, :], ACT.Abs_reciprocal_sqrt,
                                  bias=SHIFT)
 
-        def invert(c, pair):
-            nc.scalar.activation(inverses[c][pair], roots[c][pair], ACT.Square)
+        def invert(c, pair, part=slice(0, 2)):
+            nc.scalar.activation(inverses[c][pair][:, part, :], roots[c][pair][:, part, :], ACT.Square)
 
         for step in (square, root):
             for i in range(2):
                 step(0, 0, slice(i, i + 1))
         nc.gpsimd.tensor_tensor(inverses[0][0], roots[0][0], roots[0][0], ALU.mult)
-        square(0, 1)
-        square(1, 0)
-        root(0, 1)
-        square(1, 1)
-        invert(0, 1)
-        for step in (root, invert):
-            for pair in range(2):
-                step(1, pair)
-        for c in range(2, CHUNKS):
+        for step in (square, root, invert):
+            for i in range(2):
+                step(0, 1, slice(i, i + 1))
+        for c in range(1, CHUNKS):
             for step in (square, root, invert):
                 for pair in range(2):
                     step(c, pair)
+            if c == 1:
+                last = CHUNKS - 1
+                banks.append([psum.tile([P, 2, CHUNK], F32, name="late", tag="bank%d" % (2 + pair)) for pair in range(2)])
+                for t in range(4):
+                    for a in range(2):
+                        stored_pass(a, last, t, start=(t % 2 == 0 and a == 0))
+                        learned_pass(a, last, t, stop=(t % 2 == 1 and a == 1))
 
         def woven_view(ap):
             return ap.rearrange("p (c i t) -> p c t i", i=4, t=4)
@@ -239,7 +266,7 @@ def tile_list_cortex_rates_kernel(tc, tab_words, tab_scales, offs, tab2_words, t
 
         y = [[held([P, 4, PASS], F32, "y%d_0" % half, tag="root%d_1" % (2 * half + 1)),
               held([P, 4, PASS], F32, "y%d_1" % half)] for half in range(2)]
-        turns = [(0, 1, 2, 3), (6, 4, 5, 7)]
+        turns = [(6, 7, 0, 1), (4, 5, 2, 3)]
         y_woven = [[held([P, 4 * PASS], BF16, "y_woven0_%d" % a) for a in range(2)],
                    [held([P, 4 * PASS], BF16, "y_woven1_0")]]
         y_codes = held([P, 2, S], U32, "y_codes")

@@ -49,8 +49,6 @@ def tile_list_cortex_rates_kernel(tc, tab_words, tab_scales, offs, tab2_words, t
         w4_raw = held([P, 2, 2 * H], U8, "w4_raw")
         v_table = [held([P, T], I32, "v_table0")]
         w1_raw = held([P, 4, H], F32, "w1_raw")
-        gain = held([P, 4], F32, "gain")
-        floor = held([P, 2, 4], F32, "floor")
         warm = held([P, 2], F32, "warm")
 
         nc.vector.memset(warm[:, 0:1], 1.0)
@@ -77,8 +75,6 @@ def tile_list_cortex_rates_kernel(tc, tab_words, tab_scales, offs, tab2_words, t
         load_words(v_table[0], tab_words[0])
         load_w1(w1_raw, 0, 0, H)
         nc.sync.dma_start(v2_scale_rows[0:16, :].bitcast(I32), tab2_scales[0].bitcast(I32))
-        nc.gpsimd.dma_start(gain[:], g.rearrange("(p t) -> p t", t=4))
-        nc.gpsimd.dma_start(floor[:], base.rearrange("(a p t) -> p a t", a=2, t=4))
 
         v_scale_picked = held([P, S], U8, "v_scale_picked")
         staged = held([P, S + H], U8, "staged")
@@ -168,6 +164,10 @@ def tile_list_cortex_rates_kernel(tc, tab_words, tab_scales, offs, tab2_words, t
         for half in range(2):
             round_half(half)
             quantise_half(half)
+        gain = held([P, 4], F32, "gain", tag="w4_raw")
+        floor = held([P, 2, 4], F32, "floor", tag="staged")
+        nc.sync.dma_start(gain[:], g.rearrange("(p t) -> p t", t=4))
+        nc.sync.dma_start(floor[:], base.rearrange("(a p t) -> p a t", a=2, t=4))
         v_late = held([P, PASS], U32, "v_late", tag="half_woven1")
         pick_images(v_late[:], 1, PASS, S)
         for one_pass in (stored_pass, learned_pass):

@@ -222,10 +222,13 @@ def tile_list_cortex_rates_kernel(tc, tab_words, tab_scales, offs, tab2_words, t
         for step in (square, root, invert):
             for i in range(2):
                 step(0, 1, slice(i, i + 1))
-        for c in range(1, CHUNKS):
+        def curve(c):
             for step in (square, root, invert):
                 for pair in range(2):
                     step(c, pair)
+
+        for c in range(1, CHUNKS - 1):
+            curve(c)
             if c == 1:
                 last = CHUNKS - 1
                 banks.append([psum.tile([P, 2, CHUNK], F32, name="late", tag="bank%d" % (2 + pair)) for pair in range(2)])
@@ -264,8 +267,11 @@ def tile_list_cortex_rates_kernel(tc, tab_words, tab_scales, offs, tab2_words, t
         deal_v2(1)
         quantise_h(0)
 
-        y = [[held([P, 4, PASS], F32, "y%d_0" % half, tag="root%d_1" % (2 * half + 1)),
-              held([P, 4, PASS], F32, "y%d_1" % half)] for half in range(2)]
+        def y_tiles(half):
+            return [held([P, 4, PASS], F32, "y%d_0" % half, tag="root%d_1" % (2 * half + 1)),
+                    held([P, 4, PASS], F32, "y%d_1" % half)]
+
+        y = [y_tiles(0)]
         turns = [(6, 7, 0, 1), (4, 5, 2, 3)]
         y_woven = [[held([P, 4 * PASS], BF16, "y_woven0_%d" % a) for a in range(2)],
                    [held([P, 4 * PASS], BF16, "y_woven1_0")]]
@@ -289,9 +295,9 @@ def tile_list_cortex_rates_kernel(tc, tab_words, tab_scales, offs, tab2_words, t
                     slices = slice(2 * pair, 2 * pair + 2)
                     nc.vector.tensor_tensor(y[c // 2][a][:, slices, CHUNK * (c % 2):CHUNK * (c % 2 + 1)], drive[:],
                                             floor[:, a, slices].unsqueeze(2).to_broadcast([P, 2, CHUNK]), ALU.max)
-                    if c >= 2:
+                    if c >= 1:
                         store_y(c, a, slices)
-                if c < 2:
+                if c < 1:
                     store_y(c, a, slice(0, 4))
 
         def woven_part(half, a, lo, hi):
@@ -316,13 +322,20 @@ def tile_list_cortex_rates_kernel(tc, tab_words, tab_scales, offs, tab2_words, t
             fire(c)
             weave_on_gpsimd(*woven_part(*heads[c]))
             quantise_h(c + 1)
-        weave_y_on_scalar(0, 0, HEAD, CHUNK)
-        weave_y_on_scalar(0, 0, CHUNK + HEAD, PASS)
+            if c == 0:
+                weave_y_on_scalar(0, 0, HEAD, CHUNK)
+                curve(CHUNKS - 1)
+                y.append(y_tiles(1))
+            if c == 1:
+                quantise_y(0, 0, 0, CHUNK)
+                store_codes(slice(0, 1), slice(0, CHUNK), nc.sync)
         weave_y_on_scalar(0, 1, 0, PASS)
-        for a in range(2):
-            quantise_y(0, a, 0, PASS)
-            store_codes(slice(a, a + 1), slice(0, PASS), nc.sync)
-        y_woven[1].append(held([P, 4 * PASS], BF16, "y_woven1_1", tag="y_woven0_1"))
+        weave_y_on_scalar(0, 0, CHUNK + HEAD, PASS)
+        quantise_y(0, 1, 0, PASS)
+        store_codes(slice(1, 2), slice(0, PASS), nc.sync)
+        quantise_y(0, 0, CHUNK, PASS)
+        store_codes(slice(0, 1), slice(CHUNK, PASS), nc.sync)
+        y_woven[1].append(held([P, 4 * PASS], BF16, "y_woven1_1", tag="y_woven0_0"))
         weave_on_gpsimd(*woven_part(1, 1, 0, CHUNK))
         weave_y_on_scalar(1, 0, HEAD, CHUNK)
         fire(CHUNKS - 1)

@@ -24,7 +24,7 @@ SHIFT = 1.375
 V2_ROW = 4
 HEAD = 64
 VECTOR_SHARE = 128
-SCALAR_SHARE = 20
+SCALAR_SHARES = (32, 88)
 QUADS = (0, 2, 1, 3)
 FLOPS = 2 * (2 * K * H * S + H * S * S2)
 
@@ -61,8 +61,8 @@ def tile_list_cortex_rates_kernel(tc, tab_words, tab_scales, offs, tab2_words, t
         nc.gpsimd.memset(v2_scales[:].bitcast(I32), 0)
         nc.scalar.activation(warm[:, 1:2], warm[:, 0:1], ACT.Abs_reciprocal_sqrt)
 
-        def load_w1(tile, a, lo, hi):
-            nc.sync.dma_start(tile[:], w1[PASS * a:PASS * (a + 1), lo:hi].rearrange("(p j) c -> p j c", j=4))
+        def load_w1(tile, a):
+            nc.sync.dma_start(tile[:], w1[PASS * a:PASS * (a + 1), :].rearrange("(p j) c -> p j c", j=4))
 
         def load_words(tile, words):
             nc.sync.dma_start(tile[:], words.rearrange("p t i -> p (t i)").bitcast(I32))
@@ -73,7 +73,7 @@ def tile_list_cortex_rates_kernel(tc, tab_words, tab_scales, offs, tab2_words, t
         nc.sync.dma_start(w4_raw[:].bitcast(I32), w4_words.rearrange("a p c -> p a c").bitcast(I32))
         nc.sync.dma_start(neurons[:], offs2)
         load_words(v_table[0], tab_words[0])
-        load_w1(w1_raw, 0, 0, H)
+        load_w1(w1_raw, 0)
         nc.sync.dma_start(v2_scale_rows[0:16, :].bitcast(I32), tab2_scales[0].bitcast(I32))
 
         v_scale_picked = held([P, S], U8, "v_scale_picked")
@@ -90,31 +90,26 @@ def tile_list_cortex_rates_kernel(tc, tab_words, tab_scales, offs, tab2_words, t
         w4_dealt = held([P, 2, 2 * H], U8, "w4_dealt")
         nc.vector.tensor_copy(w4_dealt[:].bitcast(U16).rearrange("p a (t m) -> p a m t", t=4),
                               w4_raw[:].bitcast(U16).rearrange("p a (m t) -> p a m t", t=4))
-        half_raw = [held([P, 4, H // 2], F32, "half_raw0", tag="w4_raw"),
-                    held([P, 4, H // 2], F32, "half_raw1", tag="staged")]
-        for half in range(2):
-            load_w1(half_raw[half], 1, half * H // 2, (half + 1) * H // 2)
+        late_raw = held([P, 4, H], F32, "late_raw", tag="w4_raw")
+        load_w1(late_raw, 1)
 
         w1_woven = held([P, 4 * H], BF16, "w1_woven")
-        half_woven = [held([P, 4, 2 * P], BF16, "half_woven%d" % half) for half in range(2)]
+        pair_woven = [held([P, 2 * H], BF16, "pair_woven%d" % pair) for pair in range(2)]
         w1_codes = [held([P, H], U32, "w1_codes%d" % a) for a in range(2)]
         w1_scales = [held([P, H], U8, "w1_scales%d" % a) for a in range(2)]
 
-        def share(half, lo, hi):
-            return (half_woven[half][:].rearrange("p t (m j) -> p m j t", j=4)[:, lo:hi],
-                    half_raw[half][:].rearrange("p j (m t) -> p m j t", t=4)[:, lo:hi])
+        def share(pair, lo, hi):
+            return (pair_woven[pair][:].rearrange("p (s m j) -> p m j s", s=2, j=4)[:, lo:hi],
+                    late_raw[:].rearrange("p j (m u s) -> p u m j s", u=2, s=2)[:, pair, lo:hi])
 
-        def round_half(half):
-            nc.scalar.activation(*share(half, 0, SCALAR_SHARE), ACT.Copy)
-            nc.vector.tensor_copy(*share(half, SCALAR_SHARE, P // 2))
+        def round_pair(pair):
+            nc.scalar.activation(*share(pair, 0, SCALAR_SHARES[pair]), ACT.Copy)
+            nc.vector.tensor_copy(*share(pair, SCALAR_SHARES[pair], P))
+            cols = slice(2 * P * pair, 2 * P * (pair + 1))
+            nc.vector.quantize_mx(out=w1_codes[1][:, cols].bitcast(FP8X4), scales=w1_scales[1][:, cols],
+                                  in_=pair_woven[pair][:])
 
-        def quantise_half(half):
-            for t in range(4):
-                cols = slice(P * t + half * P // 2, P * t + (half + 1) * P // 2)
-                nc.vector.quantize_mx(out=w1_codes[1][:, cols].bitcast(FP8X4), scales=w1_scales[1][:, cols],
-                                      in_=half_woven[half][:, t, :])
-
-        v_picked = [held([P, S], U32, "v_picked0"), held([P, PASS], U32, "v_picked1")]
+        v_picked = [held([P, S], U32, "v_picked0"), held([P, S - CHUNK], U32, "v_picked1")]
 
         def pick_images(picked, a, lo, hi):
             nc.vector.tensor_copy(picked, v_table[a][:].bitcast(U32).indirect(images[:, lo // 16:hi // 16]))
@@ -140,8 +135,8 @@ def tile_list_cortex_rates_kernel(tc, tab_words, tab_scales, offs, tab2_words, t
                  for c in range(CHUNKS - 1)]
 
         def picked_words(a, c):
-            if a == 1 and c >= 2:
-                return v_late[:, CHUNK * (c - 2):CHUNK * (c - 1)].bitcast(FP8X4)
+            if a == 1 and c == CHUNKS - 1:
+                return v_late[:].bitcast(FP8X4)
             return v_picked[a][:, CHUNK * c:CHUNK * (c + 1)].bitcast(FP8X4)
 
         def stored_pass(a, c, t, start=False):
@@ -160,16 +155,16 @@ def tile_list_cortex_rates_kernel(tc, tab_words, tab_scales, offs, tab2_words, t
                                 rhs=picked_words(a, c), rhs_scale=k_scales[:, a, cols],
                                 start=False, stop=stop)
 
-        pick_images(v_picked[1][:], 1, 0, PASS)
-        for half in range(2):
-            round_half(half)
-            quantise_half(half)
+        for lo, hi in ((0, PASS), (PASS, S - CHUNK)):
+            pick_images(v_picked[1][:, lo:hi], 1, lo, hi)
+        for pair in range(2):
+            round_pair(pair)
         gain = held([P, 4], F32, "gain", tag="w4_raw")
-        floor = held([P, 2, 4], F32, "floor", tag="staged")
+        floor = held([P, 2, 4], F32, "floor", tag="pair_woven0")
         nc.sync.dma_start(gain[:], g.rearrange("(p t) -> p t", t=4))
         nc.sync.dma_start(floor[:], base.rearrange("(a p t) -> p a t", a=2, t=4))
-        v_late = held([P, PASS], U32, "v_late", tag="half_woven1")
-        pick_images(v_late[:], 1, PASS, S)
+        v_late = held([P, CHUNK], U32, "v_late", tag="pair_woven1")
+        pick_images(v_late[:], 1, S - CHUNK, S)
         for one_pass in (stored_pass, learned_pass):
             for c in range(CHUNKS - 1):
                 for t in range(4):
@@ -177,13 +172,11 @@ def tile_list_cortex_rates_kernel(tc, tab_words, tab_scales, offs, tab2_words, t
                         stored_pass(0, c, t, start=(t % 2 == 0))
                     else:
                         learned_pass(0, c, t)
-        for c in range(2):
+        for c in range(CHUNKS - 1):
             for t in range(4):
                 stored_pass(1, c, t)
         for c in range(CHUNKS - 1):
             for t in range(4):
-                if c >= 2:
-                    stored_pass(1, c, t)
                 learned_pass(1, c, t, stop=(t % 2 == 1))
 
         v2_picked = held([P, S2], U32, "v2_picked")

@@ -160,10 +160,10 @@ def tile_list_cortex_rates_kernel(tc, tab_words, tab_scales, offs, tab2_words, t
         for pair in range(2):
             round_pair(pair)
         gain = held([P, 4], F32, "gain", tag="w4_raw")
-        floor = held([P, 2, 4], F32, "floor", tag="pair_woven0")
+        floor = held([P, 2, 4], F32, "floor", tag="pair_woven1")
         nc.sync.dma_start(gain[:], g.rearrange("(p t) -> p t", t=4))
         nc.sync.dma_start(floor[:], base.rearrange("(a p t) -> p a t", a=2, t=4))
-        v_late = held([P, CHUNK], U32, "v_late", tag="pair_woven1")
+        v_late = held([P, CHUNK], U32, "v_late", tag="pair_woven0")
         pick_images(v_late[:], 1, S - CHUNK, S)
         for one_pass in (stored_pass, learned_pass):
             for c in range(CHUNKS - 1):

@@ -179,16 +179,10 @@ def tile_list_cortex_rates_kernel(tc, tab_words, tab_scales, offs, tab2_words, t
             for t in range(4):
                 learned_pass(1, c, t, stop=(t % 2 == 1))
 
-        v2_picked = held([P, S2], U32, "v2_picked")
-        v2_dealt = held([P, S2], I32, "v2_dealt")
+        v2_dealt = held([P, S2], U32, "v2_dealt")
         for a in range(2):
-            nc.vector.tensor_copy(v2_picked[:, PASS * a:PASS * (a + 1)],
+            nc.vector.tensor_copy(v2_dealt[:, PASS * a:PASS * (a + 1)].rearrange("p (t m) -> p m t", t=4),
                                   v2_table[:].bitcast(U32).indirect(neurons[:, 32 * a:32 * (a + 1)]))
-
-        def deal_v2(a):
-            cols = slice(PASS * a, PASS * (a + 1))
-            nc.vector.tensor_copy(v2_dealt[:, cols].rearrange("p (t m) -> p m t", t=4),
-                                  v2_picked[:, cols].bitcast(I32).rearrange("p (m t) -> p m t", t=4))
 
         def pair_tiles(name, c):
             return [held([P, 2, CHUNK], F32, "%s%d_%d" % (name, c, pair))[:] for pair in range(2)]
@@ -212,9 +206,10 @@ def tile_list_cortex_rates_kernel(tc, tab_words, tab_scales, offs, tab2_words, t
             for i in range(2):
                 step(0, 0, slice(i, i + 1))
         nc.gpsimd.tensor_tensor(inverses[0][0], roots[0][0], roots[0][0], ALU.mult)
-        for step in (square, root, invert):
+        for step in (square, root):
             for i in range(2):
                 step(0, 1, slice(i, i + 1))
+        nc.vector.tensor_tensor(inverses[0][1], roots[0][1], roots[0][1], ALU.mult)
         def curve(c):
             for step in (square, root, invert):
                 for pair in range(2):
@@ -244,8 +239,9 @@ def tile_list_cortex_rates_kernel(tc, tab_words, tab_scales, offs, tab2_words, t
         h_codes = [held([P, CHUNK], U32, "h_codes%d" % c) for c in range(CHUNKS)]
         h_scales = [held([P, CHUNK], U8, "h_scales%d" % c) for c in range(CHUNKS)]
 
-        def quantise_h(c):
-            nc.vector.quantize_mx(out=h_codes[c][:].bitcast(FP8X4), scales=h_scales[c][:], in_=h_woven[c][:])
+        def quantise_h(c, lo=0, hi=CHUNK):
+            nc.vector.quantize_mx(out=h_codes[c][:, lo:hi].bitcast(FP8X4), scales=h_scales[c][:, lo:hi],
+                                  in_=h_woven[c][:, 4 * lo:4 * hi])
 
         def respond(c, tag=None):
             h_sliced = held([P, 4, CHUNK], BF16, "h_sliced%d" % c, tag=tag)
@@ -255,10 +251,10 @@ def tile_list_cortex_rates_kernel(tc, tab_words, tab_scales, offs, tab2_words, t
             return h_sliced[:]
 
         first_sliced = respond(0)
-        deal_v2(0)
-        nc.vector.tensor_copy(woven_view(h_woven[0][:]), sliced_view(first_sliced))
-        deal_v2(1)
-        quantise_h(0)
+        for lo in (0, P):
+            nc.vector.tensor_copy(woven_view(h_woven[0][:, 4 * lo:4 * (lo + P)]), sliced_view(first_sliced[:, :, lo:lo + P]))
+        for lo in (0, P):
+            quantise_h(0, lo, lo + P)
 
         def y_tiles(half):
             return [held([P, 4, PASS], F32, "y%d_0" % half, tag="root%d_1" % (2 * half + 1)),

@@ -159,7 +159,7 @@ def tile_list_cortex_rates_kernel(tc, tab_words, tab_scales, offs, tab2_words, t
             pick_images(v_picked[1][:, lo:hi], 1, lo, hi)
         for pair in range(2):
             round_pair(pair)
-        gain = held([P, 4], F32, "gain", tag="w4_raw")
+        gain = held([P, 4], F32, "gain", tag="w1_woven")
         floor = held([P, 2, 4], F32, "floor", tag="pair_woven1")
         nc.sync.dma_start(gain[:], g.rearrange("(p t) -> p t", t=4))
         nc.sync.dma_start(floor[:], base.rearrange("(a p t) -> p a t", a=2, t=4))
@@ -187,9 +187,11 @@ def tile_list_cortex_rates_kernel(tc, tab_words, tab_scales, offs, tab2_words, t
         def pair_tiles(name, c):
             return [held([P, 2, CHUNK], F32, "%s%d_%d" % (name, c, pair))[:] for pair in range(2)]
 
-        squares = [pair_tiles("square", c) for c in range(CHUNKS)]
+        first_factors = [held([P, 4, CHUNK], F32, "first_factor0")[:]]
+        squares = [[held([P, 2, CHUNK], F32, "square0_0")[:], first_factors[0][:, 2:4, :]]]
+        squares.extend(pair_tiles("square", c) for c in range(1, CHUNKS))
         roots = [pair_tiles("root", c) for c in range(CHUNKS)]
-        inverses = [pair_tiles("inverse", c) for c in range(CHUNKS)]
+        inverses = [None] + [pair_tiles("inverse", c) for c in range(1, CHUNKS)]
 
         def square(c, pair, part=slice(0, 2)):
             nc.scalar.activation(squares[c][pair][:, part, :], banks[c][pair][:, part, :], ACT.Square,
@@ -205,25 +207,37 @@ def tile_list_cortex_rates_kernel(tc, tab_words, tab_scales, offs, tab2_words, t
         for step in (square, root):
             for i in range(2):
                 step(0, 0, slice(i, i + 1))
-        nc.gpsimd.tensor_tensor(inverses[0][0], roots[0][0], roots[0][0], ALU.mult)
+        for t in range(2):
+            nc.gpsimd.tensor_scalar(first_factors[0][:, t, :], squares[0][0][:, t, :], gain[:, t:t + 1], -0.0,
+                                    ALU.mult, ALU.add)
+        first_factors.append(held([P, 4, CHUNK], F32, "first_factor1", tag="square0_0")[:])
+        nc.gpsimd.tensor_tensor(first_factors[1][:, 0:2, :], roots[0][0], roots[0][0], ALU.mult)
         for step in (square, root):
             for i in range(2):
                 step(0, 1, slice(i, i + 1))
-        nc.vector.tensor_tensor(inverses[0][1], roots[0][1], roots[0][1], ALU.mult)
+        for lo in (0, P):
+            for t in (2, 3):
+                root_part = roots[0][1][:, t - 2, lo:lo + P]
+                nc.vector.scalar_tensor_tensor(first_factors[1][:, t, lo:lo + P], root_part, gain[:, t:t + 1], root_part,
+                                               ALU.mult, ALU.mult)
         def curve(c):
             for step in (square, root, invert):
                 for pair in range(2):
                     step(c, pair)
 
-        for c in range(1, CHUNKS - 1):
-            curve(c)
-            if c == 1:
-                last = CHUNKS - 1
-                banks.append([psum.tile([P, 2, CHUNK], F32, name="late", tag="bank%d" % (2 + pair)) for pair in range(2)])
-                for t in range(4):
-                    for a in range(2):
-                        stored_pass(a, last, t, start=(t % 2 == 0 and a == 0))
-                        learned_pass(a, last, t, stop=(t % 2 == 1 and a == 1))
+        last = CHUNKS - 1
+        banks.append([])
+
+        def sum_late(pair, bank):
+            banks[last].append(psum.tile([P, 2, CHUNK], F32, name="late", tag="bank%d" % bank))
+            for i in range(2):
+                for a in range(2):
+                    stored_pass(a, last, 2 * pair + i, start=(i == 0 and a == 0))
+                    learned_pass(a, last, 2 * pair + i, stop=(i == 1 and a == 1))
+
+        curve(1)
+        sum_late(0, 2)
+        curve(2)
 
         def woven_view(ap):
             return ap.rearrange("p (c i t) -> p c t i", i=4, t=4)
@@ -250,9 +264,10 @@ def tile_list_cortex_rates_kernel(tc, tab_words, tab_scales, offs, tab2_words, t
                                                inverses[c][t // 2][:, t % 2, :], ALU.mult, ALU.mult)
             return h_sliced[:]
 
-        first_sliced = respond(0)
         for lo in (0, P):
-            nc.vector.tensor_copy(woven_view(h_woven[0][:, 4 * lo:4 * (lo + P)]), sliced_view(first_sliced[:, :, lo:lo + P]))
+            nc.vector.tensor_tensor(woven_view(h_woven[0][:, 4 * lo:4 * (lo + P)]),
+                                    sliced_view(first_factors[0][:, :, lo:lo + P]),
+                                    sliced_view(first_factors[1][:, :, lo:lo + P]), ALU.mult)
         for lo in (0, P):
             quantise_h(0, lo, lo + P)
 
@@ -261,9 +276,16 @@ def tile_list_cortex_rates_kernel(tc, tab_words, tab_scales, offs, tab2_words, t
                     held([P, 4, PASS], F32, "y%d_1" % half)]
 
         y = [y_tiles(0)]
-        turns = [(6, 7, 0, 1), (4, 5, 2, 3)]
-        y_woven = [[held([P, 4 * PASS], BF16, "y_woven0_%d" % a) for a in range(2)],
-                   [held([P, 4 * PASS], BF16, "y_woven1_0")]]
+        turns = [(6, 7, 0, 1), (4, 5, 3, 7), (0, 1, 2, 6), (4, 5, 3, 7)]
+        y_woven = {}
+
+        def woven_tile(a, lo, hi, tag=None):
+            tile = held([P, 4 * (hi - lo)], BF16, "y_woven%d_%d" % (a, lo), tag=tag)
+            for col in range(lo, hi, HEAD):
+                y_woven[a, col] = (tile, lo)
+
+        for a, lo, hi in ((0, 0, P), (0, CHUNK, CHUNK + P), (0, PASS, S), (1, 0, PASS)):
+            woven_tile(a, lo, hi)
         y_codes = held([P, 2, S], U32, "y_codes")
         y_scales = held([P, 2, S], U8, "y_scales")
 
@@ -275,7 +297,7 @@ def tile_list_cortex_rates_kernel(tc, tab_words, tab_scales, offs, tab2_words, t
         def fire(c):
             for a in range(2):
                 for pair in range(2):
-                    drive = psum.tile([P, 2, CHUNK], F32, name="drive", tag="bank%d" % turns[c % 2][2 * a + pair])
+                    drive = psum.tile([P, 2, CHUNK], F32, name="drive", tag="bank%d" % turns[c][2 * a + pair])
                     for i in range(2):
                         cols = slice(PASS * a + P * (2 * pair + i), PASS * a + P * (2 * pair + i + 1))
                         nc.tensor.matmul_mx(out=drive[:, i, :], lhsT=v2_dealt[:, cols].bitcast(FP8X4),
@@ -289,56 +311,67 @@ def tile_list_cortex_rates_kernel(tc, tab_words, tab_scales, offs, tab2_words, t
                 if c < 1:
                     store_y(c, a, slice(0, 4))
 
-        def woven_part(half, a, lo, hi):
-            return y_woven[half][a][:, 4 * lo:4 * hi], y[half][a][:, :, lo:hi]
+        def woven_cols(a, lo, hi):
+            tile, first = y_woven[a, lo]
+            return tile[:, 4 * (lo - first):4 * (hi - first)]
 
-        def weave_y_on_scalar(half, a, lo, hi):
-            woven, sliced = woven_part(half, a, lo, hi)
+        def woven_part(a, lo, hi):
+            half = lo // PASS
+            return woven_cols(a, lo, hi), y[half][a][:, :, lo - PASS * half:hi - PASS * half]
+
+        def weave_y_on_scalar(a, lo, hi):
+            woven, sliced = woven_part(a, lo, hi)
             nc.scalar.activation(woven_view(woven), sliced_view(sliced), ACT.Copy)
 
-        def quantise_y(half, a, lo, hi):
-            cols = slice(PASS * half + lo, PASS * half + hi)
-            nc.vector.quantize_mx(out=y_codes[:, a, cols].bitcast(FP8X4), scales=y_scales[:, a, cols],
-                                  in_=y_woven[half][a][:, 4 * lo:4 * hi])
+        def weave_y_on_vector(a, lo, hi):
+            woven, sliced = woven_part(a, lo, hi)
+            nc.vector.tensor_copy(woven_view(woven), sliced_view(sliced))
+
+        def quantise_y(a, lo, hi):
+            nc.vector.quantize_mx(out=y_codes[:, a, lo:hi].bitcast(FP8X4), scales=y_scales[:, a, lo:hi],
+                                  in_=woven_cols(a, lo, hi))
 
         def store_codes(groups, cols, queue):
             queue.dma_start(out_1[groups, :, cols, :].rearrange("a p m t -> p a (m t)").bitcast(I32),
                             y_codes[:, groups, cols].bitcast(I32))
 
-        heads = [(0, 0, 0, HEAD), (0, 0, CHUNK, CHUNK + HEAD), (1, 0, 0, HEAD)]
         for c in range(CHUNKS - 1):
-            weave_on_gpsimd(h_woven[c + 1][:], respond(c + 1, tag="h_sliced0" if c == 0 else None))
+            weave_on_gpsimd(h_woven[c + 1][:], respond(c + 1, tag="first_factor0" if c == 0 else None))
             fire(c)
-            weave_on_gpsimd(*woven_part(*heads[c]))
+            weave_on_gpsimd(*woven_part(0, CHUNK * c, CHUNK * c + HEAD))
             quantise_h(c + 1)
             if c == 0:
-                weave_y_on_scalar(0, 0, HEAD, CHUNK)
-                curve(CHUNKS - 1)
+                sum_late(1, 6)
+                weave_y_on_scalar(0, HEAD, P)
+                curve(last)
                 y.append(y_tiles(1))
-            if c == 1:
-                quantise_y(0, 0, 0, CHUNK)
-                store_codes(slice(0, 1), slice(0, CHUNK), nc.sync)
-        weave_y_on_scalar(0, 1, 0, PASS)
-        weave_y_on_scalar(0, 0, CHUNK + HEAD, PASS)
-        quantise_y(0, 1, 0, PASS)
-        store_codes(slice(1, 2), slice(0, PASS), nc.sync)
-        quantise_y(0, 0, CHUNK, PASS)
-        store_codes(slice(0, 1), slice(CHUNK, PASS), nc.sync)
-        y_woven[1].append(held([P, 4 * PASS], BF16, "y_woven1_1", tag="y_woven0_0"))
-        weave_on_gpsimd(*woven_part(1, 1, 0, CHUNK))
-        weave_y_on_scalar(1, 0, HEAD, CHUNK)
-        fire(CHUNKS - 1)
-        weave_on_gpsimd(*woven_part(1, 0, CHUNK, CHUNK + HEAD))
-        weave_y_on_scalar(1, 0, CHUNK + HEAD, PASS)
-        quantise_y(1, 0, 0, CHUNK)
-        woven, sliced = woven_part(1, 1, CHUNK, CHUNK + VECTOR_SHARE)
-        nc.vector.tensor_copy(woven_view(woven), sliced_view(sliced))
-        weave_y_on_scalar(1, 1, CHUNK + VECTOR_SHARE, PASS)
-        quantise_y(1, 1, 0, CHUNK)
-        store_codes(slice(0, 2), slice(PASS, PASS + CHUNK), nc.sync)
+                continue
+            lo = CHUNK * (c - 1)
+            woven_tile(0, lo + P, lo + CHUNK, tag="h_sliced%d" % (c + 1))
+            weave_y_on_vector(0, lo + P, lo + CHUNK)
+            if c == 2:
+                weave_y_on_scalar(1, 0, PASS)
+                weave_y_on_scalar(0, lo + HEAD, lo + P)
+                quantise_y(1, 0, PASS)
+                store_codes(slice(1, 2), slice(0, PASS), nc.sync)
+            for part in (lo, lo + P):
+                quantise_y(0, part, part + P)
+            store_codes(slice(0, 1), slice(lo, lo + CHUNK), nc.sync)
+        woven_tile(1, PASS, S, tag="h_sliced3")
+        weave_on_gpsimd(*woven_part(1, PASS, PASS + CHUNK))
+        weave_y_on_scalar(0, PASS + HEAD, PASS + CHUNK)
+        fire(last)
+        first = CHUNK * last
+        weave_on_gpsimd(*woven_part(0, first, first + HEAD))
+        weave_y_on_scalar(0, first + HEAD, S)
+        quantise_y(0, PASS, first)
+        weave_y_on_vector(1, first, first + VECTOR_SHARE)
+        weave_y_on_scalar(1, first + VECTOR_SHARE, S)
+        quantise_y(1, PASS, first)
+        store_codes(slice(0, 2), slice(PASS, first), nc.sync)
         for a in range(2):
-            quantise_y(1, a, CHUNK, PASS)
-            store_codes(slice(a, a + 1), slice(PASS + CHUNK, S), nc.scalar if a else nc.sync)
+            quantise_y(a, first, S)
+            store_codes(slice(a, a + 1), slice(first, S), nc.scalar if a else nc.sync)
         for quad in QUADS:
             queue = nc.sync if quad < 2 else nc.scalar
             queue.dma_start(out_2[:, 4 * quad:4 * quad + 4, :].rearrange("a n c -> n a c").bitcast(I32),

@@ -105,9 +105,10 @@ def tile_list_cortex_rates_kernel(tc, tab_words, tab_scales, offs, tab2_words, t
         def round_pair(pair):
             nc.scalar.activation(*share(pair, 0, SCALAR_SHARES[pair]), ACT.Copy)
             nc.vector.tensor_copy(*share(pair, SCALAR_SHARES[pair], P))
-            cols = slice(2 * P * pair, 2 * P * (pair + 1))
-            nc.vector.quantize_mx(out=w1_codes[1][:, cols].bitcast(FP8X4), scales=w1_scales[1][:, cols],
-                                  in_=pair_woven[pair][:])
+            for i in range(2):
+                cols = slice(P * (2 * pair + i), P * (2 * pair + i + 1))
+                nc.vector.quantize_mx(out=w1_codes[1][:, cols].bitcast(FP8X4), scales=w1_scales[1][:, cols],
+                                      in_=pair_woven[pair][:, H * i:H * (i + 1)])
 
         v_picked = [held([P, S], U32, "v_picked0"), held([P, S - CHUNK], U32, "v_picked1")]
 
@@ -284,7 +285,7 @@ def tile_list_cortex_rates_kernel(tc, tab_words, tab_scales, offs, tab2_words, t
             for col in range(lo, hi, HEAD):
                 y_woven[a, col] = (tile, lo)
 
-        for a, lo, hi in ((0, 0, P), (0, CHUNK, CHUNK + P), (0, PASS, S), (1, 0, PASS)):
+        for a, lo, hi in ((0, 0, P), (0, CHUNK, PASS), (0, PASS, S), (1, 0, PASS)):
             woven_tile(a, lo, hi)
         y_codes = held([P, 2, S], U32, "y_codes")
         y_scales = held([P, 2, S], U8, "y_scales")
@@ -345,19 +346,19 @@ def tile_list_cortex_rates_kernel(tc, tab_words, tab_scales, offs, tab2_words, t
                 weave_y_on_scalar(0, HEAD, P)
                 curve(last)
                 y.append(y_tiles(1))
-                continue
-            lo = CHUNK * (c - 1)
-            woven_tile(0, lo + P, lo + CHUNK, tag="h_sliced%d" % (c + 1))
-            weave_y_on_vector(0, lo + P, lo + CHUNK)
-            if c == 2:
-                weave_y_on_scalar(1, 0, PASS)
-                weave_y_on_scalar(0, lo + HEAD, lo + P)
-                quantise_y(1, 0, PASS)
-                store_codes(slice(1, 2), slice(0, PASS), nc.sync)
-            for part in (lo, lo + P):
-                quantise_y(0, part, part + P)
-            store_codes(slice(0, 1), slice(lo, lo + CHUNK), nc.sync)
-        woven_tile(1, PASS, S, tag="h_sliced3")
+            if c == 1:
+                woven_tile(0, P, CHUNK, tag="h_sliced2")
+                weave_y_on_vector(0, P, CHUNK)
+                for part in (0, P):
+                    quantise_y(0, part, part + P)
+                store_codes(slice(0, 1), slice(0, CHUNK), nc.sync)
+        weave_y_on_scalar(1, 0, PASS)
+        weave_y_on_scalar(0, CHUNK + HEAD, PASS)
+        quantise_y(1, 0, PASS)
+        store_codes(slice(1, 2), slice(0, PASS), nc.sync)
+        quantise_y(0, CHUNK, PASS)
+        store_codes(slice(0, 1), slice(CHUNK, PASS), nc.sync)
+        woven_tile(1, PASS, S, tag="y_woven0_%d" % CHUNK)
         weave_on_gpsimd(*woven_part(1, PASS, PASS + CHUNK))
         weave_y_on_scalar(0, PASS + HEAD, PASS + CHUNK)
         fire(last)

@@ -24,7 +24,8 @@ SHIFT = 1.375
 V2_ROW = 4
 HEAD = 64
 VECTOR_SHARE = 128
-SCALAR_SHARES = (32, 88)
+V_TABLE_AT = 16 * H
+V2_TABLE_AT = V_TABLE_AT + 4 * T
 QUADS = (0, 2, 1, 3)
 FLOPS = 2 * (2 * K * H * S + H * S * S2)
 
@@ -34,21 +35,25 @@ def tile_list_cortex_rates_kernel(tc, tab_words, tab_scales, offs, tab2_words, t
     nc = tc.nc
     with ExitStack() as ctx:
         keep = ctx.enter_context(tc.tile_pool(name="keep", bufs=1))
+        reuse = ctx.enter_context(tc.tile_pool(name="reuse", bufs=1))
         psum = ctx.enter_context(tc.psum_pool(name="psum", bufs=1))
 
         def held(shape, dtype, name, tag=None):
             return keep.tile(shape, dtype, name=name, tag=tag or name, align_bytes=64)
 
+        def laid(shape, dtype, name, offset):
+            return reuse.tile(shape, dtype, name=name, offset=offset, align_bytes=64)
+
         images = keep.tile([P, S // 16], U16, name="images")
         neurons = keep.tile([P, S2 // 16], U16, name="neurons")
         v_scale_rows = held([P, T], U8, "v_scale_rows")
         w4_scale_rows = held([P, H], U8, "w4_scale_rows")
-        v2_scale_rows = held([P, T2], U8, "v2_scale_rows")
+        v2_scale_rows = laid([P, T2], U8, "v2_scale_rows", V2_TABLE_AT + 4 * T2 - T2 // 2)
         v2_scales = held([P, S2], U8, "v2_scales")
         k_scales = held([P, 2, S + H], U8, "k_scales")
         w4_raw = held([P, 2, 2 * H], U8, "w4_raw")
         v_table = [held([P, T], I32, "v_table0")]
-        w1_raw = held([P, 4, H], F32, "w1_raw")
+        w1_raw = [held([P, 4, H], F32, "w1_raw0")]
         warm = held([P, 2], F32, "warm")
 
         nc.vector.memset(warm[:, 0:1], 1.0)
@@ -61,8 +66,8 @@ def tile_list_cortex_rates_kernel(tc, tab_words, tab_scales, offs, tab2_words, t
         nc.gpsimd.memset(v2_scales[:].bitcast(I32), 0)
         nc.scalar.activation(warm[:, 1:2], warm[:, 0:1], ACT.Abs_reciprocal_sqrt)
 
-        def load_w1(tile, a):
-            nc.sync.dma_start(tile[:], w1[PASS * a:PASS * (a + 1), :].rearrange("(p j) c -> p j c", j=4))
+        def load_w1(a):
+            nc.sync.dma_start(w1_raw[a][:], w1[PASS * a:PASS * (a + 1), :].rearrange("(p j) c -> p j c", j=4))
 
         def load_words(tile, words):
             nc.sync.dma_start(tile[:], words.rearrange("p t i -> p (t i)").bitcast(I32))
@@ -73,10 +78,10 @@ def tile_list_cortex_rates_kernel(tc, tab_words, tab_scales, offs, tab2_words, t
         nc.sync.dma_start(w4_raw[:].bitcast(I32), w4_words.rearrange("a p c -> p a c").bitcast(I32))
         nc.sync.dma_start(neurons[:], offs2)
         load_words(v_table[0], tab_words[0])
-        load_w1(w1_raw, 0)
+        load_w1(0)
         nc.sync.dma_start(v2_scale_rows[0:16, :].bitcast(I32), tab2_scales[0].bitcast(I32))
 
-        v_scale_picked = held([P, S], U8, "v_scale_picked")
+        v_scale_picked = laid([P, S], U8, "v_scale_picked", V_TABLE_AT - S // 2)
         staged = held([P, S + H], U8, "staged")
         nc.vector.tensor_copy(v_scale_picked[:], v_scale_rows[:].indirect(images[:]))
         nc.vector.tensor_copy(staged[:, S:S + H].rearrange("p (t m) -> p m t", t=4),
@@ -85,100 +90,74 @@ def tile_list_cortex_rates_kernel(tc, tab_words, tab_scales, offs, tab2_words, t
         for quad in QUADS:
             nc.sync.dma_start(k_scales[32 * quad:32 * quad + 4, :, :].bitcast(I32),
                               staged[8 * quad:8 * quad + 8, :].bitcast(I32))
-        v_table.append(held([P, T], I32, "v_table1", tag="v_scale_picked"))
+        w1_raw.append(laid([P, 4, H], F32, "w1_raw1", 0))
+        load_w1(1)
+        v_table.append(laid([P, T], I32, "v_table1", V_TABLE_AT))
         load_words(v_table[1], tab_words[1])
         w4_dealt = held([P, 2, 2 * H], U8, "w4_dealt")
-        nc.vector.tensor_copy(w4_dealt[:].bitcast(U16).rearrange("p a (t m) -> p a m t", t=4),
-                              w4_raw[:].bitcast(U16).rearrange("p a (m t) -> p a m t", t=4))
-        late_raw = held([P, 4, H], F32, "late_raw", tag="w4_raw")
-        load_w1(late_raw, 1)
+        nc.scalar.copy(w4_dealt[:].bitcast(U16).rearrange("p a (t m) -> p a m t", t=4),
+                       w4_raw[:].bitcast(U16).rearrange("p a (m t) -> p a m t", t=4))
 
-        w1_woven = held([P, 4 * H], BF16, "w1_woven")
-        pair_woven = [held([P, 2 * H], BF16, "pair_woven%d" % pair) for pair in range(2)]
-        w1_codes = [held([P, H], U32, "w1_codes%d" % a) for a in range(2)]
-        w1_scales = [held([P, H], U8, "w1_scales%d" % a) for a in range(2)]
+        v_picked = [held([P, S], U32, "v_picked%d" % a) for a in range(2)]
 
-        def share(pair, lo, hi):
-            return (pair_woven[pair][:].rearrange("p (s m j) -> p m j s", s=2, j=4)[:, lo:hi],
-                    late_raw[:].rearrange("p j (m u s) -> p u m j s", u=2, s=2)[:, pair, lo:hi])
+        def pick_images(a, width):
+            for lo in range(0, S, width):
+                nc.vector.tensor_copy(v_picked[a][:, lo:lo + width],
+                                      v_table[a][:].bitcast(U32).indirect(images[:, lo // 16:(lo + width) // 16]))
 
-        def round_pair(pair):
-            nc.scalar.activation(*share(pair, 0, SCALAR_SHARES[pair]), ACT.Copy)
-            nc.vector.tensor_copy(*share(pair, SCALAR_SHARES[pair], P))
-            for i in range(2):
-                cols = slice(P * (2 * pair + i), P * (2 * pair + i + 1))
-                nc.vector.quantize_mx(out=w1_codes[1][:, cols].bitcast(FP8X4), scales=w1_scales[1][:, cols],
-                                      in_=pair_woven[pair][:, H * i:H * (i + 1)])
-
-        v_picked = [held([P, S], U32, "v_picked0"), held([P, S - CHUNK], U32, "v_picked1")]
-
-        def pick_images(picked, a, lo, hi):
-            nc.vector.tensor_copy(picked, v_table[a][:].bitcast(U32).indirect(images[:, lo // 16:hi // 16]))
-
-        for lo in (0, PASS):
-            pick_images(v_picked[0][:, lo:lo + PASS], 0, lo, lo + PASS)
-        nc.scalar.activation(w1_woven[:].rearrange("p (t m j) -> p m j t", t=4, j=4),
-                             w1_raw[:].rearrange("p j (m t) -> p m j t", t=4), ACT.Copy)
-        nc.vector.quantize_mx(out=w1_codes[0][:].bitcast(FP8X4), scales=w1_scales[0][:], in_=w1_woven[:])
-        v2_table = held([P, T2], I32, "v2_table", tag="w1_raw")
-        load_words(v2_table, tab2_words[0])
-        v2_scale_picked = held([P, S2], U8, "v2_scale_picked")
+        pick_images(0, PASS)
         v2_scale_dealt = held([P, S2], U8, "v2_scale_dealt")
-        nc.vector.tensor_copy(v2_scale_picked[:], v2_scale_rows[:].indirect(neurons[:]))
         nc.vector.tensor_copy(v2_scale_dealt[:].rearrange("p (a t m) -> p a m t", a=2, t=4),
-                              v2_scale_picked[:].rearrange("p (a m t) -> p a m t", a=2, t=4))
+                              v2_scale_rows[:].indirect(neurons[:]))
+        v2_table = laid([P, T2], I32, "v2_table", V2_TABLE_AT)
+        load_words(v2_table, tab2_words[0])
+        gain = laid([P, 4], F32, "gain", V2_TABLE_AT + 4 * T2)
+        nc.sync.dma_start(gain[:], g.rearrange("(p t) -> p t", t=4))
         for quad in QUADS:
             first = 32 * quad + V2_ROW
             nc.sync.dma_start(v2_scales[first:first + 4, :].bitcast(I32),
                               v2_scale_dealt[4 * quad:4 * quad + 4, :].bitcast(I32))
+        floor = laid([P, 2, 4], F32, "floor", V2_TABLE_AT + 4 * T2 + 64)
+        nc.sync.dma_start(floor[:], base.rearrange("(a p t) -> p a t", a=2, t=4))
+
+        w1_codes = [held([P, H], U32, "w1_codes%d" % a) for a in range(2)]
+        w1_scales = [held([P, H], U8, "w1_scales%d" % a) for a in range(2)]
+        for a in range(2):
+            w1_woven = held([P, 4 * H], BF16, "w1_woven%d" % a)
+            nc.scalar.activation(w1_woven[:].rearrange("p (t m j) -> p m j t", t=4, j=4),
+                                 w1_raw[a][:].rearrange("p j (m t) -> p m j t", t=4), ACT.Copy)
+            nc.vector.quantize_mx(out=w1_codes[a][:].bitcast(FP8X4), scales=w1_scales[a][:], in_=w1_woven[:])
+        pick_images(1, CHUNK)
 
         banks = [[psum.tile([P, 2, CHUNK], F32, name="bank%d" % (2 * c + pair)) for pair in range(2)]
-                 for c in range(CHUNKS - 1)]
+                 for c in range(2)]
 
-        def picked_words(a, c):
-            if a == 1 and c == CHUNKS - 1:
-                return v_late[:].bitcast(FP8X4)
-            return v_picked[a][:, CHUNK * c:CHUNK * (c + 1)].bitcast(FP8X4)
-
-        def stored_pass(a, c, t, start=False):
+        def stored_pass(a, c, t, stop=False):
             cols = slice(CHUNK * c, CHUNK * (c + 1))
             nc.tensor.matmul_mx(out=banks[c][t // 2][:, t % 2, :],
                                 lhsT=w4_dealt[:, a, 2 * P * t:2 * P * (t + 1)].bitcast(FP4X4),
                                 lhsT_scale=k_scales[:, a, S + P * t:S + P * (t + 1)],
-                                rhs=picked_words(a, c), rhs_scale=k_scales[:, a, cols],
-                                start=start, stop=False)
+                                rhs=v_picked[a][:, cols].bitcast(FP8X4), rhs_scale=k_scales[:, a, cols],
+                                start=False, stop=stop)
 
-        def learned_pass(a, c, t, stop=False):
+        def learned_pass(a, c, t, start=False):
             cols = slice(CHUNK * c, CHUNK * (c + 1))
             nc.tensor.matmul_mx(out=banks[c][t // 2][:, t % 2, :],
                                 lhsT=w1_codes[a][:, P * t:P * (t + 1)].bitcast(FP8X4),
                                 lhsT_scale=w1_scales[a][:, P * t:P * (t + 1)],
-                                rhs=picked_words(a, c), rhs_scale=k_scales[:, a, cols],
-                                start=False, stop=stop)
+                                rhs=v_picked[a][:, cols].bitcast(FP8X4), rhs_scale=k_scales[:, a, cols],
+                                start=start, stop=False)
 
-        for lo, hi in ((0, PASS), (PASS, S - CHUNK)):
-            pick_images(v_picked[1][:, lo:hi], 1, lo, hi)
-        for pair in range(2):
-            round_pair(pair)
-        gain = held([P, 4], F32, "gain", tag="w1_woven")
-        floor = held([P, 2, 4], F32, "floor", tag="pair_woven1")
-        nc.sync.dma_start(gain[:], g.rearrange("(p t) -> p t", t=4))
-        nc.sync.dma_start(floor[:], base.rearrange("(a p t) -> p a t", a=2, t=4))
-        v_late = held([P, CHUNK], U32, "v_late", tag="pair_woven0")
-        pick_images(v_late[:], 1, S - CHUNK, S)
-        for one_pass in (stored_pass, learned_pass):
-            for c in range(CHUNKS - 1):
-                for t in range(4):
-                    if one_pass == stored_pass:
-                        stored_pass(0, c, t, start=(t % 2 == 0))
-                    else:
-                        learned_pass(0, c, t)
-        for c in range(CHUNKS - 1):
-            for t in range(4):
-                stored_pass(1, c, t)
-        for c in range(CHUNKS - 1):
-            for t in range(4):
-                learned_pass(1, c, t, stop=(t % 2 == 1))
+        def sum_pair(c, pair):
+            for a in range(2):
+                for i in range(2):
+                    learned_pass(a, c, 2 * pair + i, start=(a == 0 and i == 0))
+                for i in range(2):
+                    stored_pass(a, c, 2 * pair + i, stop=(a == 1 and i == 1))
+
+        for c in range(2):
+            for pair in range(2):
+                sum_pair(c, pair)
 
         v2_dealt = held([P, S2], U32, "v2_dealt")
         for a in range(2):
@@ -227,17 +206,16 @@ def tile_list_cortex_rates_kernel(tc, tab_words, tab_scales, offs, tab2_words, t
                     step(c, pair)
 
         last = CHUNKS - 1
-        banks.append([])
 
-        def sum_late(pair, bank):
-            banks[last].append(psum.tile([P, 2, CHUNK], F32, name="late", tag="bank%d" % bank))
-            for i in range(2):
-                for a in range(2):
-                    stored_pass(a, last, 2 * pair + i, start=(i == 0 and a == 0))
-                    learned_pass(a, last, 2 * pair + i, stop=(i == 1 and a == 1))
+        def sum_late(c):
+            banks.append([psum.tile([P, 2, CHUNK], F32, name="late", tag="bank%d" % (2 * (c - 2) + pair))
+                          for pair in range(2)])
+            for pair in range(2):
+                sum_pair(c, pair)
 
+        sum_late(2)
         curve(1)
-        sum_late(0, 2)
+        sum_late(last)
         curve(2)
 
         def woven_view(ap):
@@ -277,7 +255,6 @@ def tile_list_cortex_rates_kernel(tc, tab_words, tab_scales, offs, tab2_words, t
                     held([P, 4, PASS], F32, "y%d_1" % half)]
 
         y = [y_tiles(0)]
-        turns = [(6, 7, 0, 1), (4, 5, 3, 7), (0, 1, 2, 6), (4, 5, 3, 7)]
         y_woven = {}
 
         def woven_tile(a, lo, hi, tag=None):
@@ -285,7 +262,7 @@ def tile_list_cortex_rates_kernel(tc, tab_words, tab_scales, offs, tab2_words, t
             for col in range(lo, hi, HEAD):
                 y_woven[a, col] = (tile, lo)
 
-        for a, lo, hi in ((0, 0, P), (0, CHUNK, PASS), (0, PASS, S), (1, 0, PASS)):
+        for a, lo, hi in ((0, 0, CHUNK), (0, CHUNK, PASS), (0, PASS, S), (1, 0, PASS)):
             woven_tile(a, lo, hi)
         y_codes = held([P, 2, S], U32, "y_codes")
         y_scales = held([P, 2, S], U8, "y_scales")
@@ -298,7 +275,7 @@ def tile_list_cortex_rates_kernel(tc, tab_words, tab_scales, offs, tab2_words, t
         def fire(c):
             for a in range(2):
                 for pair in range(2):
-                    drive = psum.tile([P, 2, CHUNK], F32, name="drive", tag="bank%d" % turns[c][2 * a + pair])
+                    drive = psum.tile([P, 2, CHUNK], F32, name="drive", tag="bank%d" % (4 + 2 * a + pair))
                     for i in range(2):
                         cols = slice(PASS * a + P * (2 * pair + i), PASS * a + P * (2 * pair + i + 1))
                         nc.tensor.matmul_mx(out=drive[:, i, :], lhsT=v2_dealt[:, cols].bitcast(FP8X4),
@@ -342,15 +319,11 @@ def tile_list_cortex_rates_kernel(tc, tab_words, tab_scales, offs, tab2_words, t
             weave_on_gpsimd(*woven_part(0, CHUNK * c, CHUNK * c + HEAD))
             quantise_h(c + 1)
             if c == 0:
-                sum_late(1, 6)
-                weave_y_on_scalar(0, HEAD, P)
+                weave_y_on_scalar(0, HEAD, CHUNK)
                 curve(last)
                 y.append(y_tiles(1))
             if c == 1:
-                woven_tile(0, P, CHUNK, tag="h_sliced2")
-                weave_y_on_vector(0, P, CHUNK)
-                for part in (0, P):
-                    quantise_y(0, part, part + P)
+                quantise_y(0, 0, CHUNK)
                 store_codes(slice(0, 1), slice(0, CHUNK), nc.sync)
         weave_y_on_scalar(1, 0, PASS)
         weave_y_on_scalar(0, CHUNK + HEAD, PASS)

@@ -100,12 +100,12 @@ def tile_list_cortex_rates_kernel(tc, tab_words, tab_scales, offs, tab2_words, t
 
         v_picked = [held([P, S], U32, "v_picked%d" % a) for a in range(2)]
 
-        def pick_images(a, width):
-            for lo in range(0, S, width):
-                nc.vector.tensor_copy(v_picked[a][:, lo:lo + width],
-                                      v_table[a][:].bitcast(U32).indirect(images[:, lo // 16:(lo + width) // 16]))
+        def pick_images(a, cuts):
+            for lo, hi in zip(cuts, cuts[1:]):
+                nc.vector.tensor_copy(v_picked[a][:, lo:hi],
+                                      v_table[a][:].bitcast(U32).indirect(images[:, lo // 16:hi // 16]))
 
-        pick_images(0, PASS)
+        pick_images(0, (0, S))
         v2_scale_dealt = held([P, S2], U8, "v2_scale_dealt")
         nc.vector.tensor_copy(v2_scale_dealt[:].rearrange("p (a t m) -> p a m t", a=2, t=4),
                               v2_scale_rows[:].indirect(neurons[:]))
@@ -127,14 +127,18 @@ def tile_list_cortex_rates_kernel(tc, tab_words, tab_scales, offs, tab2_words, t
             nc.scalar.activation(w1_woven[:].rearrange("p (t m j) -> p m j t", t=4, j=4),
                                  w1_raw[a][:].rearrange("p j (m t) -> p m j t", t=4), ACT.Copy)
             nc.vector.quantize_mx(out=w1_codes[a][:].bitcast(FP8X4), scales=w1_scales[a][:], in_=w1_woven[:])
-        pick_images(1, CHUNK)
+        pick_images(1, (0, CHUNK, PASS, S))
 
-        banks = [[psum.tile([P, 2, CHUNK], F32, name="bank%d" % (2 * c + pair)) for pair in range(2)]
-                 for c in range(2)]
+        lone = [psum.tile([P, 1, CHUNK], F32, name="bank%d" % t) for t in range(2)]
+        banks = [[None, psum.tile([P, 2, CHUNK], F32, name="bank2")],
+                 [psum.tile([P, 2, CHUNK], F32, name="bank%d" % (3 + pair)) for pair in range(2)]]
+
+        def summed(c, t):
+            return lone[t][:, 0, :] if c == 0 and t < 2 else banks[c][t // 2][:, t % 2, :]
 
         def stored_pass(a, c, t, stop=False):
             cols = slice(CHUNK * c, CHUNK * (c + 1))
-            nc.tensor.matmul_mx(out=banks[c][t // 2][:, t % 2, :],
+            nc.tensor.matmul_mx(out=summed(c, t),
                                 lhsT=w4_dealt[:, a, 2 * P * t:2 * P * (t + 1)].bitcast(FP4X4),
                                 lhsT_scale=k_scales[:, a, S + P * t:S + P * (t + 1)],
                                 rhs=v_picked[a][:, cols].bitcast(FP8X4), rhs_scale=k_scales[:, a, cols],
@@ -142,7 +146,7 @@ def tile_list_cortex_rates_kernel(tc, tab_words, tab_scales, offs, tab2_words, t
 
         def learned_pass(a, c, t, start=False):
             cols = slice(CHUNK * c, CHUNK * (c + 1))
-            nc.tensor.matmul_mx(out=banks[c][t // 2][:, t % 2, :],
+            nc.tensor.matmul_mx(out=summed(c, t),
                                 lhsT=w1_codes[a][:, P * t:P * (t + 1)].bitcast(FP8X4),
                                 lhsT_scale=w1_scales[a][:, P * t:P * (t + 1)],
                                 rhs=v_picked[a][:, cols].bitcast(FP8X4), rhs_scale=k_scales[:, a, cols],
@@ -155,9 +159,12 @@ def tile_list_cortex_rates_kernel(tc, tab_words, tab_scales, offs, tab2_words, t
                 for i in range(2):
                     stored_pass(a, c, 2 * pair + i, stop=(a == 1 and i == 1))
 
-        for c in range(2):
-            for pair in range(2):
-                sum_pair(c, pair)
+        for t in range(2):
+            for a in range(2):
+                learned_pass(a, 0, t, start=(a == 0))
+                stored_pass(a, 0, t, stop=(a == 1))
+        for c, pair in ((0, 1), (1, 0), (1, 1)):
+            sum_pair(c, pair)
 
         v2_dealt = held([P, S2], U32, "v2_dealt")
         for a in range(2):
@@ -184,9 +191,10 @@ def tile_list_cortex_rates_kernel(tc, tab_words, tab_scales, offs, tab2_words, t
         def invert(c, pair, part=slice(0, 2)):
             nc.scalar.activation(inverses[c][pair][:, part, :], roots[c][pair][:, part, :], ACT.Square)
 
-        for step in (square, root):
-            for i in range(2):
-                step(0, 0, slice(i, i + 1))
+        for i in range(2):
+            nc.scalar.activation(squares[0][0][:, i, :], summed(0, i), ACT.Square, scale=math.sqrt(SHIFT))
+        for i in range(2):
+            root(0, 0, slice(i, i + 1))
         for t in range(2):
             nc.gpsimd.tensor_scalar(first_factors[0][:, t, :], squares[0][0][:, t, :], gain[:, t:t + 1], -0.0,
                                     ALU.mult, ALU.add)
@@ -215,7 +223,6 @@ def tile_list_cortex_rates_kernel(tc, tab_words, tab_scales, offs, tab2_words, t
 
         sum_late(2)
         curve(1)
-        sum_late(last)
         curve(2)
 
         def woven_view(ap):
@@ -262,7 +269,7 @@ def tile_list_cortex_rates_kernel(tc, tab_words, tab_scales, offs, tab2_words, t
             for col in range(lo, hi, HEAD):
                 y_woven[a, col] = (tile, lo)
 
-        for a, lo, hi in ((0, 0, CHUNK), (0, CHUNK, PASS), (0, PASS, S), (1, 0, PASS)):
+        for a, lo, hi in ((0, 0, CHUNK), (0, CHUNK, PASS), (0, PASS, S - CHUNK), (0, S - CHUNK, S), (1, 0, PASS), (1, S - CHUNK, S)):
             woven_tile(a, lo, hi)
         y_codes = held([P, 2, S], U32, "y_codes")
         y_scales = held([P, 2, S], U8, "y_scales")
@@ -319,6 +326,7 @@ def tile_list_cortex_rates_kernel(tc, tab_words, tab_scales, offs, tab2_words, t
             weave_on_gpsimd(*woven_part(0, CHUNK * c, CHUNK * c + HEAD))
             quantise_h(c + 1)
             if c == 0:
+                sum_late(last)
                 weave_y_on_scalar(0, HEAD, CHUNK)
                 curve(last)
                 y.append(y_tiles(1))
@@ -331,7 +339,7 @@ def tile_list_cortex_rates_kernel(tc, tab_words, tab_scales, offs, tab2_words, t
         store_codes(slice(1, 2), slice(0, PASS), nc.sync)
         quantise_y(0, CHUNK, PASS)
         store_codes(slice(0, 1), slice(CHUNK, PASS), nc.sync)
-        woven_tile(1, PASS, S, tag="y_woven0_%d" % CHUNK)
+        woven_tile(1, PASS, S - CHUNK, tag="y_woven0_%d" % CHUNK)
         weave_on_gpsimd(*woven_part(1, PASS, PASS + CHUNK))
         weave_y_on_scalar(0, PASS + HEAD, PASS + CHUNK)
         fire(last)

@@ -51,7 +51,7 @@ def tile_list_cortex_rates_kernel(tc, tab_words, tab_scales, offs, tab2_words, t
         v2_scale_rows = laid([P, T2], U8, "v2_scale_rows", V2_TABLE_AT + 4 * T2 - T2 // 2)
         v2_scales = held([P, S2], U8, "v2_scales")
         k_scales = held([P, 2, S + H], U8, "k_scales")
-        w4_raw = held([P, 2, 2 * H], U8, "w4_raw")
+        w4_raw = [held([P, 2 * H], U8, "w4_raw0")]
         v_table = [held([P, T], I32, "v_table0")]
         w1_raw = [held([P, 4, H], F32, "w1_raw0")]
         warm = held([P, 2], F32, "warm")
@@ -75,7 +75,7 @@ def tile_list_cortex_rates_kernel(tc, tab_words, tab_scales, offs, tab2_words, t
         nc.sync.dma_start(images[:], offs)
         nc.sync.dma_start(v_scale_rows[0:32, :].bitcast(I32), tab_scales.rearrange("a q c -> q a c").bitcast(I32))
         nc.sync.dma_start(w4_scale_rows[0:32, :].bitcast(I32), w4_scales.rearrange("a q c -> q a c").bitcast(I32))
-        nc.sync.dma_start(w4_raw[:].bitcast(I32), w4_words.rearrange("a p c -> p a c").bitcast(I32))
+        nc.sync.dma_start(w4_raw[0][:].bitcast(I32), w4_words[0].bitcast(I32))
         nc.sync.dma_start(neurons[:], offs2)
         load_words(v_table[0], tab_words[0])
         load_w1(0)
@@ -94,9 +94,14 @@ def tile_list_cortex_rates_kernel(tc, tab_words, tab_scales, offs, tab2_words, t
         load_w1(1)
         v_table.append(laid([P, T], I32, "v_table1", V_TABLE_AT))
         load_words(v_table[1], tab_words[1])
-        w4_dealt = held([P, 2, 2 * H], U8, "w4_dealt")
-        nc.scalar.copy(w4_dealt[:].bitcast(U16).rearrange("p a (t m) -> p a m t", t=4),
-                       w4_raw[:].bitcast(U16).rearrange("p a (m t) -> p a m t", t=4))
+        w4_dealt = [[held([P, H], U8, "w4_dealt%d_%d" % (a, pair)) for pair in range(2)] for a in range(2)]
+
+        def deal_w4(a):
+            for pair in range(2):
+                nc.scalar.copy(w4_dealt[a][pair][:].bitcast(U16).rearrange("p (s m) -> p m s", s=2),
+                               w4_raw[a][:].bitcast(U16).rearrange("p (m u s) -> p u m s", u=2, s=2)[:, pair])
+
+        deal_w4(0)
 
         v_picked = [held([P, S], U32, "v_picked%d" % a) for a in range(2)]
 
@@ -109,6 +114,8 @@ def tile_list_cortex_rates_kernel(tc, tab_words, tab_scales, offs, tab2_words, t
         v2_scale_dealt = held([P, S2], U8, "v2_scale_dealt")
         nc.vector.tensor_copy(v2_scale_dealt[:].rearrange("p (a t m) -> p a m t", a=2, t=4),
                               v2_scale_rows[:].indirect(neurons[:]))
+        w4_raw.append(laid([P, 2 * H], U8, "w4_raw1", V2_TABLE_AT + 4 * T2 + 128))
+        nc.sync.dma_start(w4_raw[1][:].bitcast(I32), w4_words[1].bitcast(I32))
         v2_table = laid([P, T2], I32, "v2_table", V2_TABLE_AT)
         load_words(v2_table, tab2_words[0])
         gain = laid([P, 4], F32, "gain", V2_TABLE_AT + 4 * T2)
@@ -127,6 +134,7 @@ def tile_list_cortex_rates_kernel(tc, tab_words, tab_scales, offs, tab2_words, t
             nc.scalar.activation(w1_woven[:].rearrange("p (t m j) -> p m j t", t=4, j=4),
                                  w1_raw[a][:].rearrange("p j (m t) -> p m j t", t=4), ACT.Copy)
             nc.vector.quantize_mx(out=w1_codes[a][:].bitcast(FP8X4), scales=w1_scales[a][:], in_=w1_woven[:])
+        deal_w4(1)
         pick_images(1, (0, CHUNK, PASS, S))
 
         lone = [psum.tile([P, 1, CHUNK], F32, name="bank%d" % t) for t in range(2)]
@@ -136,33 +144,36 @@ def tile_list_cortex_rates_kernel(tc, tab_words, tab_scales, offs, tab2_words, t
         def summed(c, t):
             return lone[t][:, 0, :] if c == 0 and t < 2 else banks[c][t // 2][:, t % 2, :]
 
-        def stored_pass(a, c, t, stop=False):
+        def stored_pass(a, c, t):
             cols = slice(CHUNK * c, CHUNK * (c + 1))
             nc.tensor.matmul_mx(out=summed(c, t),
-                                lhsT=w4_dealt[:, a, 2 * P * t:2 * P * (t + 1)].bitcast(FP4X4),
+                                lhsT=w4_dealt[a][t // 2][:, 2 * P * (t % 2):2 * P * (t % 2 + 1)].bitcast(FP4X4),
                                 lhsT_scale=k_scales[:, a, S + P * t:S + P * (t + 1)],
                                 rhs=v_picked[a][:, cols].bitcast(FP8X4), rhs_scale=k_scales[:, a, cols],
-                                start=False, stop=stop)
+                                start=False, stop=False)
 
-        def learned_pass(a, c, t, start=False):
+        def learned_pass(a, c, t, start=False, stop=False):
             cols = slice(CHUNK * c, CHUNK * (c + 1))
             nc.tensor.matmul_mx(out=summed(c, t),
                                 lhsT=w1_codes[a][:, P * t:P * (t + 1)].bitcast(FP8X4),
                                 lhsT_scale=w1_scales[a][:, P * t:P * (t + 1)],
                                 rhs=v_picked[a][:, cols].bitcast(FP8X4), rhs_scale=k_scales[:, a, cols],
-                                start=start, stop=False)
+                                start=start, stop=stop)
+
+        def sum_slices(c, slices):
+            for t in slices:
+                learned_pass(0, c, t, start=(t == slices[0]))
+            for a in range(2):
+                for t in slices:
+                    stored_pass(a, c, t)
+            for t in slices:
+                learned_pass(1, c, t, stop=(t == slices[-1]))
 
         def sum_pair(c, pair):
-            for a in range(2):
-                for i in range(2):
-                    learned_pass(a, c, 2 * pair + i, start=(a == 0 and i == 0))
-                for i in range(2):
-                    stored_pass(a, c, 2 * pair + i, stop=(a == 1 and i == 1))
+            sum_slices(c, (2 * pair, 2 * pair + 1))
 
         for t in range(2):
-            for a in range(2):
-                learned_pass(a, 0, t, start=(a == 0))
-                stored_pass(a, 0, t, stop=(a == 1))
+            sum_slices(0, (t,))
         for c, pair in ((0, 1), (1, 0), (1, 1)):
             sum_pair(c, pair)
 
@@ -200,9 +211,9 @@ def tile_list_cortex_rates_kernel(tc, tab_words, tab_scales, offs, tab2_words, t
                                     ALU.mult, ALU.add)
         first_factors.append(held([P, 4, CHUNK], F32, "first_factor1", tag="square0_0")[:])
         nc.gpsimd.tensor_tensor(first_factors[1][:, 0:2, :], roots[0][0], roots[0][0], ALU.mult)
-        for step in (square, root):
-            for i in range(2):
-                step(0, 1, slice(i, i + 1))
+        square(0, 1)
+        square(1, 0)
+        root(0, 1)
         for lo in (0, P):
             for t in (2, 3):
                 root_part = roots[0][1][:, t - 2, lo:lo + P]
@@ -222,7 +233,10 @@ def tile_list_cortex_rates_kernel(tc, tab_words, tab_scales, offs, tab2_words, t
                 sum_pair(c, pair)
 
         sum_late(2)
-        curve(1)
+        square(1, 1)
+        for step in (root, invert):
+            for pair in range(2):
+                step(1, pair)
         curve(2)
 
         def woven_view(ap):

@@ -47,10 +47,10 @@ def tile_list_cortex_rates_kernel(tc, tab_words, tab_scales, offs, tab2_words, t
         images = keep.tile([P, S // 16], U16, name="images")
         neurons = keep.tile([P, S2 // 16], U16, name="neurons")
         v_scale_rows = held([P, T], U8, "v_scale_rows")
-        w4_scale_rows = held([P, H], U8, "w4_scale_rows")
+        w4_scale_rows = laid([P, H], U8, "w4_scale_rows", V_TABLE_AT - H // 2)
         v2_scale_rows = laid([P, T2], U8, "v2_scale_rows", V2_TABLE_AT + 4 * T2 - T2 // 2)
-        v2_scales = held([P, S2], U8, "v2_scales")
-        k_scales = held([P, 2, S + H], U8, "k_scales")
+        late_scales = held([P, 2, PASS], U8, "late_scales")
+        k_scales = held([P, 2, PASS + H], U8, "k_scales")
         w4_raw = [held([P, 2 * H], U8, "w4_raw0")]
         v_table = [held([P, T], I32, "v_table0")]
         w1_raw = [held([P, 4, H], F32, "w1_raw0")]
@@ -63,7 +63,7 @@ def tile_list_cortex_rates_kernel(tc, tab_words, tab_scales, offs, tab2_words, t
             nc.vector.memset(w4_scale_rows[lo:hi, :].bitcast(I32), 0)
         nc.gpsimd.memset(v2_scale_rows[:].bitcast(I32), 0)
         nc.gpsimd.memset(k_scales[:].rearrange("p a c -> p (a c)").bitcast(I32), 0)
-        nc.gpsimd.memset(v2_scales[:].bitcast(I32), 0)
+        nc.gpsimd.memset(late_scales[:].rearrange("p a c -> p (a c)").bitcast(I32), 0)
         nc.scalar.activation(warm[:, 1:2], warm[:, 0:1], ACT.Abs_reciprocal_sqrt)
 
         def load_w1(a):
@@ -81,12 +81,12 @@ def tile_list_cortex_rates_kernel(tc, tab_words, tab_scales, offs, tab2_words, t
         load_w1(0)
         nc.sync.dma_start(v2_scale_rows[0:16, :].bitcast(I32), tab2_scales[0].bitcast(I32))
 
-        v_scale_picked = laid([P, S], U8, "v_scale_picked", V_TABLE_AT - S // 2)
-        staged = held([P, S + H], U8, "staged")
+        v_scale_picked = held([P, S], U8, "v_scale_picked")
+        staged = held([P, PASS + H], U8, "staged")
         nc.vector.tensor_copy(v_scale_picked[:], v_scale_rows[:].indirect(images[:]))
-        nc.vector.tensor_copy(staged[:, S:S + H].rearrange("p (t m) -> p m t", t=4),
+        nc.vector.tensor_copy(staged[:, 0:PASS].bitcast(I32), v_scale_picked[:, 0:PASS].bitcast(I32))
+        nc.vector.tensor_copy(staged[:, PASS:PASS + H].rearrange("p (t m) -> p m t", t=4),
                               w4_scale_rows[:].rearrange("p (m t) -> p m t", t=4))
-        nc.vector.tensor_copy(staged[:, 0:S].bitcast(I32), v_scale_picked[:].bitcast(I32))
         for quad in QUADS:
             nc.sync.dma_start(k_scales[32 * quad:32 * quad + 4, :, :].bitcast(I32),
                               staged[8 * quad:8 * quad + 8, :].bitcast(I32))
@@ -120,10 +120,6 @@ def tile_list_cortex_rates_kernel(tc, tab_words, tab_scales, offs, tab2_words, t
         load_words(v2_table, tab2_words[0])
         gain = laid([P, 4], F32, "gain", V2_TABLE_AT + 4 * T2)
         nc.sync.dma_start(gain[:], g.rearrange("(p t) -> p t", t=4))
-        for quad in QUADS:
-            first = 32 * quad + V2_ROW
-            nc.sync.dma_start(v2_scales[first:first + 4, :].bitcast(I32),
-                              v2_scale_dealt[4 * quad:4 * quad + 4, :].bitcast(I32))
         floor = laid([P, 2, 4], F32, "floor", V2_TABLE_AT + 4 * T2 + 64)
         nc.sync.dma_start(floor[:], base.rearrange("(a p t) -> p a t", a=2, t=4))
 
@@ -134,8 +130,23 @@ def tile_list_cortex_rates_kernel(tc, tab_words, tab_scales, offs, tab2_words, t
             nc.scalar.activation(w1_woven[:].rearrange("p (t m j) -> p m j t", t=4, j=4),
                                  w1_raw[a][:].rearrange("p j (m t) -> p m j t", t=4), ACT.Copy)
             nc.vector.quantize_mx(out=w1_codes[a][:].bitcast(FP8X4), scales=w1_scales[a][:], in_=w1_woven[:])
+        staged_late = held([P, PASS], U8, "staged_late", tag="w1_woven0")
+        nc.vector.tensor_copy(staged_late[:].bitcast(I32), v_scale_picked[:, PASS:S].bitcast(I32))
+        for quad in QUADS:
+            nc.sync.dma_start(late_scales[32 * quad:32 * quad + 4, :, :].bitcast(I32),
+                              staged_late[8 * quad:8 * quad + 8, :].bitcast(I32))
+        v2_scales = held([P, S2], U8, "v2_scales", tag="w1_woven1")
+        nc.gpsimd.memset(v2_scales[:].bitcast(I32), 0)
+        for quad in QUADS:
+            first = 32 * quad + V2_ROW
+            nc.sync.dma_start(v2_scales[first:first + 4, :].bitcast(I32),
+                              v2_scale_dealt[4 * quad:4 * quad + 4, :].bitcast(I32))
         deal_w4(1)
         pick_images(1, (0, CHUNK, PASS, S))
+
+        def image_scales(a, c):
+            lo = CHUNK * (c % 2)
+            return (k_scales if c < 2 else late_scales)[:, a, lo:lo + CHUNK]
 
         lone = [psum.tile([P, 1, CHUNK], F32, name="bank%d" % t) for t in range(2)]
         banks = [[None, psum.tile([P, 2, CHUNK], F32, name="bank2")],
@@ -148,8 +159,8 @@ def tile_list_cortex_rates_kernel(tc, tab_words, tab_scales, offs, tab2_words, t
             cols = slice(CHUNK * c, CHUNK * (c + 1))
             nc.tensor.matmul_mx(out=summed(c, t),
                                 lhsT=w4_dealt[a][t // 2][:, 2 * P * (t % 2):2 * P * (t % 2 + 1)].bitcast(FP4X4),
-                                lhsT_scale=k_scales[:, a, S + P * t:S + P * (t + 1)],
-                                rhs=v_picked[a][:, cols].bitcast(FP8X4), rhs_scale=k_scales[:, a, cols],
+                                lhsT_scale=k_scales[:, a, PASS + P * t:PASS + P * (t + 1)],
+                                rhs=v_picked[a][:, cols].bitcast(FP8X4), rhs_scale=image_scales(a, c),
                                 start=False, stop=False)
 
         def learned_pass(a, c, t, start=False, stop=False):
@@ -157,7 +168,7 @@ def tile_list_cortex_rates_kernel(tc, tab_words, tab_scales, offs, tab2_words, t
             nc.tensor.matmul_mx(out=summed(c, t),
                                 lhsT=w1_codes[a][:, P * t:P * (t + 1)].bitcast(FP8X4),
                                 lhsT_scale=w1_scales[a][:, P * t:P * (t + 1)],
-                                rhs=v_picked[a][:, cols].bitcast(FP8X4), rhs_scale=k_scales[:, a, cols],
+                                rhs=v_picked[a][:, cols].bitcast(FP8X4), rhs_scale=image_scales(a, c),
                                 start=start, stop=stop)
 
         def sum_slices(c, slices):

import math
from contextlib import ExitStack

import concourse.mybir as mybir

F32 = mybir.dt.float32
BF16 = mybir.dt.bfloat16
I32 = mybir.dt.int32
U32 = mybir.dt.uint32
U16 = mybir.dt.uint16
U8 = mybir.dt.uint8
FP8X4 = mybir.dt.float8_e4m3fn_x4
FP4X4 = mybir.dt.float4_e2m1fn_x4
ACT = mybir.ActivationFunctionType
ALU = mybir.AluOpType

K, T, S, H, T2, S2 = 1024, 4096, 1024, 512, 2048, 1024
P = 128
PASS = 512
CHUNK = 256
CHUNKS = S // CHUNK
UNITS = 2 * CHUNKS
SHIFT = 1.375
V2_ROW = 4
HEAD = 64
VECTOR_SHARE = 128
V_TABLE_AT = 16 * H
V2_TABLE_AT = V_TABLE_AT + 4 * T
QUADS = (0, 2, 1, 3)
FLOPS = 2 * (2 * K * H * S + H * S * S2)


def tile_list_cortex_rates_kernel(tc, tab_words, tab_scales, offs, tab2_words, tab2_scales, offs2,
                                               w4_words, w4_scales, w1, g, base, out_0, out_1, out_2):
    nc = tc.nc
    with ExitStack() as ctx:
        keep = ctx.enter_context(tc.tile_pool(name="keep", bufs=1))
        reuse = ctx.enter_context(tc.tile_pool(name="reuse", bufs=1))
        psum = ctx.enter_context(tc.psum_pool(name="psum", bufs=1))

        def held(shape, dtype, name, tag=None):
            return keep.tile(shape, dtype, name=name, tag=tag or name, align_bytes=64)

        def laid(shape, dtype, name, offset):
            return reuse.tile(shape, dtype, name=name, offset=offset, align_bytes=64)

        images = keep.tile([P, S // 16], U16, name="images")
        neurons = keep.tile([P, S2 // 16], U16, name="neurons")
        v_scale_rows = held([P, T], U8, "v_scale_rows")
        w4_scale_rows = laid([P, H], U8, "w4_scale_rows", V_TABLE_AT - H // 2)
        v2_scale_rows = laid([P, T2], U8, "v2_scale_rows", V2_TABLE_AT + 4 * T2 - T2 // 2)
        late_scales = held([P, 2, PASS], U8, "late_scales")
        k_scales = held([P, 2, PASS + H], U8, "k_scales")
        w4_raw = [held([P, 2 * H], U8, "w4_raw0")]
        v_table = [held([P, T], I32, "v_table0")]
        w1_raw = [held([P, 4, H], F32, "w1_raw0")]
        warm = held([P, 2], F32, "warm")

        nc.vector.memset(warm[:, 0:1], 1.0)
        for lo, hi in ((32, 64), (64, P)):
            nc.vector.memset(v_scale_rows[lo:hi, :].bitcast(I32), 0)
        for lo, hi in ((32, 64), (64, P)):
            nc.vector.memset(w4_scale_rows[lo:hi, :].bitcast(I32), 0)
        nc.gpsimd.memset(v2_scale_rows[:].bitcast(I32), 0)
        nc.gpsimd.memset(k_scales[:].rearrange("p a c -> p (a c)").bitcast(I32), 0)
        nc.gpsimd.memset(late_scales[:].rearrange("p a c -> p (a c)").bitcast(I32), 0)
        nc.scalar.activation(warm[:, 1:2], warm[:, 0:1], ACT.Abs_reciprocal_sqrt)

        def load_w1(a):
            nc.sync.dma_start(w1_raw[a][:], w1[PASS * a:PASS * (a + 1), :].rearrange("(p j) c -> p j c", j=4))

        def load_words(tile, words):
            nc.sync.dma_start(tile[:], words.rearrange("p t i -> p (t i)").bitcast(I32))

        nc.sync.dma_start(images[:], offs)
        nc.sync.dma_start(v_scale_rows[0:32, :].bitcast(I32), tab_scales.rearrange("a q c -> q a c").bitcast(I32))
        nc.sync.dma_start(w4_scale_rows[0:32, :].bitcast(I32), w4_scales.rearrange("a q c -> q a c").bitcast(I32))
        nc.sync.dma_start(w4_raw[0][:].bitcast(I32), w4_words[0].bitcast(I32))
        nc.sync.dma_start(neurons[:], offs2)
        load_words(v_table[0], tab_words[0])
        load_w1(0)
        nc.sync.dma_start(v2_scale_rows[0:16, :].bitcast(I32), tab2_scales[0].bitcast(I32))

        v_scale_picked = held([P, S], U8, "v_scale_picked")
        staged = held([P, PASS + H], U8, "staged")
        nc.vector.tensor_copy(v_scale_picked[:], v_scale_rows[:].indirect(images[:]))
        nc.vector.tensor_copy(staged[:, 0:PASS].bitcast(I32), v_scale_picked[:, 0:PASS].bitcast(I32))
        nc.vector.tensor_copy(staged[:, PASS:PASS + H].rearrange("p (t m) -> p m t", t=4),
                              w4_scale_rows[:].rearrange("p (m t) -> p m t", t=4))
        for quad in QUADS:
            nc.sync.dma_start(k_scales[32 * quad:32 * quad + 4, :, :].bitcast(I32),
                              staged[8 * quad:8 * quad + 8, :].bitcast(I32))
        w1_raw.append(laid([P, 4, H], F32, "w1_raw1", 0))
        load_w1(1)
        v_table.append(laid([P, T], I32, "v_table1", V_TABLE_AT))
        load_words(v_table[1], tab_words[1])
        w4_dealt = [[held([P, H], U8, "w4_dealt%d_%d" % (a, pair)) for pair in range(2)] for a in range(2)]

        def deal_w4(a):
            for pair in range(2):
                nc.scalar.copy(w4_dealt[a][pair][:].bitcast(U16).rearrange("p (s m) -> p m s", s=2),
                               w4_raw[a][:].bitcast(U16).rearrange("p (m u s) -> p u m s", u=2, s=2)[:, pair])

        deal_w4(0)

        v_picked = [held([P, S], U32, "v_picked%d" % a) for a in range(2)]

        def pick_images(a, cuts):
            for lo, hi in zip(cuts, cuts[1:]):
                nc.vector.tensor_copy(v_picked[a][:, lo:hi],
                                      v_table[a][:].bitcast(U32).indirect(images[:, lo // 16:hi // 16]))

        pick_images(0, (0, S))
        v2_scale_dealt = held([P, S2], U8, "v2_scale_dealt")
        nc.vector.tensor_copy(v2_scale_dealt[:].rearrange("p (a t m) -> p a m t", a=2, t=4),
                              v2_scale_rows[:].indirect(neurons[:]))
        w4_raw.append(laid([P, 2 * H], U8, "w4_raw1", V2_TABLE_AT + 4 * T2 + 128))
        nc.sync.dma_start(w4_raw[1][:].bitcast(I32), w4_words[1].bitcast(I32))
        v2_table = laid([P, T2], I32, "v2_table", V2_TABLE_AT)
        load_words(v2_table, tab2_words[0])
        gain = laid([P, 4], F32, "gain", V2_TABLE_AT + 4 * T2)
        nc.sync.dma_start(gain[:], g.rearrange("(p t) -> p t", t=4))
        floor = laid([P, 2, 4], F32, "floor", V2_TABLE_AT + 4 * T2 + 64)
        nc.sync.dma_start(floor[:], base.rearrange("(a p t) -> p a t", a=2, t=4))

        w1_codes = [held([P, H], U32, "w1_codes%d" % a) for a in range(2)]
        w1_scales = [held([P, H], U8, "w1_scales%d" % a) for a in range(2)]
        for a in range(2):
            w1_woven = held([P, 4 * H], BF16, "w1_woven%d" % a)
            nc.scalar.activation(w1_woven[:].rearrange("p (t m j) -> p m j t", t=4, j=4),
                                 w1_raw[a][:].rearrange("p j (m t) -> p m j t", t=4), ACT.Copy)
            nc.vector.quantize_mx(out=w1_codes[a][:].bitcast(FP8X4), scales=w1_scales[a][:], in_=w1_woven[:])
        staged_late = held([P, PASS], U8, "staged_late", tag="w1_woven0")
        nc.vector.tensor_copy(staged_late[:].bitcast(I32), v_scale_picked[:, PASS:S].bitcast(I32))
        for quad in QUADS:
            nc.sync.dma_start(late_scales[32 * quad:32 * quad + 4, :, :].bitcast(I32),
                              staged_late[8 * quad:8 * quad + 8, :].bitcast(I32))
        v2_scales = held([P, S2], U8, "v2_scales", tag="w1_woven1")
        nc.gpsimd.memset(v2_scales[:].bitcast(I32), 0)
        for quad in QUADS:
            first = 32 * quad + V2_ROW
            nc.sync.dma_start(v2_scales[first:first + 4, :].bitcast(I32),
                              v2_scale_dealt[4 * quad:4 * quad + 4, :].bitcast(I32))
        deal_w4(1)
        pick_images(1, (0, CHUNK, PASS, S))

        def image_scales(a, c):
            lo = CHUNK * (c % 2)
            return (k_scales if c < 2 else late_scales)[:, a, lo:lo + CHUNK]

        lone = [psum.tile([P, 1, CHUNK], F32, name="bank%d" % t) for t in range(2)]
        banks = [[None, psum.tile([P, 2, CHUNK], F32, name="bank2")],
                 [psum.tile([P, 2, CHUNK], F32, name="bank%d" % (3 + pair)) for pair in range(2)]]

        def summed(c, t):
            return lone[t][:, 0, :] if c == 0 and t < 2 else banks[c][t // 2][:, t % 2, :]

        def stored_pass(a, c, t):
            cols = slice(CHUNK * c, CHUNK * (c + 1))
            nc.tensor.matmul_mx(out=summed(c, t),
                                lhsT=w4_dealt[a][t // 2][:, 2 * P * (t % 2):2 * P * (t % 2 + 1)].bitcast(FP4X4),
                                lhsT_scale=k_scales[:, a, PASS + P * t:PASS + P * (t + 1)],
                                rhs=v_picked[a][:, cols].bitcast(FP8X4), rhs_scale=image_scales(a, c),
                                start=False, stop=False)

        def learned_pass(a, c, t, start=False, stop=False):
            cols = slice(CHUNK * c, CHUNK * (c + 1))
            nc.tensor.matmul_mx(out=summed(c, t),
                                lhsT=w1_codes[a][:, P * t:P * (t + 1)].bitcast(FP8X4),
                                lhsT_scale=w1_scales[a][:, P * t:P * (t + 1)],
                                rhs=v_picked[a][:, cols].bitcast(FP8X4), rhs_scale=image_scales(a, c),
                                start=start, stop=stop)

        def sum_slices(c, slices):
            for t in slices:
                learned_pass(0, c, t, start=(t == slices[0]))
            for a in range(2):
                for t in slices:
                    stored_pass(a, c, t)
            for t in slices:
                learned_pass(1, c, t, stop=(t == slices[-1]))

        def sum_pair(c, pair):
            sum_slices(c, (2 * pair, 2 * pair + 1))

        for t in range(2):
            sum_slices(0, (t,))
        for c, pair in ((0, 1), (1, 0), (1, 1)):
            sum_pair(c, pair)

        v2_dealt = held([P, S2], U32, "v2_dealt")
        for a in range(2):
            nc.vector.tensor_copy(v2_dealt[:, PASS * a:PASS * (a + 1)].rearrange("p (t m) -> p m t", t=4),
                                  v2_table[:].bitcast(U32).indirect(neurons[:, 32 * a:32 * (a + 1)]))

        def pair_tiles(name, c):
            return [held([P, 2, CHUNK], F32, "%s%d_%d" % (name, c, pair))[:] for pair in range(2)]

        first_factors = [held([P, 4, CHUNK], F32, "first_factor0")[:]]
        squares = [[held([P, 2, CHUNK], F32, "square0_0")[:], first_factors[0][:, 2:4, :]]]
        squares.extend(pair_tiles("square", c) for c in range(1, CHUNKS))
        roots = [pair_tiles("root", c) for c in range(CHUNKS)]
        inverses = [None] + [pair_tiles("inverse", c) for c in range(1, CHUNKS)]

        def square(c, pair, part=slice(0, 2)):
            nc.scalar.activation(squares[c][pair][:, part, :], banks[c][pair][:, part, :], ACT.Square,
                                 scale=math.sqrt(SHIFT))

        def root(c, pair, part=slice(0, 2)):
            nc.scalar.activation(roots[c][pair][:, part, :], squares[c][pair][:, part, :], ACT.Abs_reciprocal_sqrt,
                                 bias=SHIFT)

        def invert(c, pair, part=slice(0, 2)):
            nc.scalar.activation(inverses[c][pair][:, part, :], roots[c][pair][:, part, :], ACT.Square)

        for i in range(2):
            nc.scalar.activation(squares[0][0][:, i, :], summed(0, i), ACT.Square, scale=math.sqrt(SHIFT))
        for i in range(2):
            root(0, 0, slice(i, i + 1))
        for t in range(2):
            nc.gpsimd.tensor_scalar(first_factors[0][:, t, :], squares[0][0][:, t, :], gain[:, t:t + 1], -0.0,
                                    ALU.mult, ALU.add)
        first_factors.append(held([P, 4, CHUNK], F32, "first_factor1", tag="square0_0")[:])
        nc.gpsimd.tensor_tensor(first_factors[1][:, 0:2, :], roots[0][0], roots[0][0], ALU.mult)
        square(0, 1)
        square(1, 0)
        root(0, 1)
        for lo in (0, P):
            for t in (2, 3):
                root_part = roots[0][1][:, t - 2, lo:lo + P]
                nc.vector.scalar_tensor_tensor(first_factors[1][:, t, lo:lo + P], root_part, gain[:, t:t + 1], root_part,
                                               ALU.mult, ALU.mult)
        def curve(c):
            for step in (square, root, invert):
                for pair in range(2):
                    step(c, pair)

        last = CHUNKS - 1

        def sum_late(c):
            banks.append([psum.tile([P, 2, CHUNK], F32, name="late", tag="bank%d" % (2 * (c - 2) + pair))
                          for pair in range(2)])
            for pair in range(2):
                sum_pair(c, pair)

        sum_late(2)
        square(1, 1)
        for step in (root, invert):
            for pair in range(2):
                step(1, pair)
        curve(2)

        def woven_view(ap):
            return ap.rearrange("p (c i t) -> p c t i", i=4, t=4)

        def sliced_view(ap):
            return ap.rearrange("p t (c i) -> p c t i", i=4)

        def weave_on_gpsimd(woven, sliced):
            nc.gpsimd.tensor_scalar(woven.rearrange("p (m t) -> p m t", t=4), sliced.rearrange("p t m -> p m t"),
                                    1.0, -0.0, ALU.mult, ALU.add)

        h_woven = [held([P, 4 * CHUNK], BF16, "h_woven%d" % c) for c in range(CHUNKS)]
        h_codes = [held([P, CHUNK], U32, "h_codes%d" % c) for c in range(CHUNKS)]
        h_scales = [held([P, CHUNK], U8, "h_scales%d" % c) for c in range(CHUNKS)]

        def quantise_h(c, lo=0, hi=CHUNK):
            nc.vector.quantize_mx(out=h_codes[c][:, lo:hi].bitcast(FP8X4), scales=h_scales[c][:, lo:hi],
                                  in_=h_woven[c][:, 4 * lo:4 * hi])

        def respond(c, tag=None):
            h_sliced = held([P, 4, CHUNK], BF16, "h_sliced%d" % c, tag=tag)
            for t in range(4):
                nc.vector.scalar_tensor_tensor(h_sliced[:, t, :], squares[c][t // 2][:, t % 2, :], gain[:, t:t + 1],
                                               inverses[c][t // 2][:, t % 2, :], ALU.mult, ALU.mult)
            return h_sliced[:]

        for lo in (0, P):
            nc.vector.tensor_tensor(woven_view(h_woven[0][:, 4 * lo:4 * (lo + P)]),
                                    sliced_view(first_factors[0][:, :, lo:lo + P]),
                                    sliced_view(first_factors[1][:, :, lo:lo + P]), ALU.mult)
        for lo in (0, P):
            quantise_h(0, lo, lo + P)

        def y_tiles(half):
            return [held([P, 4, PASS], F32, "y%d_0" % half, tag="root%d_1" % (2 * half + 1)),
                    held([P, 4, PASS], F32, "y%d_1" % half)]

        y = [y_tiles(0)]
        y_woven = {}

        def woven_tile(a, lo, hi, tag=None):
            tile = held([P, 4 * (hi - lo)], BF16, "y_woven%d_%d" % (a, lo), tag=tag)
            for col in range(lo, hi, HEAD):
                y_woven[a, col] = (tile, lo)

        for a, lo, hi in ((0, 0, CHUNK), (0, CHUNK, PASS), (0, PASS, S - CHUNK), (0, S - CHUNK, S), (1, 0, PASS), (1, S - CHUNK, S)):
            woven_tile(a, lo, hi)
        y_codes = held([P, 2, S], U32, "y_codes")
        y_scales = held([P, 2, S], U8, "y_scales")

        def store_y(c, a, slices):
            rows = out_0[PASS * a:PASS * (a + 1), CHUNK * c:CHUNK * (c + 1)]
            cols = slice(CHUNK * (c % 2), CHUNK * (c % 2 + 1))
            nc.sync.dma_start(rows.rearrange("(p t) j -> p t j", t=4)[:, slices, :], y[c // 2][a][:, slices, cols])

        def fire(c):
            for a in range(2):
                for pair in range(2):
                    drive = psum.tile([P, 2, CHUNK], F32, name="drive", tag="bank%d" % (4 + 2 * a + pair))
                    for i in range(2):
                        cols = slice(PASS * a + P * (2 * pair + i), PASS * a + P * (2 * pair + i + 1))
                        nc.tensor.matmul_mx(out=drive[:, i, :], lhsT=v2_dealt[:, cols].bitcast(FP8X4),
                                            lhsT_scale=v2_scales[V2_ROW:P, cols], rhs=h_codes[c][:].bitcast(FP8X4),
                                            rhs_scale=h_scales[c][:], start=True, stop=True)
                    slices = slice(2 * pair, 2 * pair + 2)
                    nc.vector.tensor_tensor(y[c // 2][a][:, slices, CHUNK * (c % 2):CHUNK * (c % 2 + 1)], drive[:],
                                            floor[:, a, slices].unsqueeze(2).to_broadcast([P, 2, CHUNK]), ALU.max)
                    if c >= 1:
                        store_y(c, a, slices)
                if c < 1:
                    store_y(c, a, slice(0, 4))

        def woven_cols(a, lo, hi):
            tile, first = y_woven[a, lo]
            return tile[:, 4 * (lo - first):4 * (hi - first)]

        def woven_part(a, lo, hi):
            half = lo // PASS
            return woven_cols(a, lo, hi), y[half][a][:, :, lo - PASS * half:hi - PASS * half]

        def weave_y_on_scalar(a, lo, hi):
            woven, sliced = woven_part(a, lo, hi)
            nc.scalar.activation(woven_view(woven), sliced_view(sliced), ACT.Copy)

        def weave_y_on_vector(a, lo, hi):
            woven, sliced = woven_part(a, lo, hi)
            nc.vector.tensor_copy(woven_view(woven), sliced_view(sliced))

        def quantise_y(a, lo, hi):
            nc.vector.quantize_mx(out=y_codes[:, a, lo:hi].bitcast(FP8X4), scales=y_scales[:, a, lo:hi],
                                  in_=woven_cols(a, lo, hi))

        def store_codes(groups, cols, queue):
            queue.dma_start(out_1[groups, :, cols, :].rearrange("a p m t -> p a (m t)").bitcast(I32),
                            y_codes[:, groups, cols].bitcast(I32))

        for c in range(CHUNKS - 1):
            weave_on_gpsimd(h_woven[c + 1][:], respond(c + 1, tag="first_factor0" if c == 0 else None))
            fire(c)
            weave_on_gpsimd(*woven_part(0, CHUNK * c, CHUNK * c + HEAD))
            quantise_h(c + 1)
            if c == 0:
                sum_late(last)
                weave_y_on_scalar(0, HEAD, CHUNK)
                curve(last)
                y.append(y_tiles(1))
            if c == 1:
                quantise_y(0, 0, CHUNK)
                store_codes(slice(0, 1), slice(0, CHUNK), nc.sync)
        weave_y_on_scalar(1, 0, PASS)
        weave_y_on_scalar(0, CHUNK + HEAD, PASS)
        quantise_y(1, 0, PASS)
        store_codes(slice(1, 2), slice(0, PASS), nc.sync)
        quantise_y(0, CHUNK, PASS)
        store_codes(slice(0, 1), slice(CHUNK, PASS), nc.sync)
        woven_tile(1, PASS, S - CHUNK, tag="y_woven0_%d" % CHUNK)
        weave_on_gpsimd(*woven_part(1, PASS, PASS + CHUNK))
        weave_y_on_scalar(0, PASS + HEAD, PASS + CHUNK)
        fire(last)
        first = CHUNK * last
        weave_on_gpsimd(*woven_part(0, first, first + HEAD))
        weave_y_on_scalar(0, first + HEAD, S)
        quantise_y(0, PASS, first)
        weave_y_on_vector(1, first, first + VECTOR_SHARE)
        weave_y_on_scalar(1, first + VECTOR_SHARE, S)
        quantise_y(1, PASS, first)
        store_codes(slice(0, 2), slice(PASS, first), nc.sync)
        for a in range(2):
            quantise_y(a, first, S)
            store_codes(slice(a, a + 1), slice(first, S), nc.scalar if a else nc.sync)
        for quad in QUADS:
            queue = nc.sync if quad < 2 else nc.scalar
            queue.dma_start(out_2[:, 4 * quad:4 * quad + 4, :].rearrange("a n c -> n a c").bitcast(I32),
                            y_scales[32 * quad:32 * quad + 4, :, :].bitcast(I32))
